import numpy as np
import ml_dtypes


def mxq(x, axis, fmt="e4m3"):
    dtype, down = {"e4m3": (ml_dtypes.float8_e4m3fn, 7), "e5m2": (ml_dtypes.float8_e5m2, 14)}[fmt]
    v = np.moveaxis(np.asarray(x, np.float32).astype(ml_dtypes.bfloat16).astype(np.float64), axis, -1)
    blocks = v.reshape(v.shape[:-1] + (-1, 32))
    amax = np.abs(blocks).max(-1, keepdims=True)
    byte = np.maximum(np.where(amax > 0, np.frexp(amax)[1] - 1 + 127, 0) - down, 1)
    scale = np.exp2(byte - 127.0)
    codes = (blocks / scale).astype(np.float32).astype(dtype).astype(np.float64)
    return np.moveaxis((codes * scale).reshape(v.shape), -1, axis)


WIDE = False


def mx_kscale(k):
    if not WIDE:
        return np.ones(k)
    levels = np.array([24, -24, 12, -12, 0])
    if k % 512:
        return np.exp2(np.random.permutation(np.resize(levels, k // 32))).repeat(32)
    a = np.empty((k // 512, 16))
    for p in range(k // 512):
        a[p, :8] = np.random.permutation(np.resize(levels, 8))
        for g in range(8):
            far = levels[np.abs(levels - a[p, g]) >= 10]
            a[p, g + 8] = far[np.random.randint(len(far))]
    return np.exp2(a.ravel()).repeat(32)


def f64(x):
    return np.asarray(x).astype(np.float64)


def striped(idx):
    return np.tile(idx.reshape(-1, 16).T, (8, 1)).astype(np.uint16)


def unstriped(offs):
    return offs[:16].T.reshape(-1).astype(np.int64)


E2M1 = np.array([0.0, 0.5, 1.0, 1.5, 2.0, 3.0, 4.0, 6.0, -0.0, -0.5, -1.0, -1.5, -2.0, -3.0, -4.0, -6.0])


def pack_weight(w, fmt):
    k, n = w.shape
    w = f64(np.asarray(w, np.float32).astype(ml_dtypes.bfloat16)).reshape(k // 32, 32, n)
    amax = np.abs(w).max(1)
    if fmt == "e4m3":
        byte = np.frexp(amax)[1] - 1 + 127 - 7
    else:
        mant, ex = np.frexp(amax / 6.0)
        byte = np.where(mant > 0.5, ex, ex - 1) + 127
    byte = np.clip(np.where(amax > 0, byte, 1), 1, 254)
    scaled = (w * np.exp2(127.0 - byte)[:, None, :]).reshape(k, n).astype(np.float32)
    by_word = np.ascontiguousarray(scaled.reshape(k // 512, 128, 4, n).transpose(0, 1, 3, 2))
    if fmt == "e4m3":
        words = by_word.astype(ml_dtypes.float8_e4m3fn).view(np.uint8)
    else:
        c = by_word.astype(ml_dtypes.float4_e2m1fn).view(np.uint8) & 0xF
        words = (c[..., 0::2] | (c[..., 1::2] << 4)).reshape(k // 512, 128, 2 * n)
    return np.ascontiguousarray(words), np.ascontiguousarray(byte.astype(np.uint8).reshape(k // 512, 16, n))


def unpack_weight(words, scales, fmt):
    g, _, n = scales.shape
    words = np.ascontiguousarray(words).reshape(g, 128, n, -1)
    if fmt == "e4m3":
        vals = words.view(ml_dtypes.float8_e4m3fn).astype(np.float64)
    else:
        nib = np.empty((g, 128, n, 4), np.uint8)
        nib[..., 0::2] = words & 0xF
        nib[..., 1::2] = words >> 4
        vals = E2M1[nib]
    vals = vals * np.repeat(np.exp2(scales.astype(np.float64) - 127.0), 8, axis=1)[..., None]
    return vals.transpose(0, 1, 3, 2).reshape(g * 512, n)


def pack_table4(v):
    words, scales = pack_weight(v, "e2m1")
    g, t = words.shape[0] // 2, v.shape[1]
    return np.ascontiguousarray(words.reshape(g, 2, 128, t, 2).transpose(0, 2, 3, 1, 4).reshape(g, 128, t, 4)), scales


def unpack_table4(words, scales):
    g, _, t, _ = words.shape
    return unpack_weight(words.reshape(g, 128, t, 2, 2).transpose(0, 3, 1, 2, 4).reshape(2 * g, 128, 2 * t), scales, "e2m1")


def sigm(f):
    return 1.0 / (1.0 + np.exp(-np.maximum(f, -700.0)))


K, L, R, N, T, J = 1024, 512, 512, 512, 4096, 2048


def setup_inputs():
    n = np.random.standard_normal
    s = mx_kscale(K)[:, None]
    s2 = mx_kscale(L)[:, None]
    u = mx_kscale(R)[:, None]
    p_tab = pack_table4(n((K, T)) * s)
    p_tab2 = pack_weight(n((L, T)) * s2, "e4m3")
    p_wrr = pack_weight(n((L, R)) / np.sqrt(L) / s2, "e4m3")
    p_wri = pack_weight(n((L, R)) / np.sqrt(L) / s2, "e4m3")
    return {
        "tab_words": p_tab[0],
        "tab_scales": p_tab[1],
        "tab2_words": p_tab2[0],
        "tab2_scales": p_tab2[1],
        "wer": (n((K, R)) / np.sqrt(K) / s * u.T).astype(np.float32),
        "wei": (n((K, R)) / np.sqrt(K) / s * u.T).astype(np.float32),
        "wrr_words": p_wrr[0],
        "wrr_scales": p_wrr[1],
        "wri_words": p_wri[0],
        "wri_scales": p_wri[1],
        "nr": (n((R, N)) / np.sqrt(R) / u).astype(np.float32),
        "ni": (n((R, N)) / np.sqrt(R) / u).astype(np.float32),
        "offs": striped(np.random.permutation(T)[:J]),
        "offs2": striped(np.random.permutation(T)[:J]),
    }


def reference(tab_words, tab_scales, tab2_words, tab2_scales, wer, wei, wrr_words, wrr_scales, wri_words, wri_scales, nr, ni, offs, offs2):
    idx = unstriped(offs)
    idx2 = unstriped(offs2)
    tab_ = unpack_table4(tab_words, tab_scales)[:, idx]
    tab2_ = unpack_weight(tab2_words, tab2_scales, "e4m3")[:, idx2]
    wer_ = mxq(f64(wer), 0, "e4m3")
    aer = wer_.T @ tab_
    wei_ = mxq(f64(wei), 0, "e4m3")
    aei = wei_.T @ tab_
    wrr_ = unpack_weight(wrr_words, wrr_scales, "e4m3")
    arr = wrr_.T @ tab2_
    wri_ = unpack_weight(wri_words, wri_scales, "e4m3")
    ari = wri_.T @ tab2_
    hr = aer * arr - aei * ari
    hi = aer * ari + aei * arr
    hr_ = mxq(hr, 0, "e4m3")
    hi_ = mxq(hi, 0, "e4m3")
    nr_ = mxq(f64(nr), 0, "e4m3")
    ni_ = mxq(f64(ni), 0, "e4m3")
    y = nr_.T @ hr_ + ni_.T @ hi_
    return sigm(y)

@@ -1,0 +1,262 @@
+from contextlib import ExitStack
+
+import concourse.mybir as mybir
+
+K, L, R, N, T, J = 1024, 512, 512, 512, 4096, 2048
+FLOPS = 2 * J * (2 * K * R + 2 * L * R + 2 * R * N)
+
+F32 = mybir.dt.float32
+BF16 = mybir.dt.bfloat16
+I32 = mybir.dt.int32
+U32 = mybir.dt.uint32
+U16 = mybir.dt.uint16
+U8 = mybir.dt.uint8
+FP8X4 = mybir.dt.float8_e4m3fn_x4
+FP4X4 = mybir.dt.float4_e2m1fn_x4
+MULT = mybir.AluOpType.mult
+ADD = mybir.AluOpType.add
+SIGMOID = mybir.ActivationFunctionType.Sigmoid
+
+P = 128
+PACK = 4
+K_PASS = P * PACK
+CHUNK = 512
+STEP = 128
+LANES = 16
+
+
+def tile_list_ckg_sig_kernel(
+    tc, tab_words, tab_scales, tab2_words, tab2_scales, wer, wei, wrr_words, wrr_scales,
+    wri_words, wri_scales, nr, ni, offs, offs2, out
+):
+    nc = tc.nc
+    with ExitStack() as ctx:
+        lists = ctx.enter_context(tc.tile_pool(name="lists", bufs=1))
+        keep = ctx.enter_context(tc.tile_pool(name="keep", bufs=1))
+        stage = ctx.enter_context(tc.tile_pool(name="stage", bufs=4))
+        ring = ctx.enter_context(tc.tile_pool(name="ring", bufs=3))
+        psum2 = ctx.enter_context(tc.psum_pool(name="psum2", bufs=2))
+        psum1 = ctx.enter_context(tc.psum_pool(name="psum1", bufs=1))
+
+        ent_list = lists.tile([P, J // LANES], U16, name="ent_list")
+        rel_list = lists.tile([P, J // LANES], U16, name="rel_list")
+        ent_scale_win = keep.tile([P, T // 4], I32, name="ent_scale_win", align_bytes=64)
+        rel_scale_win = keep.tile([P, T // 4], I32, name="rel_scale_win", align_bytes=64)
+        ent_word_win = keep.tile([P, T], I32, name="ent_word_win", align_bytes=64)
+        ent_pairs = keep.tile([P, J], U32, name="ent_pairs", align_bytes=64)
+        ent_codes = keep.tile([P, 2, 2 * J], U8, name="ent_codes", align_bytes=64)
+        ent_scale_rows = keep.tile([P, J], U8, name="ent_scale_rows", align_bytes=64)
+        ent_scales = keep.tile([P, 2, J // 4], I32, name="ent_scales", align_bytes=64)
+        rel_word_win = keep.tile([P, T], I32, name="rel_word_win", align_bytes=64)
+        rel_codes = keep.tile([P, J], U32, name="rel_codes", align_bytes=64)
+        rel_scales = keep.tile([P, J], U8, name="rel_scales", align_bytes=64)
+        wr_raw_words = keep.tile([P, 2, R], I32, name="wr_raw_words", align_bytes=64)
+        wr_raw_scales = keep.tile([P, 2, R // 4], I32, name="wr_raw_scales", align_bytes=64)
+        wr_codes = keep.tile([P, 2, R], I32, name="wr_codes", align_bytes=64)
+        wr_scales = keep.tile([P, 2, R // 4], I32, name="wr_scales", align_bytes=64)
+        we_codes = keep.tile([P, 4, R], U32, name="we_codes", align_bytes=64)
+        we_scales = keep.tile([P, 4, R], U8, name="we_scales", align_bytes=64)
+        n_codes = keep.tile([P, 2, N], U32, name="n_codes", align_bytes=64)
+        n_scales = keep.tile([P, 2, N], U8, name="n_scales", align_bytes=64)
+
+        nc.vector.memset(rel_scale_win[:], 0)
+        nc.vector.memset(ent_scale_win[32:64, :], 0)
+        nc.vector.memset(ent_scale_win[64:P, :], 0)
+        nc.vector.memset(ent_scales[:], 0)
+        nc.gpsimd.memset(wr_raw_scales[:], 0)
+
+        def words_view(words):
+            return words[0].rearrange("p n i -> p (n i)").bitcast(I32)
+
+        def load_rows(src):
+            raw = stage.tile([P, PACK, R], F32, name="raw")
+            nc.sync.dma_start(out=raw[:], in_=src.rearrange("(p j) c -> p j c", j=PACK))
+            return raw
+
+        nc.sync.dma_start(ent_list[:], offs)
+        nc.sync.dma_start(out=ent_scale_win[0:32, :], in_=tab_scales.rearrange("a q t -> (a q) t").bitcast(I32))
+        nc.sync.dma_start(out=ent_word_win[:], in_=words_view(tab_words))
+        we_raw = [load_rows(wer[0:K_PASS, :]), load_rows(wer[K_PASS:K, :])]
+        nc.sync.dma_start(rel_list[:], offs2)
+        we_raw += [load_rows(wei[0:K_PASS, :]), load_rows(wei[K_PASS:K, :])]
+        for w, words in enumerate((wrr_words, wri_words)):
+            nc.sync.dma_start(out=wr_raw_words[:, w, :], in_=words_view(words))
+        nc.sync.dma_start(out=rel_word_win[:], in_=words_view(tab2_words))
+        for row in range(4):
+            nc.gpsimd.dma_start(out=rel_scale_win[row:P:32, :], in_=tab2_scales[0].bitcast(I32)[row:16:4, :])
+        for w, scales in enumerate((wrr_scales, wri_scales)):
+            for row in range(4):
+                nc.gpsimd.dma_start(out=wr_raw_scales[row:P:32, w, :], in_=scales[0].bitcast(I32)[row:16:4, :])
+
+        nc.vector.tensor_copy(ent_scale_rows[:], ent_scale_win[:].bitcast(U8).indirect(ent_list[:]))
+        for a in range(2):
+            for row in range(4):
+                nc.gpsimd.dma_start(
+                    out=ent_scales[row:P:32, a, :], in_=ent_scale_rows[:].bitcast(I32)[16 * a + row:16 * (a + 1):4, :]
+                )
+
+        def gather(chunk, part):
+            cols = slice(chunk * CHUNK, (chunk + 1) * CHUNK)
+            entries = slice(chunk * CHUNK // LANES, (chunk + 1) * CHUNK // LANES)
+            if part == 0:
+                nc.vector.tensor_copy(ent_pairs[:, cols], ent_word_win[:].bitcast(U32).indirect(ent_list[:, entries]))
+            elif part == 1:
+                nc.vector.tensor_copy(
+                    out=ent_codes[:].bitcast(U16)[:, :, cols],
+                    in_=ent_pairs[:, cols].bitcast(U16).rearrange("p (n d) -> p d n", d=2),
+                )
+            elif part == 2:
+                nc.vector.tensor_copy(rel_scales[:, cols], rel_scale_win[:].bitcast(U8).indirect(rel_list[:, entries]))
+            else:
+                nc.vector.tensor_copy(rel_codes[:, cols], rel_word_win[:].bitcast(U32).indirect(rel_list[:, entries]))
+
+        def quantise_entity_weight(piece):
+            grouped = ring.tile([P, PACK * R], BF16, name="grouped", align_bytes=64)
+            src = we_raw[piece][:].rearrange("p j (b t m) -> p t b m j", t=4, m=8)
+            dst = grouped[:].rearrange("p (t b m j) -> p t b m j", t=4, m=8, j=PACK)
+            for t in range(4):
+                nc.scalar.copy(out=dst[:, t], in_=src[:, t])
+            nc.vector.quantize_mx(out=we_codes[:, piece, :].bitcast(FP8X4), scales=we_scales[:, piece, :], in_=grouped[:])
+
+        def permute_relation_weight(w):
+            nc.vector.tensor_copy(
+                out=wr_codes[:, w, :].rearrange("p (t b m) -> p t b m", t=4, m=8),
+                in_=wr_raw_words[:, w, :].rearrange("p (b t m) -> p t b m", t=4, m=8),
+            )
+            nc.vector.tensor_copy(
+                out=wr_scales[:, w, :].rearrange("p (t b m) -> p t b m", t=4, m=2),
+                in_=wr_raw_scales[:, w, :].rearrange("p (b t m) -> p t b m", t=4, m=2),
+            )
+
+        for chunk in range(4):
+            gather(chunk, 0)
+            gather(chunk, 1)
+        quantise_entity_weight(0)
+        quantise_entity_weight(1)
+        gather(0, 2)
+        gather(1, 2)
+        permute_relation_weight(0)
+        permute_relation_weight(1)
+        quantise_entity_weight(2)
+        gather(2, 2)
+        gather(3, 2)
+        quantise_entity_weight(3)
+        gather(0, 3)
+        gather(1, 3)
+
+        n_raw = []
+        for src in (nr, ni):
+            raw = stage.tile([P, PACK, N], F32, name="raw")
+            rows = src.rearrange("(b t m) n -> t b m n", t=4, m=8)
+            for t in range(4):
+                nc.sync.dma_start(out=raw[:, t, :], in_=rows[t])
+            n_raw.append(raw)
+
+        def cast_candidates(w):
+            grouped = ring.tile([P, PACK * N], BF16, name="grouped", align_bytes=64)
+            src = n_raw[w][:].rearrange("p t n -> p n t")
+            dst = grouped[:].rearrange("p (n t) -> p n t", t=PACK)
+            for a in range(4):
+                nc.scalar.copy(out=dst[:, a * P:(a + 1) * P, :], in_=src[:, a * P:(a + 1) * P, :])
+            return grouped
+
+        def quantise_candidates(w, grouped):
+            nc.vector.quantize_mx(out=n_codes[:, w, :].bitcast(FP8X4), scales=n_scales[:, w, :], in_=grouped[:])
+
+        ent_planes = ent_scales[:].bitcast(U8)
+        wr_planes = wr_scales[:].bitcast(U8)
+
+        def project(step):
+            cols = slice(step * STEP, (step + 1) * STEP)
+            rel = [
+                keep.tile([P, STEP, PACK], F32, name="rel_re", tag="turn%d" % (step % 3), align_bytes=64),
+                ring.tile([P, STEP, PACK], F32, name="rel_im"),
+            ]
+            for w in range(2):
+                bank = psum1.tile([P, PACK, STEP], F32, name="rel_bank", tag="rel%d" % w)
+                for t in range(4):
+                    nc.tensor.matmul_mx(
+                        out=bank[:, t, :],
+                        lhsT=wr_codes[:, w, t * P:(t + 1) * P].bitcast(FP8X4),
+                        lhsT_scale=wr_planes[:, w, t * P:(t + 1) * P],
+                        rhs=rel_codes[:, cols].bitcast(FP8X4),
+                        rhs_scale=rel_scales[:, cols],
+                        start=True,
+                        stop=True,
+                    )
+                nc.scalar.copy(out=rel[w][:], in_=bank[:].rearrange("p t n -> p n t"))
+            ent = []
+            for w in range(2):
+                bank = psum2.tile([P, PACK, STEP], F32, name="ent_bank", tag="ent%d" % w)
+                for t in range(4):
+                    for a in range(2):
+                        nc.tensor.matmul_mx(
+                            out=bank[:, t, :],
+                            lhsT=we_codes[:, 2 * w + a, t * P:(t + 1) * P].bitcast(FP8X4),
+                            lhsT_scale=we_scales[:, 2 * w + a, t * P:(t + 1) * P],
+                            rhs=ent_codes[:, a, 2 * step * STEP:2 * (step + 1) * STEP].bitcast(FP4X4),
+                            rhs_scale=ent_planes[:, a, cols],
+                            start=(a == 0),
+                            stop=(a == 1),
+                        )
+                ent.append(bank[:].rearrange("p t n -> p n t"))
+            return ent, rel
+
+        def multiply(ent, rel):
+            first = ring.tile([P, 2, STEP, PACK], F32, name="first")
+            second = ring.tile([P, 2, STEP, PACK], F32, name="second")
+            nc.vector.tensor_tensor(first[:, 0], ent[0], rel[0][:], MULT)
+            nc.vector.tensor_tensor(second[:, 1], ent[1], rel[0][:], MULT)
+            nc.vector.tensor_tensor(first[:, 1], ent[0], rel[1][:], MULT)
+            nc.vector.scalar_tensor_tensor(second[:, 0], ent[1], -1.0, rel[1][:], MULT, MULT)
+            return first, second
+
+        def add_products(first, second, adder):
+            h = ring.tile([P, 2 * STEP * PACK], BF16, name="h", align_bytes=64, bufs=4)
+            adder.tensor_tensor(
+                h[:], first[:].rearrange("p w n t -> p (w n t)"), second[:].rearrange("p w n t -> p (w n t)"), ADD
+            )
+            return h
+
+        out_view = out.rearrange("(a p) j -> p a j", p=P)
+
+        def score(step, h, turn):
+            h_codes = keep.tile([P, 2 * STEP], U32, name="h_codes", tag="turn%d" % (turn % 3), align_bytes=64)
+            h_scales = ring.tile([P, 2 * STEP], U8, name="h_scales", align_bytes=64)
+            nc.vector.quantize_mx(out=h_codes[:].bitcast(FP8X4), scales=h_scales[:], in_=h[:])
+            bank = psum2.tile([P, N // P, STEP], F32, name="score_bank", tag="score")
+            for a in range(N // P):
+                for w in range(2):
+                    nc.tensor.matmul_mx(
+                        out=bank[:, a, :],
+                        lhsT=n_codes[:, w, a * P:(a + 1) * P].bitcast(FP8X4),
+                        lhsT_scale=n_scales[:, w, a * P:(a + 1) * P],
+                        rhs=h_codes[:, w * STEP:(w + 1) * STEP].bitcast(FP8X4),
+                        rhs_scale=h_scales[:, w * STEP:(w + 1) * STEP],
+                        start=(w == 0),
+                        stop=(w == 1),
+                    )
+            result = ring.tile([P, N // P, STEP], F32, name="result")
+            nc.scalar.activation(result[:], bank[:], SIGMOID)
+            nc.sync.dma_start(out=out_view[:, :, step * STEP:(step + 1) * STEP], in_=result[:])
+
+        steps = J // STEP
+        projected = [project(0)]
+        sums = []
+        for step in range(steps):
+            if step + 1 < steps:
+                projected.append(project(step + 1))
+            if step < 2:
+                grouped = cast_candidates(step)
+            first, second = multiply(*projected[step])
+            if step + 1 < steps:
+                sums.append(add_products(first, second, nc.gpsimd))
+            if step < 2:
+                quantise_candidates(step, grouped)
+            else:
+                score(step - 2, sums[step - 2], step)
+            if step in (3, 7):
+                gather(step // 4 + 2, 3)
+        sums.append(add_products(first, second, nc.vector))
+        score(steps - 2, sums[steps - 2], steps)
+        score(steps - 1, sums[steps - 1], steps + 1)

@@ -33,21 +33,19 @@ def tile_list_ckg_sig_kernel(
     with ExitStack() as ctx:
         lists = ctx.enter_context(tc.tile_pool(name="lists", bufs=1))
         keep = ctx.enter_context(tc.tile_pool(name="keep", bufs=1))
-        stage = ctx.enter_context(tc.tile_pool(name="stage", bufs=4))
         ring = ctx.enter_context(tc.tile_pool(name="ring", bufs=3))
         psum2 = ctx.enter_context(tc.psum_pool(name="psum2", bufs=2))
         psum1 = ctx.enter_context(tc.psum_pool(name="psum1", bufs=1))
 
         ent_list = lists.tile([P, J // LANES], U16, name="ent_list")
         rel_list = lists.tile([P, J // LANES], U16, name="rel_list")
-        ent_scale_win = keep.tile([P, T // 4], I32, name="ent_scale_win", align_bytes=64)
+        ent_scale_win = keep.tile([P, T // 4], I32, name="ent_scale_win", tag="shared", align_bytes=64)
         rel_scale_win = keep.tile([P, T // 4], I32, name="rel_scale_win", align_bytes=64)
         ent_word_win = keep.tile([P, T], I32, name="ent_word_win", align_bytes=64)
         ent_pairs = keep.tile([P, J], U32, name="ent_pairs", align_bytes=64)
         ent_codes = keep.tile([P, 2, 2 * J], U8, name="ent_codes", align_bytes=64)
         ent_scale_rows = keep.tile([P, J], U8, name="ent_scale_rows", align_bytes=64)
         ent_scales = keep.tile([P, 2, J // 4], I32, name="ent_scales", align_bytes=64)
-        rel_word_win = keep.tile([P, T], I32, name="rel_word_win", align_bytes=64)
         rel_codes = keep.tile([P, J], U32, name="rel_codes", align_bytes=64)
         rel_scales = keep.tile([P, J], U8, name="rel_scales", align_bytes=64)
         wr_raw_words = keep.tile([P, 2, R], I32, name="wr_raw_words", align_bytes=64)
@@ -68,20 +66,19 @@ def tile_list_ckg_sig_kernel(
         def words_view(words):
             return words[0].rearrange("p n i -> p (n i)").bitcast(I32)
 
-        def load_rows(src):
-            raw = stage.tile([P, PACK, R], F32, name="raw")
+        def load_rows(src, piece):
+            raw = keep.tile([P, PACK, R], F32, name="raw", tag="raw%d" % piece)
             nc.sync.dma_start(out=raw[:], in_=src.rearrange("(p j) c -> p j c", j=PACK))
             return raw
 
         nc.sync.dma_start(ent_list[:], offs)
         nc.sync.dma_start(out=ent_scale_win[0:32, :], in_=tab_scales.rearrange("a q t -> (a q) t").bitcast(I32))
         nc.sync.dma_start(out=ent_word_win[:], in_=words_view(tab_words))
-        we_raw = [load_rows(wer[0:K_PASS, :]), load_rows(wer[K_PASS:K, :])]
+        we_raw = [load_rows(wer[0:K_PASS, :], 0), load_rows(wer[K_PASS:K, :], 1)]
         nc.sync.dma_start(rel_list[:], offs2)
-        we_raw += [load_rows(wei[0:K_PASS, :]), load_rows(wei[K_PASS:K, :])]
+        we_raw += [load_rows(wei[0:K_PASS, :], 2), load_rows(wei[K_PASS:K, :], 3)]
         for w, words in enumerate((wrr_words, wri_words)):
             nc.sync.dma_start(out=wr_raw_words[:, w, :], in_=words_view(words))
-        nc.sync.dma_start(out=rel_word_win[:], in_=words_view(tab2_words))
         for row in range(4):
             nc.gpsimd.dma_start(out=rel_scale_win[row:P:32, :], in_=tab2_scales[0].bitcast(I32)[row:16:4, :])
         for w, scales in enumerate((wrr_scales, wri_scales)):
@@ -89,11 +86,13 @@ def tile_list_ckg_sig_kernel(
                 nc.gpsimd.dma_start(out=wr_raw_scales[row:P:32, w, :], in_=scales[0].bitcast(I32)[row:16:4, :])
 
         nc.vector.tensor_copy(ent_scale_rows[:], ent_scale_win[:].bitcast(U8).indirect(ent_list[:]))
-        for a in range(2):
+        for a, queue in enumerate((nc.sync, nc.gpsimd)):
             for row in range(4):
-                nc.gpsimd.dma_start(
+                queue.dma_start(
                     out=ent_scales[row:P:32, a, :], in_=ent_scale_rows[:].bitcast(I32)[16 * a + row:16 * (a + 1):4, :]
                 )
+        rel_word_win = keep.tile([P, T], I32, name="rel_word_win", tag="shared", align_bytes=64)
+        nc.sync.dma_start(out=rel_word_win[:], in_=words_view(tab2_words))
 
         def gather(chunk, part):
             cols = slice(chunk * CHUNK, (chunk + 1) * CHUNK)
@@ -145,8 +144,8 @@ def tile_list_ckg_sig_kernel(
         gather(1, 3)
 
         n_raw = []
-        for src in (nr, ni):
-            raw = stage.tile([P, PACK, N], F32, name="raw")
+        for w, src in enumerate((nr, ni)):
+            raw = keep.tile([P, PACK, N], F32, name="raw", tag="raw%d" % (2 + w))
             rows = src.rearrange("(b t m) n -> t b m n", t=4, m=8)
             for t in range(4):
                 nc.sync.dma_start(out=raw[:, t, :], in_=rows[t])
@@ -220,10 +219,13 @@ def tile_list_ckg_sig_kernel(
 
         out_view = out.rearrange("(a p) j -> p a j", p=P)
 
-        def score(step, h, turn):
+        def quantise_sum(h, turn):
             h_codes = keep.tile([P, 2 * STEP], U32, name="h_codes", tag="turn%d" % (turn % 3), align_bytes=64)
             h_scales = ring.tile([P, 2 * STEP], U8, name="h_scales", align_bytes=64)
             nc.vector.quantize_mx(out=h_codes[:].bitcast(FP8X4), scales=h_scales[:], in_=h[:])
+            return h_codes, h_scales
+
+        def score(step, h_codes, h_scales):
             bank = psum2.tile([P, N // P, STEP], F32, name="score_bank", tag="score")
             for a in range(N // P):
                 for w in range(2):
@@ -243,9 +245,12 @@ def tile_list_ckg_sig_kernel(
         steps = J // STEP
         projected = [project(0)]
         sums = []
+        quantised = []
         for step in range(steps):
             if step + 1 < steps:
                 projected.append(project(step + 1))
+            if step >= 3:
+                score(step - 3, *quantised[step - 3])
             if step < 2:
                 grouped = cast_candidates(step)
             first, second = multiply(*projected[step])
@@ -254,9 +259,10 @@ def tile_list_ckg_sig_kernel(
             if step < 2:
                 quantise_candidates(step, grouped)
             else:
-                score(step - 2, sums[step - 2], step)
+                quantised.append(quantise_sum(sums[step - 2], step))
             if step in (3, 7):
                 gather(step // 4 + 2, 3)
+        score(steps - 3, *quantised[steps - 3])
         sums.append(add_products(first, second, nc.vector))
-        score(steps - 2, sums[steps - 2], steps)
-        score(steps - 1, sums[steps - 1], steps + 1)
+        for step in (steps - 2, steps - 1):
+            score(step, *quantise_sum(sums[step], step + 2))

@@ -49,7 +49,8 @@ def tile_list_ckg_sig_kernel(
         rel_codes = keep.tile([P, J], U32, name="rel_codes", align_bytes=64)
         rel_scales = keep.tile([P, J], U8, name="rel_scales", align_bytes=64)
         wr_raw_words = keep.tile([P, 2, R], I32, name="wr_raw_words", align_bytes=64)
-        wr_raw_scales = keep.tile([P, 2, R // 4], I32, name="wr_raw_scales", align_bytes=64)
+        wr_raw_scales = keep.tile([16, 2, R // 4], I32, name="wr_raw_scales", align_bytes=64)
+        wr_scale_rows = keep.tile([16, 2, R // 4], I32, name="wr_scale_rows", align_bytes=64)
         wr_codes = keep.tile([P, 2, R], I32, name="wr_codes", align_bytes=64)
         wr_scales = keep.tile([P, 2, R // 4], I32, name="wr_scales", align_bytes=64)
         we_codes = keep.tile([P, 4, R], U32, name="we_codes", align_bytes=64)
@@ -57,11 +58,9 @@ def tile_list_ckg_sig_kernel(
         n_codes = keep.tile([P, 2, N], U32, name="n_codes", align_bytes=64)
         n_scales = keep.tile([P, 2, N], U8, name="n_scales", align_bytes=64)
 
-        nc.vector.memset(rel_scale_win[:], 0)
         nc.vector.memset(ent_scale_win[32:64, :], 0)
         nc.vector.memset(ent_scale_win[64:P, :], 0)
-        nc.vector.memset(ent_scales[:], 0)
-        nc.gpsimd.memset(wr_raw_scales[:], 0)
+        nc.gpsimd.memset(rel_scale_win[:], 0)
 
         def words_view(words):
             return words[0].rearrange("p n i -> p (n i)").bitcast(I32)
@@ -74,20 +73,29 @@ def tile_list_ckg_sig_kernel(
         nc.sync.dma_start(ent_list[:], offs)
         nc.sync.dma_start(out=ent_scale_win[0:32, :], in_=tab_scales.rearrange("a q t -> (a q) t").bitcast(I32))
         nc.sync.dma_start(out=ent_word_win[:], in_=words_view(tab_words))
+        for w, scales in enumerate((wrr_scales, wri_scales)):
+            nc.sync.dma_start(out=wr_raw_scales[:, w, :], in_=scales[0].bitcast(I32))
         we_raw = [load_rows(wer[0:K_PASS, :], 0), load_rows(wer[K_PASS:K, :], 1)]
         nc.sync.dma_start(rel_list[:], offs2)
-        we_raw += [load_rows(wei[0:K_PASS, :], 2), load_rows(wei[K_PASS:K, :], 3)]
         for w, words in enumerate((wrr_words, wri_words)):
             nc.sync.dma_start(out=wr_raw_words[:, w, :], in_=words_view(words))
+        we_raw += [load_rows(wei[0:K_PASS, :], 2), load_rows(wei[K_PASS:K, :], 3)]
         for row in range(4):
             nc.gpsimd.dma_start(out=rel_scale_win[row:P:32, :], in_=tab2_scales[0].bitcast(I32)[row:16:4, :])
-        for w, scales in enumerate((wrr_scales, wri_scales)):
-            for row in range(4):
-                nc.gpsimd.dma_start(out=wr_raw_scales[row:P:32, w, :], in_=scales[0].bitcast(I32)[row:16:4, :])
+        nc.gpsimd.memset(ent_scales[:], 0)
+        nc.gpsimd.memset(wr_scales[:], 0)
 
         nc.vector.tensor_copy(ent_scale_rows[:], ent_scale_win[:].bitcast(U8).indirect(ent_list[:]))
-        for a, queue in enumerate((nc.sync, nc.gpsimd)):
+        for w in range(2):
+            nc.vector.tensor_copy(
+                out=wr_scale_rows[:, w, :].rearrange("p (t b m) -> p t b m", t=4, m=2),
+                in_=wr_raw_scales[:, w, :].rearrange("p (b t m) -> p t b m", t=4, m=2),
+            )
+        for row in range(4):
+            nc.gpsimd.dma_start(out=wr_scales[row:P:32], in_=wr_scale_rows[row:16:4])
+        for a in range(2):
             for row in range(4):
+                queue = nc.sync if row < 3 else nc.gpsimd
                 queue.dma_start(
                     out=ent_scales[row:P:32, a, :], in_=ent_scale_rows[:].bitcast(I32)[16 * a + row:16 * (a + 1):4, :]
                 )
@@ -121,10 +129,6 @@ def tile_list_ckg_sig_kernel(
             nc.vector.tensor_copy(
                 out=wr_codes[:, w, :].rearrange("p (t b m) -> p t b m", t=4, m=8),
                 in_=wr_raw_words[:, w, :].rearrange("p (b t m) -> p t b m", t=4, m=8),
-            )
-            nc.vector.tensor_copy(
-                out=wr_scales[:, w, :].rearrange("p (t b m) -> p t b m", t=4, m=2),
-                in_=wr_raw_scales[:, w, :].rearrange("p (b t m) -> p t b m", t=4, m=2),
             )
 
         for chunk in range(4):

@@ -55,11 +55,13 @@ def tile_list_ckg_sig_kernel(
         wr_scales = keep.tile([P, 2, R // 4], I32, name="wr_scales", align_bytes=64)
         we_codes = keep.tile([P, 4, R], U32, name="we_codes", align_bytes=64)
         we_scales = keep.tile([P, 4, R], U8, name="we_scales", align_bytes=64)
-        n_codes = keep.tile([P, 2, N], U32, name="n_codes", align_bytes=64)
         n_scales = keep.tile([P, 2, N], U8, name="n_scales", align_bytes=64)
 
         nc.vector.memset(ent_scale_win[32:64, :], 0)
         nc.vector.memset(ent_scale_win[64:P, :], 0)
+        warm = keep.tile([P, 2], F32, name="warm")
+        nc.vector.memset(warm[:, 0:1], 0.0)
+        nc.scalar.activation(warm[:, 1:2], warm[:, 0:1], SIGMOID)
         nc.gpsimd.memset(rel_scale_win[:], 0)
 
         def words_view(words):
@@ -155,16 +157,21 @@ def tile_list_ckg_sig_kernel(
                 nc.sync.dma_start(out=raw[:, t, :], in_=rows[t])
             n_raw.append(raw)
 
-        def cast_candidates(w):
-            grouped = ring.tile([P, PACK * N], BF16, name="grouped", align_bytes=64)
-            src = n_raw[w][:].rearrange("p t n -> p n t")
-            dst = grouped[:].rearrange("p (n t) -> p n t", t=PACK)
-            for a in range(4):
-                nc.scalar.copy(out=dst[:, a * P:(a + 1) * P, :], in_=src[:, a * P:(a + 1) * P, :])
-            return grouped
+        n_grouped = keep.tile([P, 2, N * PACK], BF16, name="n_grouped", align_bytes=64)
 
-        def quantise_candidates(w, grouped):
-            nc.vector.quantize_mx(out=n_codes[:, w, :].bitcast(FP8X4), scales=n_scales[:, w, :], in_=grouped[:])
+        n_codes = []
+
+        def cast_candidates(w, half):
+            cols = slice(half * N // 2, (half + 1) * N // 2)
+            nc.scalar.copy(
+                out=n_grouped[:, w, :].rearrange("p (n t) -> p n t", t=PACK)[:, cols, :],
+                in_=n_raw[w][:].rearrange("p t n -> p n t")[:, cols, :],
+            )
+
+        def quantise_candidates(w):
+            codes = keep.tile([P, N], U32, name="n_codes", tag="cand%d" % w, align_bytes=64)
+            nc.vector.quantize_mx(out=codes[:].bitcast(FP8X4), scales=n_scales[:, w, :], in_=n_grouped[:, w, :])
+            n_codes.append(codes)
 
         ent_planes = ent_scales[:].bitcast(U8)
         wr_planes = wr_scales[:].bitcast(U8)
@@ -172,8 +179,10 @@ def tile_list_ckg_sig_kernel(
         def project(step):
             cols = slice(step * STEP, (step + 1) * STEP)
             rel = [
-                keep.tile([P, STEP, PACK], F32, name="rel_re", tag="turn%d" % (step % 3), align_bytes=64),
-                ring.tile([P, STEP, PACK], F32, name="rel_im"),
+                keep.tile([P, STEP, PACK], F32, name="rel_re", tag="turn%d" % (step % 4), align_bytes=64),
+                keep.tile([P, STEP, PACK], F32, name="rel_im", tag="cand%d" % (step - 2), align_bytes=64)
+                if step in (2, 3)
+                else ring.tile([P, STEP, PACK], F32, name="rel_im"),
             ]
             for w in range(2):
                 bank = psum1.tile([P, PACK, STEP], F32, name="rel_bank", tag="rel%d" % w)
@@ -224,8 +233,8 @@ def tile_list_ckg_sig_kernel(
         out_view = out.rearrange("(a p) j -> p a j", p=P)
 
         def quantise_sum(h, turn):
-            h_codes = keep.tile([P, 2 * STEP], U32, name="h_codes", tag="turn%d" % (turn % 3), align_bytes=64)
-            h_scales = ring.tile([P, 2 * STEP], U8, name="h_scales", align_bytes=64)
+            h_codes = keep.tile([P, 2 * STEP], U32, name="h_codes", tag="turn%d" % (turn % 4), align_bytes=64)
+            h_scales = ring.tile([P, 2 * STEP], U8, name="h_scales", align_bytes=64, bufs=4)
             nc.vector.quantize_mx(out=h_codes[:].bitcast(FP8X4), scales=h_scales[:], in_=h[:])
             return h_codes, h_scales
 
@@ -235,7 +244,7 @@ def tile_list_ckg_sig_kernel(
                 for w in range(2):
                     nc.tensor.matmul_mx(
                         out=bank[:, a, :],
-                        lhsT=n_codes[:, w, a * P:(a + 1) * P].bitcast(FP8X4),
+                        lhsT=n_codes[w][:, a * P:(a + 1) * P].bitcast(FP8X4),
                         lhsT_scale=n_scales[:, w, a * P:(a + 1) * P],
                         rhs=h_codes[:, w * STEP:(w + 1) * STEP].bitcast(FP8X4),
                         rhs_scale=h_scales[:, w * STEP:(w + 1) * STEP],
@@ -253,19 +262,24 @@ def tile_list_ckg_sig_kernel(
         for step in range(steps):
             if step + 1 < steps:
                 projected.append(project(step + 1))
-            if step >= 3:
+            if step == 4:
+                score(0, *quantised[0])
+            if step >= 4:
                 score(step - 3, *quantised[step - 3])
-            if step < 2:
-                grouped = cast_candidates(step)
+            if step == 0:
+                cast_candidates(0, 0)
+                cast_candidates(0, 1)
+            if step in (1, 2):
+                cast_candidates(1, step - 1)
             first, second = multiply(*projected[step])
             if step + 1 < steps:
                 sums.append(add_products(first, second, nc.gpsimd))
-            if step < 2:
-                quantise_candidates(step, grouped)
-            else:
+            if step >= 2:
                 quantised.append(quantise_sum(sums[step - 2], step))
-            if step in (3, 7):
-                gather(step // 4 + 2, 3)
+            if step in (2, 3):
+                quantise_candidates(step - 2)
+            if step in (5, 9):
+                gather(step // 4 + 1, 3)
         score(steps - 3, *quantised[steps - 3])
         sums.append(add_products(first, second, nc.vector))
         for step in (steps - 2, steps - 1):

@@ -34,22 +34,24 @@ def tile_list_ckg_sig_kernel(
         lists = ctx.enter_context(tc.tile_pool(name="lists", bufs=1))
         keep = ctx.enter_context(tc.tile_pool(name="keep", bufs=1))
         ring = ctx.enter_context(tc.tile_pool(name="ring", bufs=3))
+        arena = ctx.enter_context(tc.tile_pool(name="arena", bufs=1))
         psum2 = ctx.enter_context(tc.psum_pool(name="psum2", bufs=2))
         psum1 = ctx.enter_context(tc.psum_pool(name="psum1", bufs=1))
 
+        def placed(shape, dtype, name, kib):
+            return arena.tile(shape, dtype, name=name, tag=name, offset=int(kib * 1024), align_bytes=64)
+
         ent_list = lists.tile([P, J // LANES], U16, name="ent_list")
         rel_list = lists.tile([P, J // LANES], U16, name="rel_list")
-        ent_scale_win = keep.tile([P, T // 4], I32, name="ent_scale_win", tag="shared", align_bytes=64)
-        rel_scale_win = keep.tile([P, T // 4], I32, name="rel_scale_win", align_bytes=64)
+        ent_scale_win = placed([P, T // 4], I32, "ent_scale_win", 22)
+        rel_scale_win = placed([P, T // 4], I32, "rel_scale_win", 54)
         ent_word_win = keep.tile([P, T], I32, name="ent_word_win", align_bytes=64)
-        ent_pairs = keep.tile([P, J], U32, name="ent_pairs", align_bytes=64)
         ent_codes = keep.tile([P, 2, 2 * J], U8, name="ent_codes", align_bytes=64)
-        ent_scale_rows = keep.tile([P, J], U8, name="ent_scale_rows", align_bytes=64)
-        ent_scales = keep.tile([P, 2, J // 4], I32, name="ent_scales", align_bytes=64)
-        rel_codes = keep.tile([P, J], U32, name="rel_codes", align_bytes=64)
-        rel_scales = keep.tile([P, J], U8, name="rel_scales", align_bytes=64)
-        wr_raw_words = keep.tile([P, 2, R], I32, name="wr_raw_words", align_bytes=64)
-        wr_raw_scales = keep.tile([16, 2, R // 4], I32, name="wr_raw_scales", align_bytes=64)
+        scale_rows = keep.tile([P, 2, J], U8, name="scale_rows", align_bytes=64)
+        planes = keep.tile([P, 3, J // 4], I32, name="planes", align_bytes=64)
+        rel_codes = [keep.tile([P, CHUNK], U32, name="rel_codes%d" % c, align_bytes=64) for c in range(4)]
+        wr_raw_words = placed([P, 2, R], I32, "wr_raw_words", 32)
+        wr_raw_scales = placed([16, 2, R // 4], I32, "wr_raw_scales", 7.5)
         wr_scale_rows = keep.tile([16, 2, R // 4], I32, name="wr_scale_rows", align_bytes=64)
         wr_codes = keep.tile([P, 2, R], I32, name="wr_codes", align_bytes=64)
         wr_scales = keep.tile([P, 2, R // 4], I32, name="wr_scales", align_bytes=64)
@@ -57,52 +59,60 @@ def tile_list_ckg_sig_kernel(
         we_scales = keep.tile([P, 4, R], U8, name="we_scales", align_bytes=64)
         n_scales = keep.tile([P, 2, N], U8, name="n_scales", align_bytes=64)
 
+        nc.vector.memset(rel_scale_win[:], 0)
         nc.vector.memset(ent_scale_win[32:64, :], 0)
         nc.vector.memset(ent_scale_win[64:P, :], 0)
         warm = keep.tile([P, 2], F32, name="warm")
-        nc.vector.memset(warm[:, 0:1], 0.0)
+        nc.gpsimd.memset(wr_scales[:], 0)
+        nc.gpsimd.memset(warm[:, 0:1], 0.0)
         nc.scalar.activation(warm[:, 1:2], warm[:, 0:1], SIGMOID)
-        nc.gpsimd.memset(rel_scale_win[:], 0)
+        nc.gpsimd.memset(planes[:], 0)
 
         def words_view(words):
             return words[0].rearrange("p n i -> p (n i)").bitcast(I32)
 
         def load_rows(src, piece):
-            raw = keep.tile([P, PACK, R], F32, name="raw", tag="raw%d" % piece)
+            raw = placed([P, PACK, R], F32, "raw%d" % piece, 8 * piece)
             nc.sync.dma_start(out=raw[:], in_=src.rearrange("(p j) c -> p j c", j=PACK))
             return raw
 
-        nc.sync.dma_start(ent_list[:], offs)
-        nc.sync.dma_start(out=ent_scale_win[0:32, :], in_=tab_scales.rearrange("a q t -> (a q) t").bitcast(I32))
-        nc.sync.dma_start(out=ent_word_win[:], in_=words_view(tab_words))
+        def permute_relation_weight(w):
+            nc.vector.tensor_copy(
+                out=wr_codes[:, w, :].rearrange("p (t b m) -> p t b m", t=4, m=8),
+                in_=wr_raw_words[:, w, :].rearrange("p (b t m) -> p t b m", t=4, m=8),
+            )
+
         for w, scales in enumerate((wrr_scales, wri_scales)):
             nc.sync.dma_start(out=wr_raw_scales[:, w, :], in_=scales[0].bitcast(I32))
-        we_raw = [load_rows(wer[0:K_PASS, :], 0), load_rows(wer[K_PASS:K, :], 1)]
+        nc.sync.dma_start(ent_list[:], offs)
+        nc.sync.dma_start(out=ent_scale_win[0:32, :], in_=tab_scales.rearrange("a q t -> (a q) t").bitcast(I32))
         nc.sync.dma_start(rel_list[:], offs2)
+        nc.sync.dma_start(out=ent_word_win[:], in_=words_view(tab_words))
         for w, words in enumerate((wrr_words, wri_words)):
             nc.sync.dma_start(out=wr_raw_words[:, w, :], in_=words_view(words))
-        we_raw += [load_rows(wei[0:K_PASS, :], 2), load_rows(wei[K_PASS:K, :], 3)]
-        for row in range(4):
-            nc.gpsimd.dma_start(out=rel_scale_win[row:P:32, :], in_=tab2_scales[0].bitcast(I32)[row:16:4, :])
-        nc.gpsimd.memset(ent_scales[:], 0)
-        nc.gpsimd.memset(wr_scales[:], 0)
+        nc.sync.dma_start(out=rel_scale_win[0:16, :], in_=tab2_scales[0].bitcast(I32))
 
-        nc.vector.tensor_copy(ent_scale_rows[:], ent_scale_win[:].bitcast(U8).indirect(ent_list[:]))
         for w in range(2):
             nc.vector.tensor_copy(
                 out=wr_scale_rows[:, w, :].rearrange("p (t b m) -> p t b m", t=4, m=2),
                 in_=wr_raw_scales[:, w, :].rearrange("p (b t m) -> p t b m", t=4, m=2),
             )
+        we_raw = [load_rows(wer[0:K_PASS, :], 0), load_rows(wer[K_PASS:K, :], 1)]
         for row in range(4):
-            nc.gpsimd.dma_start(out=wr_scales[row:P:32], in_=wr_scale_rows[row:16:4])
-        for a in range(2):
-            for row in range(4):
-                queue = nc.sync if row < 3 else nc.gpsimd
-                queue.dma_start(
-                    out=ent_scales[row:P:32, a, :], in_=ent_scale_rows[:].bitcast(I32)[16 * a + row:16 * (a + 1):4, :]
-                )
-        rel_word_win = keep.tile([P, T], I32, name="rel_word_win", tag="shared", align_bytes=64)
+            nc.sync.dma_start(out=wr_scales[row:P:32], in_=wr_scale_rows[row:16:4])
+        nc.vector.tensor_copy(scale_rows[:, 1, :], ent_scale_win[:].bitcast(U8).indirect(ent_list[:]))
+        we_raw += [load_rows(wei[0:K_PASS, :], 2), load_rows(wei[K_PASS:K, :], 3)]
+        permute_relation_weight(0)
+        permute_relation_weight(1)
+        nc.vector.tensor_copy(scale_rows[:, 0, :], rel_scale_win[:].bitcast(U8).indirect(rel_list[:]))
+        rel_word_win = placed([P, T], I32, "rel_word_win", 40)
         nc.sync.dma_start(out=rel_word_win[:], in_=words_view(tab2_words))
+        ent_pairs = placed([P, J], U32, "ent_pairs", 56)
+        rows = scale_rows[:].bitcast(I32)
+        for row in range(4):
+            nc.sync.dma_start(out=planes[row:P:32, 0:2, :], in_=rows[row:16:4])
+        for row in range(4):
+            nc.sync.dma_start(out=planes[row:P:32, 2, :], in_=rows[16 + row:32:4, 1, :])
 
         def gather(chunk, part):
             cols = slice(chunk * CHUNK, (chunk + 1) * CHUNK)
@@ -114,44 +124,30 @@ def tile_list_ckg_sig_kernel(
                     out=ent_codes[:].bitcast(U16)[:, :, cols],
                     in_=ent_pairs[:, cols].bitcast(U16).rearrange("p (n d) -> p d n", d=2),
                 )
-            elif part == 2:
-                nc.vector.tensor_copy(rel_scales[:, cols], rel_scale_win[:].bitcast(U8).indirect(rel_list[:, entries]))
             else:
-                nc.vector.tensor_copy(rel_codes[:, cols], rel_word_win[:].bitcast(U32).indirect(rel_list[:, entries]))
+                nc.vector.tensor_copy(rel_codes[chunk][:], rel_word_win[:].bitcast(U32).indirect(rel_list[:, entries]))
 
         def quantise_entity_weight(piece):
-            grouped = ring.tile([P, PACK * R], BF16, name="grouped", align_bytes=64)
+            grouped = ring.tile([P, PACK * R], BF16, name="grouped", align_bytes=64, bufs=4)
             src = we_raw[piece][:].rearrange("p j (b t m) -> p t b m j", t=4, m=8)
             dst = grouped[:].rearrange("p (t b m j) -> p t b m j", t=4, m=8, j=PACK)
             for t in range(4):
                 nc.scalar.copy(out=dst[:, t], in_=src[:, t])
             nc.vector.quantize_mx(out=we_codes[:, piece, :].bitcast(FP8X4), scales=we_scales[:, piece, :], in_=grouped[:])
 
-        def permute_relation_weight(w):
-            nc.vector.tensor_copy(
-                out=wr_codes[:, w, :].rearrange("p (t b m) -> p t b m", t=4, m=8),
-                in_=wr_raw_words[:, w, :].rearrange("p (b t m) -> p t b m", t=4, m=8),
-            )
-
         for chunk in range(4):
             gather(chunk, 0)
             gather(chunk, 1)
         quantise_entity_weight(0)
         quantise_entity_weight(1)
-        gather(0, 2)
-        gather(1, 2)
-        permute_relation_weight(0)
-        permute_relation_weight(1)
         quantise_entity_weight(2)
-        gather(2, 2)
-        gather(3, 2)
         quantise_entity_weight(3)
         gather(0, 3)
         gather(1, 3)
 
         n_raw = []
         for w, src in enumerate((nr, ni)):
-            raw = keep.tile([P, PACK, N], F32, name="raw", tag="raw%d" % (2 + w))
+            raw = placed([P, PACK, N], F32, "n_raw%d" % w, 16 + 8 * w)
             rows = src.rearrange("(b t m) n -> t b m n", t=4, m=8)
             for t in range(4):
                 nc.sync.dma_start(out=raw[:, t, :], in_=rows[t])
@@ -173,7 +169,8 @@ def tile_list_ckg_sig_kernel(
             nc.vector.quantize_mx(out=codes[:].bitcast(FP8X4), scales=n_scales[:, w, :], in_=n_grouped[:, w, :])
             n_codes.append(codes)
 
-        ent_planes = ent_scales[:].bitcast(U8)
+        rel_scales = planes[:].bitcast(U8)[:, 0, :]
+        ent_planes = planes[:].bitcast(U8)[:, 1:3, :]
         wr_planes = wr_scales[:].bitcast(U8)
 
         def project(step):
@@ -191,7 +188,7 @@ def tile_list_ckg_sig_kernel(
                         out=bank[:, t, :],
                         lhsT=wr_codes[:, w, t * P:(t + 1) * P].bitcast(FP8X4),
                         lhsT_scale=wr_planes[:, w, t * P:(t + 1) * P],
-                        rhs=rel_codes[:, cols].bitcast(FP8X4),
+                        rhs=rel_codes[step // 4][:, step % 4 * STEP:(step % 4 + 1) * STEP].bitcast(FP8X4),
                         rhs_scale=rel_scales[:, cols],
                         start=True,
                         stop=True,

@@ -173,13 +173,13 @@ def tile_list_ckg_sig_kernel(
         ent_planes = planes[:].bitcast(U8)[:, 1:3, :]
         wr_planes = wr_scales[:].bitcast(U8)
 
-        def project(step):
+        def project_relation(step):
             cols = slice(step * STEP, (step + 1) * STEP)
             rel = [
-                keep.tile([P, STEP, PACK], F32, name="rel_re", tag="turn%d" % (step % 4), align_bytes=64),
+                ring.tile([P, STEP, PACK], F32, name="rel_re", bufs=4),
                 keep.tile([P, STEP, PACK], F32, name="rel_im", tag="cand%d" % (step - 2), align_bytes=64)
                 if step in (2, 3)
-                else ring.tile([P, STEP, PACK], F32, name="rel_im"),
+                else ring.tile([P, STEP, PACK], F32, name="rel_im", bufs=4),
             ]
             for w in range(2):
                 bank = psum1.tile([P, PACK, STEP], F32, name="rel_bank", tag="rel%d" % w)
@@ -194,8 +194,12 @@ def tile_list_ckg_sig_kernel(
                         stop=True,
                     )
                 nc.scalar.copy(out=rel[w][:], in_=bank[:].rearrange("p t n -> p n t"))
-            ent = []
-            for w in range(2):
+            return rel
+
+        def project_entity(step):
+            cols = slice(step * STEP, (step + 1) * STEP)
+            ent = {}
+            for w in (1, 0):
                 bank = psum2.tile([P, PACK, STEP], F32, name="ent_bank", tag="ent%d" % w)
                 for t in range(4):
                     for a in range(2):
@@ -208,8 +212,8 @@ def tile_list_ckg_sig_kernel(
                             start=(a == 0),
                             stop=(a == 1),
                         )
-                ent.append(bank[:].rearrange("p t n -> p n t"))
-            return ent, rel
+                ent[w] = bank[:].rearrange("p t n -> p n t")
+            return ent
 
         def multiply(ent, rel):
             first = ring.tile([P, 2, STEP, PACK], F32, name="first")
@@ -229,18 +233,18 @@ def tile_list_ckg_sig_kernel(
 
         out_view = out.rearrange("(a p) j -> p a j", p=P)
 
-        def quantise_sum(h, turn):
-            h_codes = keep.tile([P, 2 * STEP], U32, name="h_codes", tag="turn%d" % (turn % 4), align_bytes=64)
+        def quantise_sum(h):
+            h_codes = ring.tile([P, 2 * STEP], U32, name="h_codes", align_bytes=64, bufs=4)
             h_scales = ring.tile([P, 2 * STEP], U8, name="h_scales", align_bytes=64, bufs=4)
             nc.vector.quantize_mx(out=h_codes[:].bitcast(FP8X4), scales=h_scales[:], in_=h[:])
             return h_codes, h_scales
 
-        def score(step, h_codes, h_scales):
-            bank = psum2.tile([P, N // P, STEP], F32, name="score_bank", tag="score")
-            for a in range(N // P):
+        def score(step, h_codes, h_scales, blocks=range(N // P), queue=nc.sync):
+            bank = psum2.tile([P, len(blocks), STEP], F32, name="score_bank", tag="score")
+            for at, a in enumerate(blocks):
                 for w in range(2):
                     nc.tensor.matmul_mx(
-                        out=bank[:, a, :],
+                        out=bank[:, at, :],
                         lhsT=n_codes[w][:, a * P:(a + 1) * P].bitcast(FP8X4),
                         lhsT_scale=n_scales[:, w, a * P:(a + 1) * P],
                         rhs=h_codes[:, w * STEP:(w + 1) * STEP].bitcast(FP8X4),
@@ -248,17 +252,20 @@ def tile_list_ckg_sig_kernel(
                         start=(w == 0),
                         stop=(w == 1),
                     )
-            result = ring.tile([P, N // P, STEP], F32, name="result")
+            result = ring.tile([P, len(blocks), STEP], F32, name="result")
             nc.scalar.activation(result[:], bank[:], SIGMOID)
-            nc.sync.dma_start(out=out_view[:, :, step * STEP:(step + 1) * STEP], in_=result[:])
+            queue.dma_start(out=out_view[:, blocks[0]:blocks[-1] + 1, step * STEP:(step + 1) * STEP], in_=result[:])
 
         steps = J // STEP
-        projected = [project(0)]
+        rels = [project_relation(0), project_relation(1)]
+        ents = [project_entity(0)]
         sums = []
         quantised = []
         for step in range(steps):
+            if step + 2 < steps:
+                rels.append(project_relation(step + 2))
             if step + 1 < steps:
-                projected.append(project(step + 1))
+                ents.append(project_entity(step + 1))
             if step == 4:
                 score(0, *quantised[0])
             if step >= 4:
@@ -268,16 +275,17 @@ def tile_list_ckg_sig_kernel(
                 cast_candidates(0, 1)
             if step in (1, 2):
                 cast_candidates(1, step - 1)
-            first, second = multiply(*projected[step])
+            first, second = multiply(ents[step], rels[step])
             if step + 1 < steps:
                 sums.append(add_products(first, second, nc.gpsimd))
             if step >= 2:
-                quantised.append(quantise_sum(sums[step - 2], step))
+                quantised.append(quantise_sum(sums[step - 2]))
             if step in (2, 3):
                 quantise_candidates(step - 2)
             if step in (5, 9):
                 gather(step // 4 + 1, 3)
         score(steps - 3, *quantised[steps - 3])
-        sums.append(add_products(first, second, nc.vector))
-        for step in (steps - 2, steps - 1):
-            score(step, *quantise_sum(sums[step], step + 2))
+        score(steps - 2, *quantise_sum(sums[steps - 2]))
+        last = quantise_sum(add_products(first, second, nc.vector))
+        score(steps - 1, *last, blocks=range(0, 2))
+        score(steps - 1, *last, blocks=range(2, 4), queue=nc.scalar)

@@ -1,6 +1,7 @@
 from contextlib import ExitStack
 
 import concourse.mybir as mybir
+from concourse.masks import make_identity
 
 K, L, R, N, T, J = 1024, 512, 512, 512, 4096, 2048
 FLOPS = 2 * J * (2 * K * R + 2 * L * R + 2 * R * N)
@@ -23,6 +24,7 @@ K_PASS = P * PACK
 CHUNK = 512
 STEP = 128
 LANES = 16
+TURNED = J // STEP - 1
 
 
 def tile_list_ckg_sig_kernel(
@@ -63,10 +65,12 @@ def tile_list_ckg_sig_kernel(
         nc.vector.memset(ent_scale_win[32:64, :], 0)
         nc.vector.memset(ent_scale_win[64:P, :], 0)
         warm = keep.tile([P, 2], F32, name="warm")
-        nc.gpsimd.memset(wr_scales[:], 0)
+        nc.vector.memset(wr_scales[:], 0)
         nc.gpsimd.memset(warm[:, 0:1], 0.0)
         nc.scalar.activation(warm[:, 1:2], warm[:, 0:1], SIGMOID)
-        nc.gpsimd.memset(planes[:], 0)
+        nc.vector.memset(planes[:], 0)
+        identity = keep.tile([P, P], F32, name="identity")
+        make_identity(nc, identity[:])
 
         def words_view(words):
             return words[0].rearrange("p n i -> p (n i)").bitcast(I32)
@@ -181,8 +185,20 @@ def tile_list_ckg_sig_kernel(
                 if step in (2, 3)
                 else ring.tile([P, STEP, PACK], F32, name="rel_im", bufs=4),
             ]
-            for w in range(2):
+            for w in (step % 2, 1 - step % 2):
                 bank = psum1.tile([P, PACK, STEP], F32, name="rel_bank", tag="rel%d" % w)
+                if step == TURNED:
+                    nc.tensor.matmul_mx(
+                        out=bank[:].rearrange("p t n -> p (t n)"),
+                        lhsT=rel_codes[step // 4][:, step % 4 * STEP:(step % 4 + 1) * STEP].bitcast(FP8X4),
+                        lhsT_scale=rel_scales[:, cols],
+                        rhs=wr_codes[:, w, :].bitcast(FP8X4),
+                        rhs_scale=wr_planes[:, w, :],
+                        start=True,
+                        stop=True,
+                    )
+                    nc.scalar.copy(out=rel[w][:].rearrange("p n t -> p (n t)"), in_=bank[:].rearrange("p t n -> p (t n)"))
+                    continue
                 for t in range(4):
                     nc.tensor.matmul_mx(
                         out=bank[:, t, :],
@@ -201,6 +217,19 @@ def tile_list_ckg_sig_kernel(
             ent = {}
             for w in (1, 0):
                 bank = psum2.tile([P, PACK, STEP], F32, name="ent_bank", tag="ent%d" % w)
+                if step == TURNED:
+                    for a in range(2):
+                        nc.tensor.matmul_mx(
+                            out=bank[:].rearrange("p t n -> p (t n)"),
+                            lhsT=ent_codes[:, a, 2 * step * STEP:2 * (step + 1) * STEP].bitcast(FP4X4),
+                            lhsT_scale=ent_planes[:, a, cols],
+                            rhs=we_codes[:, 2 * w + a, :].bitcast(FP8X4),
+                            rhs_scale=we_scales[:, 2 * w + a, :],
+                            start=(a == 0),
+                            stop=(a == 1),
+                        )
+                    ent[w] = bank[:].rearrange("p t n -> p (t n)").rearrange("p (n t) -> p n t", t=PACK)
+                    continue
                 for t in range(4):
                     for a in range(2):
                         nc.tensor.matmul_mx(
@@ -231,11 +260,30 @@ def tile_list_ckg_sig_kernel(
             )
             return h
 
+        def add_by_turning(first, second):
+            h = ring.tile([P, 2 * STEP * PACK], BF16, name="h", align_bytes=64, bufs=4)
+            for w in (1, 0):
+                bank = psum1.tile([P, PACK, STEP], F32, name="rel_bank", tag="rel%d" % w)
+                for t in range(PACK):
+                    for term, product in enumerate((first, second)):
+                        nc.tensor.matmul(
+                            bank[:, t, :],
+                            product[:, w].rearrange("p n t -> p (n t)")[:, t * P:(t + 1) * P],
+                            identity[:],
+                            start=(term == 0),
+                            stop=(term == 1),
+                            is_transpose=True,
+                        )
+                nc.scalar.copy(
+                    out=h[:].rearrange("p (w n t) -> p w n t", w=2, t=PACK)[:, w], in_=bank[:].rearrange("p t n -> p n t")
+                )
+            return h
+
         out_view = out.rearrange("(a p) j -> p a j", p=P)
 
         def quantise_sum(h):
-            h_codes = ring.tile([P, 2 * STEP], U32, name="h_codes", align_bytes=64, bufs=4)
-            h_scales = ring.tile([P, 2 * STEP], U8, name="h_scales", align_bytes=64, bufs=4)
+            h_codes = ring.tile([P, 2 * STEP], U32, name="h_codes", align_bytes=64, bufs=5)
+            h_scales = ring.tile([P, 2 * STEP], U8, name="h_scales", align_bytes=64, bufs=5)
             nc.vector.quantize_mx(out=h_codes[:].bitcast(FP8X4), scales=h_scales[:], in_=h[:])
             return h_codes, h_scales
 
@@ -252,13 +300,14 @@ def tile_list_ckg_sig_kernel(
                         start=(w == 0),
                         stop=(w == 1),
                     )
-            result = ring.tile([P, len(blocks), STEP], F32, name="result")
+            result = ring.tile([P, len(blocks), STEP], F32, name="result", bufs=4)
             nc.scalar.activation(result[:], bank[:], SIGMOID)
             queue.dma_start(out=out_view[:, blocks[0]:blocks[-1] + 1, step * STEP:(step + 1) * STEP], in_=result[:])
 
         steps = J // STEP
-        rels = [project_relation(0), project_relation(1)]
+        rels = [project_relation(0)]
         ents = [project_entity(0)]
+        rels.append(project_relation(1))
         sums = []
         quantised = []
         for step in range(steps):
@@ -266,9 +315,9 @@ def tile_list_ckg_sig_kernel(
                 rels.append(project_relation(step + 2))
             if step + 1 < steps:
                 ents.append(project_entity(step + 1))
-            if step == 4:
-                score(0, *quantised[0])
             if step >= 4:
+                score(step - 4, *quantised[step - 4])
+            if step + 1 == steps:
                 score(step - 3, *quantised[step - 3])
             if step == 0:
                 cast_candidates(0, 0)
@@ -284,8 +333,9 @@ def tile_list_ckg_sig_kernel(
                 quantise_candidates(step - 2)
             if step in (5, 9):
                 gather(step // 4 + 1, 3)
+        sums.append(add_by_turning(first, second))
         score(steps - 3, *quantised[steps - 3])
         score(steps - 2, *quantise_sum(sums[steps - 2]))
-        last = quantise_sum(add_products(first, second, nc.vector))
+        last = quantise_sum(sums[steps - 1])
         score(steps - 1, *last, blocks=range(0, 2))
         score(steps - 1, *last, blocks=range(2, 4), queue=nc.scalar)

@@ -21,10 +21,25 @@ SIGMOID = mybir.ActivationFunctionType.Sigmoid
 P = 128
 PACK = 4
 K_PASS = P * PACK
+RUN = 8
+SCALE_ROWS = K_PASS // 32
+QUADRANT = 32
+LANES = 16
 CHUNK = 512
 STEP = 128
-LANES = 16
-TURNED = J // STEP - 1
+STEPS = J // STEP
+TURNED = STEPS - 1
+QUANTISE_LAG = 2
+SCORE_LAG = 4
+FIRST_CANDIDATE_STEP = 2
+
+WEIGHT_ROWS_AT = (0, 8, 16, 48)
+WR_RAW_SCALES_AT = 7.5
+ENT_SCALE_WIN_AT = 22
+REL_WORD_WIN_AT = 24
+WR_RAW_WORDS_AT = 32
+REL_SCALE_WIN_AT = 54
+ENT_PAIRS_AT = 56
 
 
 def tile_list_ckg_sig_kernel(
@@ -45,120 +60,125 @@ def tile_list_ckg_sig_kernel(
 
         ent_list = lists.tile([P, J // LANES], U16, name="ent_list")
         rel_list = lists.tile([P, J // LANES], U16, name="rel_list")
-        ent_scale_win = placed([P, T // 4], I32, "ent_scale_win", 22)
-        rel_scale_win = placed([P, T // 4], I32, "rel_scale_win", 54)
+        ent_scale_win = placed([P, T // 4], I32, "ent_scale_win", ENT_SCALE_WIN_AT)
+        rel_scale_win = placed([P, T // 4], I32, "rel_scale_win", REL_SCALE_WIN_AT)
         ent_word_win = keep.tile([P, T], I32, name="ent_word_win", align_bytes=64)
         ent_codes = keep.tile([P, 2, 2 * J], U8, name="ent_codes", align_bytes=64)
         scale_rows = keep.tile([P, 2, J], U8, name="scale_rows", align_bytes=64)
         planes = keep.tile([P, 3, J // 4], I32, name="planes", align_bytes=64)
-        rel_codes = [keep.tile([P, CHUNK], U32, name="rel_codes%d" % c, align_bytes=64) for c in range(4)]
-        wr_raw_words = placed([P, 2, R], I32, "wr_raw_words", 32)
-        wr_raw_scales = placed([16, 2, R // 4], I32, "wr_raw_scales", 7.5)
-        wr_scale_rows = keep.tile([16, 2, R // 4], I32, name="wr_scale_rows", align_bytes=64)
+        rel_codes = [keep.tile([P, CHUNK], U32, name="rel_codes%d" % c, align_bytes=64) for c in range(3)]
+        wr_raw_words = placed([P, 2, R], I32, "wr_raw_words", WR_RAW_WORDS_AT)
+        wr_raw_scales = placed([SCALE_ROWS, 2, R // 4], I32, "wr_raw_scales", WR_RAW_SCALES_AT)
+        wr_scale_rows = keep.tile([SCALE_ROWS, 2, R // 4], I32, name="wr_scale_rows", align_bytes=64)
         wr_codes = keep.tile([P, 2, R], I32, name="wr_codes", align_bytes=64)
         wr_scales = keep.tile([P, 2, R // 4], I32, name="wr_scales", align_bytes=64)
         we_codes = keep.tile([P, 4, R], U32, name="we_codes", align_bytes=64)
         we_scales = keep.tile([P, 4, R], U8, name="we_scales", align_bytes=64)
         n_scales = keep.tile([P, 2, N], U8, name="n_scales", align_bytes=64)
 
-        nc.vector.memset(rel_scale_win[:], 0)
+        nc.gpsimd.memset(rel_scale_win[:], 0)
         nc.vector.memset(ent_scale_win[32:64, :], 0)
         nc.vector.memset(ent_scale_win[64:P, :], 0)
-        warm = keep.tile([P, 2], F32, name="warm")
-        nc.vector.memset(wr_scales[:], 0)
-        nc.gpsimd.memset(warm[:, 0:1], 0.0)
-        nc.scalar.activation(warm[:, 1:2], warm[:, 0:1], SIGMOID)
-        nc.vector.memset(planes[:], 0)
-        identity = keep.tile([P, P], F32, name="identity")
-        make_identity(nc, identity[:])
+        nc.gpsimd.memset(wr_scales[:], 0)
+        nc.vector.memset(planes[:].rearrange("p a c -> p (a c)"), 0)
 
         def words_view(words):
             return words[0].rearrange("p n i -> p (n i)").bitcast(I32)
 
         def load_rows(src, piece):
-            raw = placed([P, PACK, R], F32, "raw%d" % piece, 8 * piece)
+            raw = placed([P, PACK, R], F32, "raw%d" % piece, WEIGHT_ROWS_AT[piece])
             nc.sync.dma_start(out=raw[:], in_=src.rearrange("(p j) c -> p j c", j=PACK))
             return raw
 
         def permute_relation_weight(w):
             nc.vector.tensor_copy(
-                out=wr_codes[:, w, :].rearrange("p (t b m) -> p t b m", t=4, m=8),
-                in_=wr_raw_words[:, w, :].rearrange("p (b t m) -> p t b m", t=4, m=8),
+                out=wr_codes[:, w, :].rearrange("p (t b m) -> p t b m", t=PACK, m=RUN),
+                in_=wr_raw_words[:, w, :].rearrange("p (b t m) -> p t b m", t=PACK, m=RUN),
             )
 
         for w, scales in enumerate((wrr_scales, wri_scales)):
             nc.sync.dma_start(out=wr_raw_scales[:, w, :], in_=scales[0].bitcast(I32))
         nc.sync.dma_start(ent_list[:], offs)
-        nc.sync.dma_start(out=ent_scale_win[0:32, :], in_=tab_scales.rearrange("a q t -> (a q) t").bitcast(I32))
+        nc.sync.dma_start(out=ent_scale_win[0:2 * SCALE_ROWS, :], in_=tab_scales.rearrange("a q t -> (a q) t").bitcast(I32))
         nc.sync.dma_start(rel_list[:], offs2)
         nc.sync.dma_start(out=ent_word_win[:], in_=words_view(tab_words))
         for w, words in enumerate((wrr_words, wri_words)):
             nc.sync.dma_start(out=wr_raw_words[:, w, :], in_=words_view(words))
-        nc.sync.dma_start(out=rel_scale_win[0:16, :], in_=tab2_scales[0].bitcast(I32))
+        nc.sync.dma_start(out=rel_scale_win[0:SCALE_ROWS, :], in_=tab2_scales[0].bitcast(I32))
 
         for w in range(2):
             nc.vector.tensor_copy(
-                out=wr_scale_rows[:, w, :].rearrange("p (t b m) -> p t b m", t=4, m=2),
-                in_=wr_raw_scales[:, w, :].rearrange("p (b t m) -> p t b m", t=4, m=2),
+                out=wr_scale_rows[:, w, :].rearrange("p (t b m) -> p t b m", t=PACK, m=RUN // 4),
+                in_=wr_raw_scales[:, w, :].rearrange("p (b t m) -> p t b m", t=PACK, m=RUN // 4),
             )
         we_raw = [load_rows(wer[0:K_PASS, :], 0), load_rows(wer[K_PASS:K, :], 1)]
         for row in range(4):
-            nc.sync.dma_start(out=wr_scales[row:P:32], in_=wr_scale_rows[row:16:4])
+            nc.sync.dma_start(out=wr_scales[row:P:QUADRANT], in_=wr_scale_rows[row:SCALE_ROWS:4])
         nc.vector.tensor_copy(scale_rows[:, 1, :], ent_scale_win[:].bitcast(U8).indirect(ent_list[:]))
-        we_raw += [load_rows(wei[0:K_PASS, :], 2), load_rows(wei[K_PASS:K, :], 3)]
+        we_raw.append(load_rows(wei[0:K_PASS, :], 2))
         permute_relation_weight(0)
         permute_relation_weight(1)
-        nc.vector.tensor_copy(scale_rows[:, 0, :], rel_scale_win[:].bitcast(U8).indirect(rel_list[:]))
-        rel_word_win = placed([P, T], I32, "rel_word_win", 40)
+        rel_word_win = placed([P, T], I32, "rel_word_win", REL_WORD_WIN_AT)
         nc.sync.dma_start(out=rel_word_win[:], in_=words_view(tab2_words))
-        ent_pairs = placed([P, J], U32, "ent_pairs", 56)
-        rows = scale_rows[:].bitcast(I32)
+        nc.vector.tensor_copy(scale_rows[:, 0, :], rel_scale_win[:].bitcast(U8).indirect(rel_list[:]))
+        we_raw.append(load_rows(wei[K_PASS:K, :], 3))
+        ent_pairs = placed([P, J], U32, "ent_pairs", ENT_PAIRS_AT)
+        gathered_rows = scale_rows[:].bitcast(I32)
         for row in range(4):
-            nc.sync.dma_start(out=planes[row:P:32, 0:2, :], in_=rows[row:16:4])
+            nc.sync.dma_start(out=planes[row:P:QUADRANT, 0:2, :], in_=gathered_rows[row:SCALE_ROWS:4])
         for row in range(4):
-            nc.sync.dma_start(out=planes[row:P:32, 2, :], in_=rows[16 + row:32:4, 1, :])
+            nc.sync.dma_start(
+                out=planes[row:P:QUADRANT, 2, :], in_=gathered_rows[SCALE_ROWS + row:2 * SCALE_ROWS:4, 1, :]
+            )
 
-        def gather(chunk, part):
-            cols = slice(chunk * CHUNK, (chunk + 1) * CHUNK)
+        def gather_entity(half):
+            cols = slice(half * J // 2, (half + 1) * J // 2)
+            entries = slice(half * J // 2 // LANES, (half + 1) * J // 2 // LANES)
+            nc.vector.tensor_copy(ent_pairs[:, cols], ent_word_win[:].bitcast(U32).indirect(ent_list[:, entries]))
+
+        def part_entity(half):
+            cols = slice(half * J // 2, (half + 1) * J // 2)
+            nc.vector.tensor_copy(
+                out=ent_codes[:].bitcast(U16)[:, :, cols],
+                in_=ent_pairs[:, cols].bitcast(U16).rearrange("p (n d) -> p d n", d=2),
+            )
+
+        def gather_relation(chunk):
             entries = slice(chunk * CHUNK // LANES, (chunk + 1) * CHUNK // LANES)
-            if part == 0:
-                nc.vector.tensor_copy(ent_pairs[:, cols], ent_word_win[:].bitcast(U32).indirect(ent_list[:, entries]))
-            elif part == 1:
-                nc.vector.tensor_copy(
-                    out=ent_codes[:].bitcast(U16)[:, :, cols],
-                    in_=ent_pairs[:, cols].bitcast(U16).rearrange("p (n d) -> p d n", d=2),
-                )
-            else:
-                nc.vector.tensor_copy(rel_codes[chunk][:], rel_word_win[:].bitcast(U32).indirect(rel_list[:, entries]))
+            nc.vector.tensor_copy(rel_codes[chunk][:], rel_word_win[:].bitcast(U32).indirect(rel_list[:, entries]))
 
         def quantise_entity_weight(piece):
-            grouped = ring.tile([P, PACK * R], BF16, name="grouped", align_bytes=64, bufs=4)
-            src = we_raw[piece][:].rearrange("p j (b t m) -> p t b m j", t=4, m=8)
-            dst = grouped[:].rearrange("p (t b m j) -> p t b m j", t=4, m=8, j=PACK)
-            for t in range(4):
+            grouped = keep.tile([P, PACK * R], BF16, name="grouped", tag="cast%d" % piece, align_bytes=64)
+            src = we_raw[piece][:].rearrange("p j (b t m) -> p t b m j", t=PACK, m=RUN)
+            dst = grouped[:].rearrange("p (t b m j) -> p t b m j", t=PACK, m=RUN, j=PACK)
+            for t in range(PACK):
                 nc.scalar.copy(out=dst[:, t], in_=src[:, t])
             nc.vector.quantize_mx(out=we_codes[:, piece, :].bitcast(FP8X4), scales=we_scales[:, piece, :], in_=grouped[:])
 
-        for chunk in range(4):
-            gather(chunk, 0)
-            gather(chunk, 1)
+        gather_entity(0)
+        gather_entity(1)
+        part_entity(0)
+        part_entity(1)
         quantise_entity_weight(0)
         quantise_entity_weight(1)
         quantise_entity_weight(2)
+        for chunk in range(3):
+            gather_relation(chunk)
         quantise_entity_weight(3)
-        gather(0, 3)
-        gather(1, 3)
+        rel_codes.append(keep.tile([P, CHUNK], U32, name="rel_codes3", tag="cast3", align_bytes=64))
+        gather_relation(3)
+        identity = placed([P, P], F32, "identity", REL_WORD_WIN_AT)
+        make_identity(nc, identity[:])
 
         n_raw = []
         for w, src in enumerate((nr, ni)):
-            raw = placed([P, PACK, N], F32, "n_raw%d" % w, 16 + 8 * w)
-            rows = src.rearrange("(b t m) n -> t b m n", t=4, m=8)
-            for t in range(4):
+            raw = placed([P, PACK, N], F32, "n_raw%d" % w, WEIGHT_ROWS_AT[2 + w])
+            rows = src.rearrange("(b t m) n -> t b m n", t=PACK, m=RUN)
+            for t in range(PACK):
                 nc.sync.dma_start(out=raw[:, t, :], in_=rows[t])
             n_raw.append(raw)
 
         n_grouped = keep.tile([P, 2, N * PACK], BF16, name="n_grouped", align_bytes=64)
-
         n_codes = []
 
         def cast_candidates(w, half):
@@ -179,10 +199,13 @@ def tile_list_ckg_sig_kernel(
 
         def project_relation(step):
             cols = slice(step * STEP, (step + 1) * STEP)
+            chunk, at = divmod(step * STEP, CHUNK)
+            codes = rel_codes[chunk][:, at:at + STEP].bitcast(FP8X4)
+            candidate = step - FIRST_CANDIDATE_STEP
             rel = [
                 ring.tile([P, STEP, PACK], F32, name="rel_re", bufs=4),
-                keep.tile([P, STEP, PACK], F32, name="rel_im", tag="cand%d" % (step - 2), align_bytes=64)
-                if step in (2, 3)
+                keep.tile([P, STEP, PACK], F32, name="rel_im", tag="cand%d" % candidate, align_bytes=64)
+                if candidate in (0, 1)
                 else ring.tile([P, STEP, PACK], F32, name="rel_im", bufs=4),
             ]
             for w in (step % 2, 1 - step % 2):
@@ -190,7 +213,7 @@ def tile_list_ckg_sig_kernel(
                 if step == TURNED:
                     nc.tensor.matmul_mx(
                         out=bank[:].rearrange("p t n -> p (t n)"),
-                        lhsT=rel_codes[step // 4][:, step % 4 * STEP:(step % 4 + 1) * STEP].bitcast(FP8X4),
+                        lhsT=codes,
                         lhsT_scale=rel_scales[:, cols],
                         rhs=wr_codes[:, w, :].bitcast(FP8X4),
                         rhs_scale=wr_planes[:, w, :],
@@ -199,12 +222,12 @@ def tile_list_ckg_sig_kernel(
                     )
                     nc.scalar.copy(out=rel[w][:].rearrange("p n t -> p (n t)"), in_=bank[:].rearrange("p t n -> p (t n)"))
                     continue
-                for t in range(4):
+                for t in range(PACK):
                     nc.tensor.matmul_mx(
                         out=bank[:, t, :],
                         lhsT=wr_codes[:, w, t * P:(t + 1) * P].bitcast(FP8X4),
                         lhsT_scale=wr_planes[:, w, t * P:(t + 1) * P],
-                        rhs=rel_codes[step // 4][:, step % 4 * STEP:(step % 4 + 1) * STEP].bitcast(FP8X4),
+                        rhs=codes,
                         rhs_scale=rel_scales[:, cols],
                         start=True,
                         stop=True,
@@ -214,6 +237,7 @@ def tile_list_ckg_sig_kernel(
 
         def project_entity(step):
             cols = slice(step * STEP, (step + 1) * STEP)
+            codes = [ent_codes[:, a, 2 * step * STEP:2 * (step + 1) * STEP].bitcast(FP4X4) for a in range(2)]
             ent = {}
             for w in (1, 0):
                 bank = psum2.tile([P, PACK, STEP], F32, name="ent_bank", tag="ent%d" % w)
@@ -221,7 +245,7 @@ def tile_list_ckg_sig_kernel(
                     for a in range(2):
                         nc.tensor.matmul_mx(
                             out=bank[:].rearrange("p t n -> p (t n)"),
-                            lhsT=ent_codes[:, a, 2 * step * STEP:2 * (step + 1) * STEP].bitcast(FP4X4),
+                            lhsT=codes[a],
                             lhsT_scale=ent_planes[:, a, cols],
                             rhs=we_codes[:, 2 * w + a, :].bitcast(FP8X4),
                             rhs_scale=we_scales[:, 2 * w + a, :],
@@ -230,13 +254,13 @@ def tile_list_ckg_sig_kernel(
                         )
                     ent[w] = bank[:].rearrange("p t n -> p (t n)").rearrange("p (n t) -> p n t", t=PACK)
                     continue
-                for t in range(4):
+                for t in range(PACK):
                     for a in range(2):
                         nc.tensor.matmul_mx(
                             out=bank[:, t, :],
                             lhsT=we_codes[:, 2 * w + a, t * P:(t + 1) * P].bitcast(FP8X4),
                             lhsT_scale=we_scales[:, 2 * w + a, t * P:(t + 1) * P],
-                            rhs=ent_codes[:, a, 2 * step * STEP:2 * (step + 1) * STEP].bitcast(FP4X4),
+                            rhs=codes[a],
                             rhs_scale=ent_planes[:, a, cols],
                             start=(a == 0),
                             stop=(a == 1),
@@ -253,15 +277,18 @@ def tile_list_ckg_sig_kernel(
             nc.vector.scalar_tensor_tensor(second[:, 0], ent[1], -1.0, rel[1][:], MULT, MULT)
             return first, second
 
-        def add_products(first, second, adder):
-            h = ring.tile([P, 2 * STEP * PACK], BF16, name="h", align_bytes=64, bufs=4)
-            adder.tensor_tensor(
+        def new_sums():
+            return ring.tile([P, 2 * STEP * PACK], BF16, name="h", align_bytes=64, bufs=QUANTISE_LAG + 2)
+
+        def add_products(first, second):
+            h = new_sums()
+            nc.gpsimd.tensor_tensor(
                 h[:], first[:].rearrange("p w n t -> p (w n t)"), second[:].rearrange("p w n t -> p (w n t)"), ADD
             )
             return h
 
         def add_by_turning(first, second):
-            h = ring.tile([P, 2 * STEP * PACK], BF16, name="h", align_bytes=64, bufs=4)
+            h = new_sums()
             for w in (1, 0):
                 bank = psum1.tile([P, PACK, STEP], F32, name="rel_bank", tag="rel%d" % w)
                 for t in range(PACK):
@@ -282,8 +309,8 @@ def tile_list_ckg_sig_kernel(
         out_view = out.rearrange("(a p) j -> p a j", p=P)
 
         def quantise_sum(h):
-            h_codes = ring.tile([P, 2 * STEP], U32, name="h_codes", align_bytes=64, bufs=5)
-            h_scales = ring.tile([P, 2 * STEP], U8, name="h_scales", align_bytes=64, bufs=5)
+            h_codes = ring.tile([P, 2 * STEP], U32, name="h_codes", align_bytes=64, bufs=SCORE_LAG + 1)
+            h_scales = ring.tile([P, 2 * STEP], U8, name="h_scales", align_bytes=64, bufs=SCORE_LAG + 1)
             nc.vector.quantize_mx(out=h_codes[:].bitcast(FP8X4), scales=h_scales[:], in_=h[:])
             return h_codes, h_scales
 
@@ -304,38 +331,35 @@ def tile_list_ckg_sig_kernel(
             nc.scalar.activation(result[:], bank[:], SIGMOID)
             queue.dma_start(out=out_view[:, blocks[0]:blocks[-1] + 1, step * STEP:(step + 1) * STEP], in_=result[:])
 
-        steps = J // STEP
         rels = [project_relation(0)]
         ents = [project_entity(0)]
         rels.append(project_relation(1))
         sums = []
         quantised = []
-        for step in range(steps):
-            if step + 2 < steps:
+        for step in range(STEPS):
+            if step + 2 < STEPS:
                 rels.append(project_relation(step + 2))
-            if step + 1 < steps:
+            if step + 1 < STEPS:
                 ents.append(project_entity(step + 1))
-            if step >= 4:
-                score(step - 4, *quantised[step - 4])
-            if step + 1 == steps:
-                score(step - 3, *quantised[step - 3])
+            if step >= SCORE_LAG:
+                score(step - SCORE_LAG, *quantised[step - SCORE_LAG])
+            if step == TURNED:
+                score(step - SCORE_LAG + 1, *quantised[step - SCORE_LAG + 1])
             if step == 0:
                 cast_candidates(0, 0)
                 cast_candidates(0, 1)
             if step in (1, 2):
                 cast_candidates(1, step - 1)
             first, second = multiply(ents[step], rels[step])
-            if step + 1 < steps:
-                sums.append(add_products(first, second, nc.gpsimd))
-            if step >= 2:
-                quantised.append(quantise_sum(sums[step - 2]))
-            if step in (2, 3):
-                quantise_candidates(step - 2)
-            if step in (5, 9):
-                gather(step // 4 + 1, 3)
+            if step != TURNED:
+                sums.append(add_products(first, second))
+            if step >= QUANTISE_LAG:
+                quantised.append(quantise_sum(sums[step - QUANTISE_LAG]))
+            if step - FIRST_CANDIDATE_STEP in (0, 1):
+                quantise_candidates(step - FIRST_CANDIDATE_STEP)
         sums.append(add_by_turning(first, second))
-        score(steps - 3, *quantised[steps - 3])
-        score(steps - 2, *quantise_sum(sums[steps - 2]))
-        last = quantise_sum(sums[steps - 1])
-        score(steps - 1, *last, blocks=range(0, 2))
-        score(steps - 1, *last, blocks=range(2, 4), queue=nc.scalar)
+        score(STEPS - 3, *quantised[STEPS - 3])
+        score(STEPS - 2, *quantise_sum(sums[STEPS - 2]))
+        last = quantise_sum(sums[STEPS - 1])
+        score(STEPS - 1, *last, blocks=range(0, 2))
+        score(STEPS - 1, *last, blocks=range(2, 4), queue=nc.scalar)

@@ -28,6 +28,7 @@ LANES = 16
 CHUNK = 512
 STEP = 128
 STEPS = J // STEP
+SOON = 6 * STEP
 TURNED = STEPS - 1
 QUANTISE_LAG = 2
 SCORE_LAG = 4
@@ -65,8 +66,8 @@ def tile_list_ckg_sig_kernel(
         ent_word_win = keep.tile([P, T], I32, name="ent_word_win", align_bytes=64)
         ent_codes = keep.tile([P, 2, 2 * J], U8, name="ent_codes", align_bytes=64)
         scale_rows = keep.tile([P, 2, J], U8, name="scale_rows", align_bytes=64)
-        planes = keep.tile([P, 3, J // 4], I32, name="planes", align_bytes=64)
-        rel_codes = [keep.tile([P, CHUNK], U32, name="rel_codes%d" % c, align_bytes=64) for c in range(3)]
+        planes = [keep.tile([P, 3, SOON // 4], I32, name="planes", align_bytes=64)]
+        rel_codes = [keep.tile([P, CHUNK], U32, name="rel_codes%d" % c, align_bytes=64) for c in range(4)]
         wr_raw_words = placed([P, 2, R], I32, "wr_raw_words", WR_RAW_WORDS_AT)
         wr_raw_scales = placed([SCALE_ROWS, 2, R // 4], I32, "wr_raw_scales", WR_RAW_SCALES_AT)
         wr_scale_rows = keep.tile([SCALE_ROWS, 2, R // 4], I32, name="wr_scale_rows", align_bytes=64)
@@ -80,7 +81,7 @@ def tile_list_ckg_sig_kernel(
         nc.vector.memset(ent_scale_win[32:64, :], 0)
         nc.vector.memset(ent_scale_win[64:P, :], 0)
         nc.gpsimd.memset(wr_scales[:], 0)
-        nc.vector.memset(planes[:].rearrange("p a c -> p (a c)"), 0)
+        nc.vector.memset(planes[0][:].rearrange("p a c -> p (a c)"), 0)
 
         def words_view(words):
             return words[0].rearrange("p n i -> p (n i)").bitcast(I32)
@@ -116,20 +117,28 @@ def tile_list_ckg_sig_kernel(
             nc.sync.dma_start(out=wr_scales[row:P:QUADRANT], in_=wr_scale_rows[row:SCALE_ROWS:4])
         nc.vector.tensor_copy(scale_rows[:, 1, :], ent_scale_win[:].bitcast(U8).indirect(ent_list[:]))
         we_raw.append(load_rows(wei[0:K_PASS, :], 2))
+        gathered_rows = scale_rows[:].bitcast(I32)
+
+        def move_last_plane(plane, words, rows=range(4)):
+            for row in rows:
+                nc.sync.dma_start(
+                    out=plane[row:P:QUADRANT, 2, :], in_=gathered_rows[SCALE_ROWS + row:2 * SCALE_ROWS:4, 1, words]
+                )
+
+        def move_first_planes(plane, words):
+            for row in range(4):
+                nc.sync.dma_start(out=plane[row:P:QUADRANT, 0:2, :], in_=gathered_rows[row:SCALE_ROWS:4, :, words])
+
         permute_relation_weight(0)
         permute_relation_weight(1)
         rel_word_win = placed([P, T], I32, "rel_word_win", REL_WORD_WIN_AT)
         nc.sync.dma_start(out=rel_word_win[:], in_=words_view(tab2_words))
         nc.vector.tensor_copy(scale_rows[:, 0, :], rel_scale_win[:].bitcast(U8).indirect(rel_list[:]))
+        move_last_plane(planes[0], slice(0, SOON // 4), range(1))
         we_raw.append(load_rows(wei[K_PASS:K, :], 3))
         ent_pairs = placed([P, J], U32, "ent_pairs", ENT_PAIRS_AT)
-        gathered_rows = scale_rows[:].bitcast(I32)
-        for row in range(4):
-            nc.sync.dma_start(out=planes[row:P:QUADRANT, 0:2, :], in_=gathered_rows[row:SCALE_ROWS:4])
-        for row in range(4):
-            nc.sync.dma_start(
-                out=planes[row:P:QUADRANT, 2, :], in_=gathered_rows[SCALE_ROWS + row:2 * SCALE_ROWS:4, 1, :]
-            )
+        move_first_planes(planes[0], slice(0, SOON // 4))
+        move_last_plane(planes[0], slice(0, SOON // 4), range(1, 4))
 
         def gather_entity(half):
             cols = slice(half * J // 2, (half + 1) * J // 2)
@@ -162,11 +171,9 @@ def tile_list_ckg_sig_kernel(
         quantise_entity_weight(0)
         quantise_entity_weight(1)
         quantise_entity_weight(2)
-        for chunk in range(3):
+        for chunk in range(4):
             gather_relation(chunk)
         quantise_entity_weight(3)
-        rel_codes.append(keep.tile([P, CHUNK], U32, name="rel_codes3", tag="cast3", align_bytes=64))
-        gather_relation(3)
         identity = placed([P, P], F32, "identity", REL_WORD_WIN_AT)
         make_identity(nc, identity[:])
 
@@ -177,6 +184,10 @@ def tile_list_ckg_sig_kernel(
             for t in range(PACK):
                 nc.sync.dma_start(out=raw[:, t, :], in_=rows[t])
             n_raw.append(raw)
+
+        planes.append(keep.tile([P, 3, (J - SOON) // 4], I32, name="later_planes", tag="cast3", align_bytes=64))
+        move_first_planes(planes[1], slice(SOON // 4, J // 4))
+        move_last_plane(planes[1], slice(SOON // 4, J // 4))
 
         n_grouped = keep.tile([P, 2, N * PACK], BF16, name="n_grouped", align_bytes=64)
         n_codes = []
@@ -193,12 +204,14 @@ def tile_list_ckg_sig_kernel(
             nc.vector.quantize_mx(out=codes[:].bitcast(FP8X4), scales=n_scales[:, w, :], in_=n_grouped[:, w, :])
             n_codes.append(codes)
 
-        rel_scales = planes[:].bitcast(U8)[:, 0, :]
-        ent_planes = planes[:].bitcast(U8)[:, 1:3, :]
+        def plane_of(step, which):
+            part = int(step * STEP >= SOON)
+            at = step * STEP - part * SOON
+            return planes[part][:].bitcast(U8)[:, which, at:at + STEP]
+
         wr_planes = wr_scales[:].bitcast(U8)
 
         def project_relation(step):
-            cols = slice(step * STEP, (step + 1) * STEP)
             chunk, at = divmod(step * STEP, CHUNK)
             codes = rel_codes[chunk][:, at:at + STEP].bitcast(FP8X4)
             candidate = step - FIRST_CANDIDATE_STEP
@@ -214,7 +227,7 @@ def tile_list_ckg_sig_kernel(
                     nc.tensor.matmul_mx(
                         out=bank[:].rearrange("p t n -> p (t n)"),
                         lhsT=codes,
-                        lhsT_scale=rel_scales[:, cols],
+                        lhsT_scale=plane_of(step, 0),
                         rhs=wr_codes[:, w, :].bitcast(FP8X4),
                         rhs_scale=wr_planes[:, w, :],
                         start=True,
@@ -228,7 +241,7 @@ def tile_list_ckg_sig_kernel(
                         lhsT=wr_codes[:, w, t * P:(t + 1) * P].bitcast(FP8X4),
                         lhsT_scale=wr_planes[:, w, t * P:(t + 1) * P],
                         rhs=codes,
-                        rhs_scale=rel_scales[:, cols],
+                        rhs_scale=plane_of(step, 0),
                         start=True,
                         stop=True,
                     )
@@ -236,17 +249,16 @@ def tile_list_ckg_sig_kernel(
             return rel
 
         def project_entity(step):
-            cols = slice(step * STEP, (step + 1) * STEP)
             codes = [ent_codes[:, a, 2 * step * STEP:2 * (step + 1) * STEP].bitcast(FP4X4) for a in range(2)]
             ent = {}
-            for w in (1, 0):
+            for w in (0, 1) if step == 0 else (1, 0):
                 bank = psum2.tile([P, PACK, STEP], F32, name="ent_bank", tag="ent%d" % w)
                 if step == TURNED:
                     for a in range(2):
                         nc.tensor.matmul_mx(
                             out=bank[:].rearrange("p t n -> p (t n)"),
                             lhsT=codes[a],
-                            lhsT_scale=ent_planes[:, a, cols],
+                            lhsT_scale=plane_of(step, 1 + a),
                             rhs=we_codes[:, 2 * w + a, :].bitcast(FP8X4),
                             rhs_scale=we_scales[:, 2 * w + a, :],
                             start=(a == 0),
@@ -261,19 +273,22 @@ def tile_list_ckg_sig_kernel(
                             lhsT=we_codes[:, 2 * w + a, t * P:(t + 1) * P].bitcast(FP8X4),
                             lhsT_scale=we_scales[:, 2 * w + a, t * P:(t + 1) * P],
                             rhs=codes[a],
-                            rhs_scale=ent_planes[:, a, cols],
+                            rhs_scale=plane_of(step, 1 + a),
                             start=(a == 0),
                             stop=(a == 1),
                         )
                 ent[w] = bank[:].rearrange("p t n -> p n t")
             return ent
 
-        def multiply(ent, rel):
+        def multiply(ent, rel, real_first):
             first = ring.tile([P, 2, STEP, PACK], F32, name="first")
             second = ring.tile([P, 2, STEP, PACK], F32, name="second")
             nc.vector.tensor_tensor(first[:, 0], ent[0], rel[0][:], MULT)
+            if real_first:
+                nc.vector.tensor_tensor(first[:, 1], ent[0], rel[1][:], MULT)
             nc.vector.tensor_tensor(second[:, 1], ent[1], rel[0][:], MULT)
-            nc.vector.tensor_tensor(first[:, 1], ent[0], rel[1][:], MULT)
+            if not real_first:
+                nc.vector.tensor_tensor(first[:, 1], ent[0], rel[1][:], MULT)
             nc.vector.scalar_tensor_tensor(second[:, 0], ent[1], -1.0, rel[1][:], MULT, MULT)
             return first, second
 
@@ -350,7 +365,7 @@ def tile_list_ckg_sig_kernel(
                 cast_candidates(0, 1)
             if step in (1, 2):
                 cast_candidates(1, step - 1)
-            first, second = multiply(ents[step], rels[step])
+            first, second = multiply(ents[step], rels[step], step == 0)
             if step != TURNED:
                 sums.append(add_products(first, second))
             if step >= QUANTISE_LAG:

@@ -28,7 +28,9 @@ LANES = 16
 CHUNK = 512
 STEP = 128
 STEPS = J // STEP
+SCORE_STEPS_ALONE = 4
 SOON = 6 * STEP
+PAIRED = STEPS - SCORE_STEPS_ALONE
 TURNED = STEPS - 1
 QUANTISE_LAG = 2
 SCORE_LAG = 4
@@ -86,13 +88,15 @@ def tile_list_ckg_sig_kernel(
         def words_view(words):
             return words[0].rearrange("p n i -> p (n i)").bitcast(I32)
 
-        def load_rows(src, piece):
+        def load_rows(src, piece, parts=1):
             raw = placed([P, PACK, R], F32, "raw%d" % piece, WEIGHT_ROWS_AT[piece])
-            nc.sync.dma_start(out=raw[:], in_=src.rearrange("(p j) c -> p j c", j=PACK))
+            for part in range(parts):
+                cols = slice(part * R // parts, (part + 1) * R // parts)
+                nc.sync.dma_start(out=raw[:, :, cols], in_=src.rearrange("(p j) c -> p j c", j=PACK)[:, :, cols])
             return raw
 
         def permute_relation_weight(w):
-            nc.vector.tensor_copy(
+            nc.gpsimd.tensor_copy(
                 out=wr_codes[:, w, :].rearrange("p (t b m) -> p t b m", t=PACK, m=RUN),
                 in_=wr_raw_words[:, w, :].rearrange("p (b t m) -> p t b m", t=PACK, m=RUN),
             )
@@ -135,7 +139,7 @@ def tile_list_ckg_sig_kernel(
         nc.sync.dma_start(out=rel_word_win[:], in_=words_view(tab2_words))
         nc.vector.tensor_copy(scale_rows[:, 0, :], rel_scale_win[:].bitcast(U8).indirect(rel_list[:]))
         move_last_plane(planes[0], slice(0, SOON // 4), range(1))
-        we_raw.append(load_rows(wei[K_PASS:K, :], 3))
+        we_raw.append(load_rows(wei[K_PASS:K, :], 3, parts=2))
         ent_pairs = placed([P, J], U32, "ent_pairs", ENT_PAIRS_AT)
         move_first_planes(planes[0], slice(0, SOON // 4))
         move_last_plane(planes[0], slice(0, SOON // 4), range(1, 4))
@@ -156,12 +160,14 @@ def tile_list_ckg_sig_kernel(
             entries = slice(chunk * CHUNK // LANES, (chunk + 1) * CHUNK // LANES)
             nc.vector.tensor_copy(rel_codes[chunk][:], rel_word_win[:].bitcast(U32).indirect(rel_list[:, entries]))
 
-        def quantise_entity_weight(piece):
+        def quantise_entity_weight(piece, parts=1):
             grouped = keep.tile([P, PACK * R], BF16, name="grouped", tag="cast%d" % piece, align_bytes=64)
             src = we_raw[piece][:].rearrange("p j (b t m) -> p t b m j", t=PACK, m=RUN)
             dst = grouped[:].rearrange("p (t b m j) -> p t b m j", t=PACK, m=RUN, j=PACK)
-            for t in range(PACK):
-                nc.scalar.copy(out=dst[:, t], in_=src[:, t])
+            for part in range(parts):
+                blocks = slice(part * SCALE_ROWS // parts, (part + 1) * SCALE_ROWS // parts)
+                for t in range(PACK):
+                    nc.scalar.copy(out=dst[:, t, blocks], in_=src[:, t, blocks])
             nc.vector.quantize_mx(out=we_codes[:, piece, :].bitcast(FP8X4), scales=we_scales[:, piece, :], in_=grouped[:])
 
         gather_entity(0)
@@ -173,7 +179,7 @@ def tile_list_ckg_sig_kernel(
         quantise_entity_weight(2)
         for chunk in range(4):
             gather_relation(chunk)
-        quantise_entity_weight(3)
+        quantise_entity_weight(3, parts=2)
         identity = placed([P, P], F32, "identity", REL_WORD_WIN_AT)
         make_identity(nc, identity[:])
 
@@ -324,10 +330,42 @@ def tile_list_ckg_sig_kernel(
         out_view = out.rearrange("(a p) j -> p a j", p=P)
 
         def quantise_sum(h):
-            h_codes = ring.tile([P, 2 * STEP], U32, name="h_codes", align_bytes=64, bufs=SCORE_LAG + 1)
-            h_scales = ring.tile([P, 2 * STEP], U8, name="h_scales", align_bytes=64, bufs=SCORE_LAG + 1)
+            h_codes = ring.tile([P, 2 * STEP], U32, name="h_codes", align_bytes=64, bufs=4)
+            h_scales = ring.tile([P, 2 * STEP], U8, name="h_scales", align_bytes=64, bufs=4)
             nc.vector.quantize_mx(out=h_codes[:].bitcast(FP8X4), scales=h_scales[:], in_=h[:])
             return h_codes, h_scales
+
+        def quantise_into_pair(h, pair, half):
+            cols = slice(half * STEP, (half + 1) * STEP)
+            for w in range(2):
+                nc.vector.quantize_mx(
+                    out=pair[0][:, w, cols].bitcast(FP8X4),
+                    scales=pair[1][:, w, cols],
+                    in_=h[:, w * STEP * PACK:(w + 1) * STEP * PACK],
+                )
+
+        def new_pair():
+            codes = ring.tile([P, 2, 2 * STEP], U32, name="pair_codes", align_bytes=64)
+            scales = ring.tile([P, 2, 2 * STEP], U8, name="pair_scales", align_bytes=64)
+            return codes, scales
+
+        def score_pair(index, pair, blocks):
+            bank = psum2.tile([P, len(blocks), 2 * STEP], F32, name="score_bank", tag="score")
+            for at, a in enumerate(blocks):
+                for w in range(2):
+                    nc.tensor.matmul_mx(
+                        out=bank[:, at, :],
+                        lhsT=n_codes[w][:, a * P:(a + 1) * P].bitcast(FP8X4),
+                        lhsT_scale=n_scales[:, w, a * P:(a + 1) * P],
+                        rhs=pair[0][:, w, :].bitcast(FP8X4),
+                        rhs_scale=pair[1][:, w, :],
+                        start=(w == 0),
+                        stop=(w == 1),
+                    )
+            result = ring.tile([P, len(blocks), 2 * STEP], F32, name="result", bufs=4)
+            nc.scalar.activation(result[:], bank[:], SIGMOID)
+            cols = slice(2 * index * STEP, 2 * (index + 1) * STEP)
+            nc.sync.dma_start(out=out_view[:, blocks[0]:blocks[-1] + 1, cols], in_=result[:])
 
         def score(step, h_codes, h_scales, blocks=range(N // P), queue=nc.sync):
             bank = psum2.tile([P, len(blocks), STEP], F32, name="score_bank", tag="score")
@@ -350,16 +388,18 @@ def tile_list_ckg_sig_kernel(
         ents = [project_entity(0)]
         rels.append(project_relation(1))
         sums = []
-        quantised = []
+        pairs = []
+        quantised = {}
         for step in range(STEPS):
             if step + 2 < STEPS:
                 rels.append(project_relation(step + 2))
             if step + 1 < STEPS:
                 ents.append(project_entity(step + 1))
             if step >= SCORE_LAG:
-                score(step - SCORE_LAG, *quantised[step - SCORE_LAG])
+                index, half = divmod(step - SCORE_LAG, 2)
+                score_pair(index, pairs[index], range(2 * half, 2 * half + 2))
             if step == TURNED:
-                score(step - SCORE_LAG + 1, *quantised[step - SCORE_LAG + 1])
+                score(PAIRED, *quantised[PAIRED])
             if step == 0:
                 cast_candidates(0, 0)
                 cast_candidates(0, 1)
@@ -368,8 +408,13 @@ def tile_list_ckg_sig_kernel(
             first, second = multiply(ents[step], rels[step], step == 0)
             if step != TURNED:
                 sums.append(add_products(first, second))
-            if step >= QUANTISE_LAG:
-                quantised.append(quantise_sum(sums[step - QUANTISE_LAG]))
+            due = step - QUANTISE_LAG
+            if due >= PAIRED:
+                quantised[due] = quantise_sum(sums[due])
+            elif due >= 0:
+                if due % 2 == 0:
+                    pairs.append(new_pair())
+                quantise_into_pair(sums[due], pairs[-1], due % 2)
             if step - FIRST_CANDIDATE_STEP in (0, 1):
                 quantise_candidates(step - FIRST_CANDIDATE_STEP)
         sums.append(add_by_turning(first, second))

@@ -36,13 +36,14 @@ QUANTISE_LAG = 2
 SCORE_LAG = 4
 FIRST_CANDIDATE_STEP = 2
 
-WEIGHT_ROWS_AT = (0, 8, 16, 48)
+WEIGHT_ROWS_AT = (0, 8, 16, 51)
 WR_RAW_SCALES_AT = 7.5
-ENT_SCALE_WIN_AT = 22
-REL_WORD_WIN_AT = 24
-WR_RAW_WORDS_AT = 32
-REL_SCALE_WIN_AT = 54
-ENT_PAIRS_AT = 56
+ENT_SCALE_WIN_AT = 23.5
+SOON_PLANES_AT = 24
+REL_WORD_WIN_AT = 27
+WR_RAW_WORDS_AT = 35
+REL_SCALE_WIN_AT = 57
+ENT_PAIRS_AT = 59
 
 
 def tile_list_ckg_sig_kernel(
@@ -68,7 +69,6 @@ def tile_list_ckg_sig_kernel(
         ent_word_win = keep.tile([P, T], I32, name="ent_word_win", align_bytes=64)
         ent_codes = keep.tile([P, 2, 2 * J], U8, name="ent_codes", align_bytes=64)
         scale_rows = keep.tile([P, 2, J], U8, name="scale_rows", align_bytes=64)
-        planes = [keep.tile([P, 3, SOON // 4], I32, name="planes", align_bytes=64)]
         rel_codes = [keep.tile([P, CHUNK], U32, name="rel_codes%d" % c, align_bytes=64) for c in range(4)]
         wr_raw_words = placed([P, 2, R], I32, "wr_raw_words", WR_RAW_WORDS_AT)
         wr_raw_scales = placed([SCALE_ROWS, 2, R // 4], I32, "wr_raw_scales", WR_RAW_SCALES_AT)
@@ -83,7 +83,6 @@ def tile_list_ckg_sig_kernel(
         nc.vector.memset(ent_scale_win[32:64, :], 0)
         nc.vector.memset(ent_scale_win[64:P, :], 0)
         nc.gpsimd.memset(wr_scales[:], 0)
-        nc.vector.memset(planes[0][:].rearrange("p a c -> p (a c)"), 0)
 
         def words_view(words):
             return words[0].rearrange("p n i -> p (n i)").bitcast(I32)
@@ -101,10 +100,10 @@ def tile_list_ckg_sig_kernel(
                 in_=wr_raw_words[:, w, :].rearrange("p (b t m) -> p t b m", t=PACK, m=RUN),
             )
 
-        for w, scales in enumerate((wrr_scales, wri_scales)):
-            nc.sync.dma_start(out=wr_raw_scales[:, w, :], in_=scales[0].bitcast(I32))
         nc.sync.dma_start(ent_list[:], offs)
         nc.sync.dma_start(out=ent_scale_win[0:2 * SCALE_ROWS, :], in_=tab_scales.rearrange("a q t -> (a q) t").bitcast(I32))
+        for w, scales in enumerate((wrr_scales, wri_scales)):
+            nc.sync.dma_start(out=wr_raw_scales[:, w, :], in_=scales[0].bitcast(I32))
         nc.sync.dma_start(rel_list[:], offs2)
         nc.sync.dma_start(out=ent_word_win[:], in_=words_view(tab_words))
         for w, words in enumerate((wrr_words, wri_words)):
@@ -112,7 +111,7 @@ def tile_list_ckg_sig_kernel(
         nc.sync.dma_start(out=rel_scale_win[0:SCALE_ROWS, :], in_=tab2_scales[0].bitcast(I32))
 
         for w in range(2):
-            nc.vector.tensor_copy(
+            nc.gpsimd.tensor_copy(
                 out=wr_scale_rows[:, w, :].rearrange("p (t b m) -> p t b m", t=PACK, m=RUN // 4),
                 in_=wr_raw_scales[:, w, :].rearrange("p (b t m) -> p t b m", t=PACK, m=RUN // 4),
             )
@@ -122,6 +121,7 @@ def tile_list_ckg_sig_kernel(
         nc.vector.tensor_copy(scale_rows[:, 1, :], ent_scale_win[:].bitcast(U8).indirect(ent_list[:]))
         we_raw.append(load_rows(wei[0:K_PASS, :], 2))
         gathered_rows = scale_rows[:].bitcast(I32)
+        planes = [placed([P, 3, SOON // 4], I32, "planes", SOON_PLANES_AT)]
 
         def move_last_plane(plane, words, rows=range(4)):
             for row in rows:
@@ -221,12 +221,10 @@ def tile_list_ckg_sig_kernel(
             chunk, at = divmod(step * STEP, CHUNK)
             codes = rel_codes[chunk][:, at:at + STEP].bitcast(FP8X4)
             candidate = step - FIRST_CANDIDATE_STEP
-            rel = [
-                ring.tile([P, STEP, PACK], F32, name="rel_re", bufs=4),
-                keep.tile([P, STEP, PACK], F32, name="rel_im", tag="cand%d" % candidate, align_bytes=64)
-                if candidate in (0, 1)
-                else ring.tile([P, STEP, PACK], F32, name="rel_im", bufs=4),
-            ]
+            if candidate in (0, 1):
+                both = keep.tile([P, 2, STEP, PACK], F32, name="rel", tag="cand%d" % candidate, align_bytes=64)
+            else:
+                both = ring.tile([P, 2, STEP, PACK], F32, name="rel", bufs=4)
             for w in (step % 2, 1 - step % 2):
                 bank = psum1.tile([P, PACK, STEP], F32, name="rel_bank", tag="rel%d" % w)
                 if step == TURNED:
@@ -239,7 +237,7 @@ def tile_list_ckg_sig_kernel(
                         start=True,
                         stop=True,
                     )
-                    nc.scalar.copy(out=rel[w][:].rearrange("p n t -> p (n t)"), in_=bank[:].rearrange("p t n -> p (t n)"))
+                    nc.scalar.copy(out=both[:, w].rearrange("p n t -> p (n t)"), in_=bank[:].rearrange("p t n -> p (t n)"))
                     continue
                 for t in range(PACK):
                     nc.tensor.matmul_mx(
@@ -251,8 +249,8 @@ def tile_list_ckg_sig_kernel(
                         start=True,
                         stop=True,
                     )
-                nc.scalar.copy(out=rel[w][:], in_=bank[:].rearrange("p t n -> p n t"))
-            return rel
+                nc.scalar.copy(out=both[:, w], in_=bank[:].rearrange("p t n -> p n t"))
+            return both
 
         def project_entity(step):
             codes = [ent_codes[:, a, 2 * step * STEP:2 * (step + 1) * STEP].bitcast(FP4X4) for a in range(2)]
@@ -286,16 +284,20 @@ def tile_list_ckg_sig_kernel(
                 ent[w] = bank[:].rearrange("p t n -> p n t")
             return ent
 
-        def multiply(ent, rel, real_first):
+        def multiply(ent, rel, order):
             first = ring.tile([P, 2, STEP, PACK], F32, name="first")
             second = ring.tile([P, 2, STEP, PACK], F32, name="second")
-            nc.vector.tensor_tensor(first[:, 0], ent[0], rel[0][:], MULT)
-            if real_first:
-                nc.vector.tensor_tensor(first[:, 1], ent[0], rel[1][:], MULT)
-            nc.vector.tensor_tensor(second[:, 1], ent[1], rel[0][:], MULT)
-            if not real_first:
-                nc.vector.tensor_tensor(first[:, 1], ent[0], rel[1][:], MULT)
-            nc.vector.scalar_tensor_tensor(second[:, 0], ent[1], -1.0, rel[1][:], MULT, MULT)
+            for product in order:
+                if product == "aer both":
+                    nc.vector.tensor_tensor(first[:], ent[0].unsqueeze(1).to_broadcast([P, 2, STEP, PACK]), rel[:], MULT)
+                elif product == "aer arr":
+                    nc.vector.tensor_tensor(first[:, 0], ent[0], rel[:, 0], MULT)
+                elif product == "aer ari":
+                    nc.vector.tensor_tensor(first[:, 1], ent[0], rel[:, 1], MULT)
+                elif product == "aei arr":
+                    nc.vector.tensor_tensor(second[:, 1], ent[1], rel[:, 0], MULT)
+                else:
+                    nc.vector.scalar_tensor_tensor(second[:, 0], ent[1], -1.0, rel[:, 1], MULT, MULT)
             return first, second
 
         def new_sums():
@@ -322,7 +324,7 @@ def tile_list_ckg_sig_kernel(
                             stop=(term == 1),
                             is_transpose=True,
                         )
-                nc.scalar.copy(
+                (nc.scalar.copy if w == 1 else nc.vector.tensor_copy)(
                     out=h[:].rearrange("p (w n t) -> p w n t", w=2, t=PACK)[:, w], in_=bank[:].rearrange("p t n -> p n t")
                 )
             return h
@@ -362,7 +364,7 @@ def tile_list_ckg_sig_kernel(
                         start=(w == 0),
                         stop=(w == 1),
                     )
-            result = ring.tile([P, len(blocks), 2 * STEP], F32, name="result", bufs=4)
+            result = ring.tile([P, len(blocks), 2 * STEP], F32, name="result", bufs=6)
             nc.scalar.activation(result[:], bank[:], SIGMOID)
             cols = slice(2 * index * STEP, 2 * (index + 1) * STEP)
             nc.sync.dma_start(out=out_view[:, blocks[0]:blocks[-1] + 1, cols], in_=result[:])
@@ -380,9 +382,40 @@ def tile_list_ckg_sig_kernel(
                         start=(w == 0),
                         stop=(w == 1),
                     )
-            result = ring.tile([P, len(blocks), STEP], F32, name="result", bufs=4)
+            result = ring.tile([P, len(blocks), STEP], F32, name="result", bufs=6)
             nc.scalar.activation(result[:], bank[:], SIGMOID)
             queue.dma_start(out=out_view[:, blocks[0]:blocks[-1] + 1, step * STEP:(step + 1) * STEP], in_=result[:])
+
+        def score_last(h):
+            h_codes = ring.tile([P, 2 * STEP], U32, name="h_codes", align_bytes=64, bufs=4)
+            h_scales = ring.tile([P, 2 * STEP], U8, name="h_scales", align_bytes=64, bufs=4)
+            shares = (range(0, 2), range(2, 3), range(3, 4))
+            banks = [
+                psum2.tile([P, len(blocks), STEP], F32, name="last_bank", tag=tag)
+                for blocks, tag in zip(shares, ("ent0", "ent1", "score"))
+            ]
+            for w in (1, 0):
+                cols = slice(w * STEP, (w + 1) * STEP)
+                nc.vector.quantize_mx(
+                    out=h_codes[:, cols].bitcast(FP8X4),
+                    scales=h_scales[:, cols],
+                    in_=h[:, w * STEP * PACK:(w + 1) * STEP * PACK],
+                )
+                for blocks, bank in zip(shares, banks):
+                    for at, a in enumerate(blocks):
+                        nc.tensor.matmul_mx(
+                            out=bank[:, at, :],
+                            lhsT=n_codes[w][:, a * P:(a + 1) * P].bitcast(FP8X4),
+                            lhsT_scale=n_scales[:, w, a * P:(a + 1) * P],
+                            rhs=h_codes[:, cols].bitcast(FP8X4),
+                            rhs_scale=h_scales[:, cols],
+                            start=(w == 1 and at == 0),
+                            stop=(w == 0 and at == len(blocks) - 1),
+                        )
+            for blocks, bank, queue in zip(shares, banks, (nc.sync, nc.sync, nc.scalar)):
+                result = keep.tile([P, len(blocks), STEP], F32, name="last_result%d" % blocks[0])
+                nc.scalar.activation(result[:], bank[:], SIGMOID)
+                queue.dma_start(out=out_view[:, blocks[0]:blocks[-1] + 1, J - STEP:J], in_=result[:])
 
         rels = [project_relation(0)]
         ents = [project_entity(0)]
@@ -405,7 +438,13 @@ def tile_list_ckg_sig_kernel(
                 cast_candidates(0, 1)
             if step in (1, 2):
                 cast_candidates(1, step - 1)
-            first, second = multiply(ents[step], rels[step], step == 0)
+            if step == 0:
+                order = ("aer arr", "aer ari", "aei arr", "aei ari")
+            elif step == TURNED:
+                order = ("aer ari", "aei arr", "aer arr", "aei ari")
+            else:
+                order = ("aer both", "aei arr", "aei ari")
+            first, second = multiply(ents[step], rels[step], order)
             if step != TURNED:
                 sums.append(add_products(first, second))
             due = step - QUANTISE_LAG
@@ -417,9 +456,7 @@ def tile_list_ckg_sig_kernel(
                 quantise_into_pair(sums[due], pairs[-1], due % 2)
             if step - FIRST_CANDIDATE_STEP in (0, 1):
                 quantise_candidates(step - FIRST_CANDIDATE_STEP)
-        sums.append(add_by_turning(first, second))
+        last_sums = add_by_turning(first, second)
         score(STEPS - 3, *quantised[STEPS - 3])
         score(STEPS - 2, *quantise_sum(sums[STEPS - 2]))
-        last = quantise_sum(sums[STEPS - 1])
-        score(STEPS - 1, *last, blocks=range(0, 2))
-        score(STEPS - 1, *last, blocks=range(2, 4), queue=nc.scalar)
+        score_last(last_sums)

@@ -29,7 +29,7 @@ CHUNK = 512
 STEP = 128
 STEPS = J // STEP
 SCORE_STEPS_ALONE = 4
-SOON = 6 * STEP
+SOON = 8 * STEP
 PAIRED = STEPS - SCORE_STEPS_ALONE
 TURNED = STEPS - 1
 QUANTISE_LAG = 2
@@ -195,19 +195,19 @@ def tile_list_ckg_sig_kernel(
         move_first_planes(planes[1], slice(SOON // 4, J // 4))
         move_last_plane(planes[1], slice(SOON // 4, J // 4))
 
-        n_grouped = keep.tile([P, 2, N * PACK], BF16, name="n_grouped", align_bytes=64)
+        n_grouped = [keep.tile([P, N * PACK], BF16, name="nr_grouped", align_bytes=64)]
         n_codes = []
 
         def cast_candidates(w, half):
             cols = slice(half * N // 2, (half + 1) * N // 2)
             nc.scalar.copy(
-                out=n_grouped[:, w, :].rearrange("p (n t) -> p n t", t=PACK)[:, cols, :],
+                out=n_grouped[w][:].rearrange("p (n t) -> p n t", t=PACK)[:, cols, :],
                 in_=n_raw[w][:].rearrange("p t n -> p n t")[:, cols, :],
             )
 
         def quantise_candidates(w):
             codes = keep.tile([P, N], U32, name="n_codes", tag="cand%d" % w, align_bytes=64)
-            nc.vector.quantize_mx(out=codes[:].bitcast(FP8X4), scales=n_scales[:, w, :], in_=n_grouped[:, w, :])
+            nc.vector.quantize_mx(out=codes[:].bitcast(FP8X4), scales=n_scales[:, w, :], in_=n_grouped[w][:])
             n_codes.append(codes)
 
         def plane_of(step, which):
@@ -223,6 +223,8 @@ def tile_list_ckg_sig_kernel(
             candidate = step - FIRST_CANDIDATE_STEP
             if candidate in (0, 1):
                 both = keep.tile([P, 2, STEP, PACK], F32, name="rel", tag="cand%d" % candidate, align_bytes=64)
+            elif step == 1:
+                both = keep.tile([P, 2, STEP, PACK], F32, name="rel", tag="ni_grouped", align_bytes=64)
             else:
                 both = ring.tile([P, 2, STEP, PACK], F32, name="rel", bufs=4)
             for w in (step % 2, 1 - step % 2):
@@ -433,11 +435,12 @@ def tile_list_ckg_sig_kernel(
                 score_pair(index, pairs[index], range(2 * half, 2 * half + 2))
             if step == TURNED:
                 score(PAIRED, *quantised[PAIRED])
-            if step == 0:
-                cast_candidates(0, 0)
-                cast_candidates(0, 1)
-            if step in (1, 2):
-                cast_candidates(1, step - 1)
+            if step in (0, 1):
+                cast_candidates(0, step)
+            if step == 2:
+                n_grouped.append(keep.tile([P, N * PACK], BF16, name="ni_grouped", align_bytes=64))
+                cast_candidates(1, 0)
+                cast_candidates(1, 1)
             if step == 0:
                 order = ("aer arr", "aer ari", "aei arr", "aei ari")
             elif step == TURNED:

@@ -44,6 +44,8 @@ REL_WORD_WIN_AT = 27
 WR_RAW_WORDS_AT = 35
 REL_SCALE_WIN_AT = 57
 ENT_PAIRS_AT = 59
+LAST_CAST_AT = 67
+LATER_PLANES_AT = 69
 
 
 def tile_list_ckg_sig_kernel(
@@ -69,7 +71,7 @@ def tile_list_ckg_sig_kernel(
         ent_word_win = keep.tile([P, T], I32, name="ent_word_win", align_bytes=64)
         ent_codes = keep.tile([P, 2, 2 * J], U8, name="ent_codes", align_bytes=64)
         scale_rows = keep.tile([P, 2, J], U8, name="scale_rows", align_bytes=64)
-        rel_codes = [keep.tile([P, CHUNK], U32, name="rel_codes%d" % c, align_bytes=64) for c in range(4)]
+        rel_codes = [keep.tile([P, CHUNK], U32, name="rel_codes%d" % c, align_bytes=64) for c in range(3)]
         wr_raw_words = placed([P, 2, R], I32, "wr_raw_words", WR_RAW_WORDS_AT)
         wr_raw_scales = placed([SCALE_ROWS, 2, R // 4], I32, "wr_raw_scales", WR_RAW_SCALES_AT)
         wr_scale_rows = keep.tile([SCALE_ROWS, 2, R // 4], I32, name="wr_scale_rows", align_bytes=64)
@@ -83,6 +85,9 @@ def tile_list_ckg_sig_kernel(
         nc.vector.memset(ent_scale_win[32:64, :], 0)
         nc.vector.memset(ent_scale_win[64:P, :], 0)
         nc.gpsimd.memset(wr_scales[:], 0)
+
+        identity = keep.tile([P, P], F32, name="identity")
+        make_identity(nc, identity[:])
 
         def words_view(words):
             return words[0].rearrange("p n i -> p (n i)").bitcast(I32)
@@ -161,7 +166,10 @@ def tile_list_ckg_sig_kernel(
             nc.vector.tensor_copy(rel_codes[chunk][:], rel_word_win[:].bitcast(U32).indirect(rel_list[:, entries]))
 
         def quantise_entity_weight(piece, parts=1):
-            grouped = keep.tile([P, PACK * R], BF16, name="grouped", tag="cast%d" % piece, align_bytes=64)
+            if piece == 3:
+                grouped = placed([P, PACK * R], BF16, "last_cast", LAST_CAST_AT)
+            else:
+                grouped = keep.tile([P, PACK * R], BF16, name="cast%d" % piece, align_bytes=64)
             src = we_raw[piece][:].rearrange("p j (b t m) -> p t b m j", t=PACK, m=RUN)
             dst = grouped[:].rearrange("p (t b m j) -> p t b m j", t=PACK, m=RUN, j=PACK)
             for part in range(parts):
@@ -177,11 +185,11 @@ def tile_list_ckg_sig_kernel(
         quantise_entity_weight(0)
         quantise_entity_weight(1)
         quantise_entity_weight(2)
-        for chunk in range(4):
+        for chunk in range(3):
             gather_relation(chunk)
         quantise_entity_weight(3, parts=2)
-        identity = placed([P, P], F32, "identity", REL_WORD_WIN_AT)
-        make_identity(nc, identity[:])
+        rel_codes.append(placed([P, CHUNK], U32, "rel_codes3", LAST_CAST_AT))
+        gather_relation(3)
 
         n_raw = []
         for w, src in enumerate((nr, ni)):
@@ -191,11 +199,11 @@ def tile_list_ckg_sig_kernel(
                 nc.sync.dma_start(out=raw[:, t, :], in_=rows[t])
             n_raw.append(raw)
 
-        planes.append(keep.tile([P, 3, (J - SOON) // 4], I32, name="later_planes", tag="cast3", align_bytes=64))
+        planes.append(placed([P, 3, (J - SOON) // 4], I32, "later_planes", LATER_PLANES_AT))
         move_first_planes(planes[1], slice(SOON // 4, J // 4))
         move_last_plane(planes[1], slice(SOON // 4, J // 4))
 
-        n_grouped = [keep.tile([P, N * PACK], BF16, name="nr_grouped", align_bytes=64)]
+        n_grouped = []
         n_codes = []
 
         def cast_candidates(w, half):
@@ -223,8 +231,8 @@ def tile_list_ckg_sig_kernel(
             candidate = step - FIRST_CANDIDATE_STEP
             if candidate in (0, 1):
                 both = keep.tile([P, 2, STEP, PACK], F32, name="rel", tag="cand%d" % candidate, align_bytes=64)
-            elif step == 1:
-                both = keep.tile([P, 2, STEP, PACK], F32, name="rel", tag="ni_grouped", align_bytes=64)
+            elif step in (0, 1):
+                both = keep.tile([P, 2, STEP, PACK], F32, name="rel", tag="n_grouped%d" % step, align_bytes=64)
             else:
                 both = ring.tile([P, 2, STEP, PACK], F32, name="rel", bufs=4)
             for w in (step % 2, 1 - step % 2):
@@ -435,12 +443,10 @@ def tile_list_ckg_sig_kernel(
                 score_pair(index, pairs[index], range(2 * half, 2 * half + 2))
             if step == TURNED:
                 score(PAIRED, *quantised[PAIRED])
-            if step in (0, 1):
-                cast_candidates(0, step)
-            if step == 2:
-                n_grouped.append(keep.tile([P, N * PACK], BF16, name="ni_grouped", align_bytes=64))
-                cast_candidates(1, 0)
-                cast_candidates(1, 1)
+            if step in (1, 2):
+                n_grouped.append(keep.tile([P, N * PACK], BF16, name="n_grouped%d" % (step - 1), align_bytes=64))
+                cast_candidates(step - 1, 0)
+                cast_candidates(step - 1, 1)
             if step == 0:
                 order = ("aer arr", "aer ari", "aei arr", "aei ari")
             elif step == TURNED:

@@ -43,7 +43,7 @@ SOON_PLANES_AT = 24
 REL_WORD_WIN_AT = 27
 WR_RAW_WORDS_AT = 35
 REL_SCALE_WIN_AT = 57
-ENT_PAIRS_AT = 59
+ENT_CODES_AT = 59
 LAST_CAST_AT = 67
 LATER_PLANES_AT = 69
 
@@ -69,7 +69,7 @@ def tile_list_ckg_sig_kernel(
         ent_scale_win = placed([P, T // 4], I32, "ent_scale_win", ENT_SCALE_WIN_AT)
         rel_scale_win = placed([P, T // 4], I32, "rel_scale_win", REL_SCALE_WIN_AT)
         ent_word_win = keep.tile([P, T], I32, name="ent_word_win", align_bytes=64)
-        ent_codes = keep.tile([P, 2, 2 * J], U8, name="ent_codes", align_bytes=64)
+        ent_pairs = keep.tile([P, J], U32, name="ent_pairs", align_bytes=64)
         scale_rows = keep.tile([P, 2, J], U8, name="scale_rows", align_bytes=64)
         rel_codes = [keep.tile([P, CHUNK], U32, name="rel_codes%d" % c, align_bytes=64) for c in range(3)]
         wr_raw_words = placed([P, 2, R], I32, "wr_raw_words", WR_RAW_WORDS_AT)
@@ -142,12 +142,6 @@ def tile_list_ckg_sig_kernel(
         permute_relation_weight(1)
         rel_word_win = placed([P, T], I32, "rel_word_win", REL_WORD_WIN_AT)
         nc.sync.dma_start(out=rel_word_win[:], in_=words_view(tab2_words))
-        nc.vector.tensor_copy(scale_rows[:, 0, :], rel_scale_win[:].bitcast(U8).indirect(rel_list[:]))
-        move_last_plane(planes[0], slice(0, SOON // 4), range(1))
-        we_raw.append(load_rows(wei[K_PASS:K, :], 3, parts=2))
-        ent_pairs = placed([P, J], U32, "ent_pairs", ENT_PAIRS_AT)
-        move_first_planes(planes[0], slice(0, SOON // 4))
-        move_last_plane(planes[0], slice(0, SOON // 4), range(1, 4))
 
         def gather_entity(half):
             cols = slice(half * J // 2, (half + 1) * J // 2)
@@ -180,6 +174,12 @@ def tile_list_ckg_sig_kernel(
 
         gather_entity(0)
         gather_entity(1)
+        nc.vector.tensor_copy(scale_rows[:, 0, :], rel_scale_win[:].bitcast(U8).indirect(rel_list[:]))
+        move_last_plane(planes[0], slice(0, SOON // 4), range(1))
+        we_raw.append(load_rows(wei[K_PASS:K, :], 3, parts=2))
+        move_first_planes(planes[0], slice(0, SOON // 4))
+        move_last_plane(planes[0], slice(0, SOON // 4), range(1, 4))
+        ent_codes = placed([P, 2, 2 * J], U8, "ent_codes", ENT_CODES_AT)
         part_entity(0)
         part_entity(1)
         quantise_entity_weight(0)

@@ -100,9 +100,9 @@ def tile_list_ckg_sig_kernel(
             return raw
 
         def permute_relation_weight(w):
-            nc.gpsimd.tensor_copy(
-                out=wr_codes[:, w, :].rearrange("p (t b m) -> p t b m", t=PACK, m=RUN),
-                in_=wr_raw_words[:, w, :].rearrange("p (b t m) -> p t b m", t=PACK, m=RUN),
+            nc.scalar.copy(
+                out=wr_codes[:].bitcast(U32)[:, w, :].rearrange("p (t b m) -> p t b m", t=PACK, m=RUN),
+                in_=wr_raw_words[:].bitcast(U32)[:, w, :].rearrange("p (b t m) -> p t b m", t=PACK, m=RUN),
             )
 
         nc.sync.dma_start(ent_list[:], offs)
@@ -116,9 +116,9 @@ def tile_list_ckg_sig_kernel(
         nc.sync.dma_start(out=rel_scale_win[0:SCALE_ROWS, :], in_=tab2_scales[0].bitcast(I32))
 
         for w in range(2):
-            nc.gpsimd.tensor_copy(
-                out=wr_scale_rows[:, w, :].rearrange("p (t b m) -> p t b m", t=PACK, m=RUN // 4),
-                in_=wr_raw_scales[:, w, :].rearrange("p (b t m) -> p t b m", t=PACK, m=RUN // 4),
+            nc.scalar.copy(
+                out=wr_scale_rows[:].bitcast(U32)[:, w, :].rearrange("p (t b m) -> p t b m", t=PACK, m=RUN // 4),
+                in_=wr_raw_scales[:].bitcast(U32)[:, w, :].rearrange("p (b t m) -> p t b m", t=PACK, m=RUN // 4),
             )
         we_raw = [load_rows(wer[0:K_PASS, :], 0), load_rows(wer[K_PASS:K, :], 1)]
         for row in range(4):

@@ -306,8 +306,14 @@ def tile_list_ckg_sig_kernel(
                     nc.vector.tensor_tensor(first[:, 1], ent[0], rel[:, 1], MULT)
                 elif product == "aei arr":
                     nc.vector.tensor_tensor(second[:, 1], ent[1], rel[:, 0], MULT)
-                else:
+                elif product == "aei ari":
                     nc.vector.scalar_tensor_tensor(second[:, 0], ent[1], -1.0, rel[:, 1], MULT, MULT)
+                else:
+                    for half in range(2):
+                        part = slice(half * STEP // 2, (half + 1) * STEP // 2)
+                        nc.vector.scalar_tensor_tensor(
+                            second[:, 0, part], ent[1][:, part], -1.0, rel[:, 1, part], MULT, MULT
+                        )
             return first, second
 
         def new_sums():
@@ -324,14 +330,14 @@ def tile_list_ckg_sig_kernel(
             h = new_sums()
             for w in (1, 0):
                 bank = psum1.tile([P, PACK, STEP], F32, name="rel_bank", tag="rel%d" % w)
-                for t in range(PACK):
-                    for term, product in enumerate((first, second)):
+                for term, product in enumerate((first, second)):
+                    for t in range(PACK):
                         nc.tensor.matmul(
                             bank[:, t, :],
                             product[:, w].rearrange("p n t -> p (n t)")[:, t * P:(t + 1) * P],
                             identity[:],
-                            start=(term == 0),
-                            stop=(term == 1),
+                            start=(term == 0 and t == 0),
+                            stop=(term == 1 and t == PACK - 1),
                             is_transpose=True,
                         )
                 (nc.scalar.copy if w == 1 else nc.vector.tensor_copy)(
@@ -450,7 +456,7 @@ def tile_list_ckg_sig_kernel(
             if step == 0:
                 order = ("aer arr", "aer ari", "aei arr", "aei ari")
             elif step == TURNED:
-                order = ("aer ari", "aei arr", "aer arr", "aei ari")
+                order = ("aer ari", "aei arr", "aer arr", "aei ari in halves")
             else:
                 order = ("aer both", "aei arr", "aei ari")
             first, second = multiply(ents[step], rels[step], order)

@@ -143,18 +143,6 @@ def tile_list_ckg_sig_kernel(
         rel_word_win = placed([P, T], I32, "rel_word_win", REL_WORD_WIN_AT)
         nc.sync.dma_start(out=rel_word_win[:], in_=words_view(tab2_words))
 
-        def gather_entity(half):
-            cols = slice(half * J // 2, (half + 1) * J // 2)
-            entries = slice(half * J // 2 // LANES, (half + 1) * J // 2 // LANES)
-            nc.vector.tensor_copy(ent_pairs[:, cols], ent_word_win[:].bitcast(U32).indirect(ent_list[:, entries]))
-
-        def part_entity(half):
-            cols = slice(half * J // 2, (half + 1) * J // 2)
-            nc.vector.tensor_copy(
-                out=ent_codes[:].bitcast(U16)[:, :, cols],
-                in_=ent_pairs[:, cols].bitcast(U16).rearrange("p (n d) -> p d n", d=2),
-            )
-
         def gather_relation(chunk):
             entries = slice(chunk * CHUNK // LANES, (chunk + 1) * CHUNK // LANES)
             nc.vector.tensor_copy(rel_codes[chunk][:], rel_word_win[:].bitcast(U32).indirect(rel_list[:, entries]))
@@ -172,16 +160,16 @@ def tile_list_ckg_sig_kernel(
                     nc.scalar.copy(out=dst[:, t, blocks], in_=src[:, t, blocks])
             nc.vector.quantize_mx(out=we_codes[:, piece, :].bitcast(FP8X4), scales=we_scales[:, piece, :], in_=grouped[:])
 
-        gather_entity(0)
-        gather_entity(1)
+        nc.vector.tensor_copy(ent_pairs[:], ent_word_win[:].bitcast(U32).indirect(ent_list[:]))
         nc.vector.tensor_copy(scale_rows[:, 0, :], rel_scale_win[:].bitcast(U8).indirect(rel_list[:]))
         move_last_plane(planes[0], slice(0, SOON // 4), range(1))
         we_raw.append(load_rows(wei[K_PASS:K, :], 3, parts=2))
         move_first_planes(planes[0], slice(0, SOON // 4))
         move_last_plane(planes[0], slice(0, SOON // 4), range(1, 4))
         ent_codes = placed([P, 2, 2 * J], U8, "ent_codes", ENT_CODES_AT)
-        part_entity(0)
-        part_entity(1)
+        nc.vector.tensor_copy(
+            out=ent_codes[:].bitcast(U16), in_=ent_pairs[:].bitcast(U16).rearrange("p (n d) -> p d n", d=2)
+        )
         quantise_entity_weight(0)
         quantise_entity_weight(1)
         quantise_entity_weight(2)
@@ -309,8 +297,7 @@ def tile_list_ckg_sig_kernel(
                 elif product == "aei ari":
                     nc.vector.scalar_tensor_tensor(second[:, 0], ent[1], -1.0, rel[:, 1], MULT, MULT)
                 else:
-                    for half in range(2):
-                        part = slice(half * STEP // 2, (half + 1) * STEP // 2)
+                    for part in (slice(0, 3 * STEP // 4), slice(3 * STEP // 4, STEP)):
                         nc.vector.scalar_tensor_tensor(
                             second[:, 0, part], ent[1][:, part], -1.0, rel[:, 1, part], MULT, MULT
                         )
@@ -350,7 +337,13 @@ def tile_list_ckg_sig_kernel(
         def quantise_sum(h):
             h_codes = ring.tile([P, 2 * STEP], U32, name="h_codes", align_bytes=64, bufs=4)
             h_scales = ring.tile([P, 2 * STEP], U8, name="h_scales", align_bytes=64, bufs=4)
-            nc.vector.quantize_mx(out=h_codes[:].bitcast(FP8X4), scales=h_scales[:], in_=h[:])
+            for w in range(2):
+                cols = slice(w * STEP, (w + 1) * STEP)
+                nc.vector.quantize_mx(
+                    out=h_codes[:, cols].bitcast(FP8X4),
+                    scales=h_scales[:, cols],
+                    in_=h[:, w * STEP * PACK:(w + 1) * STEP * PACK],
+                )
             return h_codes, h_scales
 
         def quantise_into_pair(h, pair, half):
@@ -407,8 +400,8 @@ def tile_list_ckg_sig_kernel(
             h_scales = ring.tile([P, 2 * STEP], U8, name="h_scales", align_bytes=64, bufs=4)
             shares = (range(0, 2), range(2, 3), range(3, 4))
             banks = [
-                psum2.tile([P, len(blocks), STEP], F32, name="last_bank", tag=tag)
-                for blocks, tag in zip(shares, ("ent0", "ent1", "score"))
+                pool.tile([P, len(blocks), STEP], F32, name="last_bank", tag=tag)
+                for blocks, pool, tag in zip(shares, (psum2, psum2, psum1), ("ent0", "ent1", "rel1"))
             ]
             for w in (1, 0):
                 cols = slice(w * STEP, (w + 1) * STEP)

@@ -28,24 +28,41 @@ LANES = 16
 CHUNK = 512
 STEP = 128
 STEPS = J // STEP
-SCORE_STEPS_ALONE = 4
-SOON = 8 * STEP
-PAIRED = STEPS - SCORE_STEPS_ALONE
-TURNED = STEPS - 1
+SOON = 4 * STEP
+SPREAD = 0
+LAST = STEPS - 1
+ROUNDS = STEPS - 1
+PAIRED = 10
+PIECES = 16
+FIRST_PIECE_ROUND = 2
+PIECE_ROUNDS = 9
+EARLY_PIECES = 3
 QUANTISE_LAG = 2
 SCORE_LAG = 4
-FIRST_CANDIDATE_STEP = 2
+FIRST_CANDIDATE_ROUND = 2
 
-WEIGHT_ROWS_AT = (0, 8, 16, 51)
-WR_RAW_SCALES_AT = 7.5
-ENT_SCALE_WIN_AT = 23.5
-SOON_PLANES_AT = 24
-REL_WORD_WIN_AT = 27
-WR_RAW_WORDS_AT = 35
-REL_SCALE_WIN_AT = 57
-ENT_CODES_AT = 59
-LAST_CAST_AT = 67
-LATER_PLANES_AT = 69
+WEIGHT_ROWS_AT = (0, 32, 40, 49)
+ENT_PAIRS_AT = 8
+ENT_WORD_WIN_AT = 16
+FIRST_AT = 8
+SECOND_AT = 20
+WR_RAW_SCALES_AT = 31.5
+WR_RAW_WORDS_AT = 46.5
+SOON_PLANES_AT = 48
+LATER_PLANES_AT = 4
+N_GROUPED_AT = (53, 0)
+HELD_STEP = 7
+LAST_CAST_AT = 138
+AHEAD = 7
+REL_WORD_WIN_AT = 57
+LAST_RESULTS_AT = 61
+SECOND_CAST_AT = 73
+ENT_CODES_AT = 73
+ENT_SCALE_WIN_AT = 81
+REL_SCALE_WIN_AT = 85
+SPREAD_REL_AT = 89
+REL_AT = 94
+REL_CODES_AT = (85, 87)
 
 
 def tile_list_ckg_sig_kernel(
@@ -59,19 +76,34 @@ def tile_list_ckg_sig_kernel(
         ring = ctx.enter_context(tc.tile_pool(name="ring", bufs=3))
         arena = ctx.enter_context(tc.tile_pool(name="arena", bufs=1))
         psum2 = ctx.enter_context(tc.psum_pool(name="psum2", bufs=2))
+        psum3 = ctx.enter_context(tc.psum_pool(name="psum3", bufs=3))
         psum1 = ctx.enter_context(tc.psum_pool(name="psum1", bufs=1))
 
         def placed(shape, dtype, name, kib):
             return arena.tile(shape, dtype, name=name, tag=name, offset=int(kib * 1024), align_bytes=64)
 
+        def rel_at(step):
+            if step == SPREAD:
+                return SPREAD_REL_AT
+            if step == HELD_STEP:
+                return LAST_CAST_AT + 2
+            if step == LAST:
+                return REL_AT
+            if step > AHEAD:
+                return rel_at(step - AHEAD) + 3
+            return REL_AT + 7 * (step - 1)
+
         ent_list = lists.tile([P, J // LANES], U16, name="ent_list")
         rel_list = lists.tile([P, J // LANES], U16, name="rel_list")
         ent_scale_win = placed([P, T // 4], I32, "ent_scale_win", ENT_SCALE_WIN_AT)
         rel_scale_win = placed([P, T // 4], I32, "rel_scale_win", REL_SCALE_WIN_AT)
-        ent_word_win = keep.tile([P, T], I32, name="ent_word_win", align_bytes=64)
-        ent_pairs = keep.tile([P, J], U32, name="ent_pairs", align_bytes=64)
-        scale_rows = keep.tile([P, 2, J], U8, name="scale_rows", align_bytes=64)
-        rel_codes = [keep.tile([P, CHUNK], U32, name="rel_codes%d" % c, align_bytes=64) for c in range(3)]
+        rel_word_win = placed([P, T], I32, "rel_word_win", REL_WORD_WIN_AT)
+        ent_rows = keep.tile([P, J], U8, name="ent_rows", align_bytes=64)
+        rel_planes = [
+            keep.tile([P, CHUNK], U8, name="rel_plane0", align_bytes=64),
+            keep.tile([P, J - CHUNK], U8, name="rel_plane1", align_bytes=64),
+        ]
+        rel_codes = [keep.tile([P, CHUNK], U32, name="rel_codes0", align_bytes=64)]
         wr_raw_words = placed([P, 2, R], I32, "wr_raw_words", WR_RAW_WORDS_AT)
         wr_raw_scales = placed([SCALE_ROWS, 2, R // 4], I32, "wr_raw_scales", WR_RAW_SCALES_AT)
         wr_scale_rows = keep.tile([SCALE_ROWS, 2, R // 4], I32, name="wr_scale_rows", align_bytes=64)
@@ -99,56 +131,57 @@ def tile_list_ckg_sig_kernel(
                 nc.sync.dma_start(out=raw[:, :, cols], in_=src.rearrange("(p j) c -> p j c", j=PACK)[:, :, cols])
             return raw
 
-        def permute_relation_weight(w):
-            nc.scalar.copy(
-                out=wr_codes[:].bitcast(U32)[:, w, :].rearrange("p (t b m) -> p t b m", t=PACK, m=RUN),
-                in_=wr_raw_words[:].bitcast(U32)[:, w, :].rearrange("p (b t m) -> p t b m", t=PACK, m=RUN),
-            )
-
         nc.sync.dma_start(ent_list[:], offs)
-        nc.sync.dma_start(out=ent_scale_win[0:2 * SCALE_ROWS, :], in_=tab_scales.rearrange("a q t -> (a q) t").bitcast(I32))
+        nc.sync.dma_start(out=ent_scale_win[0:2 * SCALE_ROWS, :], in_=tab_scales.bitcast(I32).rearrange("a q t -> q a t"))
+        nc.sync.dma_start(rel_list[:], offs2)
         for w, scales in enumerate((wrr_scales, wri_scales)):
             nc.sync.dma_start(out=wr_raw_scales[:, w, :], in_=scales[0].bitcast(I32))
-        nc.sync.dma_start(rel_list[:], offs2)
-        nc.sync.dma_start(out=ent_word_win[:], in_=words_view(tab_words))
+        nc.sync.dma_start(out=rel_word_win[:], in_=words_view(tab2_words))
+        for quad in range(4):
+            nc.sync.dma_start(
+                out=rel_scale_win[QUADRANT * quad:QUADRANT * quad + 4, :], in_=tab2_scales[0].bitcast(I32)[4 * quad:4 * quad + 4]
+            )
         for w, words in enumerate((wrr_words, wri_words)):
             nc.sync.dma_start(out=wr_raw_words[:, w, :], in_=words_view(words))
-        nc.sync.dma_start(out=rel_scale_win[0:SCALE_ROWS, :], in_=tab2_scales[0].bitcast(I32))
-
+        we_raw = [load_rows(wer[0:K_PASS, :], 0)]
         for w in range(2):
             nc.scalar.copy(
                 out=wr_scale_rows[:].bitcast(U32)[:, w, :].rearrange("p (t b m) -> p t b m", t=PACK, m=RUN // 4),
                 in_=wr_raw_scales[:].bitcast(U32)[:, w, :].rearrange("p (b t m) -> p t b m", t=PACK, m=RUN // 4),
             )
-        we_raw = [load_rows(wer[0:K_PASS, :], 0), load_rows(wer[K_PASS:K, :], 1)]
         for row in range(4):
-            nc.sync.dma_start(out=wr_scales[row:P:QUADRANT], in_=wr_scale_rows[row:SCALE_ROWS:4])
-        nc.vector.tensor_copy(scale_rows[:, 1, :], ent_scale_win[:].bitcast(U8).indirect(ent_list[:]))
-        we_raw.append(load_rows(wei[0:K_PASS, :], 2))
-        gathered_rows = scale_rows[:].bitcast(I32)
-        planes = [placed([P, 3, SOON // 4], I32, "planes", SOON_PLANES_AT)]
+            nc.scalar.dma_start(out=wr_scales[row:P:QUADRANT], in_=wr_scale_rows[row:SCALE_ROWS:4])
+        ent_word_win = placed([P, T], I32, "ent_word_win", ENT_WORD_WIN_AT)
+        nc.sync.dma_start(out=ent_word_win[:], in_=words_view(tab_words))
+        we_raw.append(load_rows(wer[K_PASS:K, :], 1))
+        for w in range(2):
+            nc.scalar.copy(
+                out=wr_codes[:].bitcast(U32)[:, w, :].rearrange("p (t b m) -> p t b m", t=PACK, m=RUN),
+                in_=wr_raw_words[:].bitcast(U32)[:, w, :].rearrange("p (b t m) -> p t b m", t=PACK, m=RUN),
+            )
 
-        def move_last_plane(plane, words, rows=range(4)):
-            for row in rows:
+        nc.vector.tensor_copy(ent_rows[:], ent_scale_win[:].bitcast(U8).indirect(ent_list[:]))
+
+        def move_planes(name, kib, words):
+            plane = placed([P, 2, words.stop - words.start], I32, name, kib)
+            for quad in range(4):
                 nc.sync.dma_start(
-                    out=plane[row:P:QUADRANT, 2, :], in_=gathered_rows[SCALE_ROWS + row:2 * SCALE_ROWS:4, 1, words]
+                    out=plane[QUADRANT * quad:QUADRANT * quad + 4], in_=ent_rows[:].bitcast(I32)[8 * quad:8 * quad + 8, words]
                 )
+            return plane
 
-        def move_first_planes(plane, words):
-            for row in range(4):
-                nc.sync.dma_start(out=plane[row:P:QUADRANT, 0:2, :], in_=gathered_rows[row:SCALE_ROWS:4, :, words])
-
-        permute_relation_weight(0)
-        permute_relation_weight(1)
-        rel_word_win = placed([P, T], I32, "rel_word_win", REL_WORD_WIN_AT)
-        nc.sync.dma_start(out=rel_word_win[:], in_=words_view(tab2_words))
+        we_raw.append(load_rows(wei[0:K_PASS, :], 2))
+        ent_planes = [move_planes("soon_planes", SOON_PLANES_AT, slice(0, SOON // 4))]
+        we_raw.append(load_rows(wei[K_PASS:K, :], 3, parts=2))
 
         def gather_relation(chunk):
             entries = slice(chunk * CHUNK // LANES, (chunk + 1) * CHUNK // LANES)
             nc.vector.tensor_copy(rel_codes[chunk][:], rel_word_win[:].bitcast(U32).indirect(rel_list[:, entries]))
 
         def quantise_entity_weight(piece, parts=1):
-            if piece == 3:
+            if piece == 1:
+                grouped = placed([P, PACK * R], BF16, "second_cast", SECOND_CAST_AT)
+            elif piece == 3:
                 grouped = placed([P, PACK * R], BF16, "last_cast", LAST_CAST_AT)
             else:
                 grouped = keep.tile([P, PACK * R], BF16, name="cast%d" % piece, align_bytes=64)
@@ -157,85 +190,95 @@ def tile_list_ckg_sig_kernel(
             for part in range(parts):
                 blocks = slice(part * SCALE_ROWS // parts, (part + 1) * SCALE_ROWS // parts)
                 for t in range(PACK):
-                    nc.scalar.copy(out=dst[:, t, blocks], in_=src[:, t, blocks])
+                    if piece < 2:
+                        nc.gpsimd.tensor_scalar(dst[:, t, blocks], src[:, t, blocks], 1.0, 0.0, MULT, ADD)
+                    else:
+                        nc.scalar.copy(out=dst[:, t, blocks], in_=src[:, t, blocks])
             nc.vector.quantize_mx(out=we_codes[:, piece, :].bitcast(FP8X4), scales=we_scales[:, piece, :], in_=grouped[:])
 
-        nc.vector.tensor_copy(ent_pairs[:], ent_word_win[:].bitcast(U32).indirect(ent_list[:]))
-        nc.vector.tensor_copy(scale_rows[:, 0, :], rel_scale_win[:].bitcast(U8).indirect(rel_list[:]))
-        move_last_plane(planes[0], slice(0, SOON // 4), range(1))
-        we_raw.append(load_rows(wei[K_PASS:K, :], 3, parts=2))
-        move_first_planes(planes[0], slice(0, SOON // 4))
-        move_last_plane(planes[0], slice(0, SOON // 4), range(1, 4))
-        ent_codes = placed([P, 2, 2 * J], U8, "ent_codes", ENT_CODES_AT)
-        nc.vector.tensor_copy(
-            out=ent_codes[:].bitcast(U16), in_=ent_pairs[:].bitcast(U16).rearrange("p (n d) -> p d n", d=2)
-        )
-        quantise_entity_weight(0)
-        quantise_entity_weight(1)
-        quantise_entity_weight(2)
-        for chunk in range(3):
+        nc.vector.tensor_copy(rel_planes[0][:], rel_scale_win[:].bitcast(U8).indirect(rel_list[:, 0:CHUNK // LANES]))
+        gather_relation(0)
+        nc.vector.tensor_copy(rel_planes[1][:], rel_scale_win[:].bitcast(U8).indirect(rel_list[:, CHUNK // LANES:J // LANES]))
+        for chunk in (1, 2):
+            rel_codes.append(placed([P, CHUNK], U32, "rel_codes%d" % chunk, REL_CODES_AT[chunk - 1]))
             gather_relation(chunk)
+        quantise_entity_weight(0)
+        ent_pairs = placed([P, J], U32, "ent_pairs", ENT_PAIRS_AT)
+        nc.vector.tensor_copy(ent_pairs[:], ent_word_win[:].bitcast(U32).indirect(ent_list[:]))
+        quantise_entity_weight(1)
+        ent_codes = []
+        for name, lo, hi in (("soon_codes", 0, SOON), ("later_codes", SOON, J)):
+            codes = placed([P, 2, 2 * (hi - lo)], U8, name, ENT_CODES_AT + lo / 256)
+            nc.vector.tensor_copy(
+                out=codes[:].bitcast(U16), in_=ent_pairs[:, lo:hi].bitcast(U16).rearrange("p (n d) -> p d n", d=2)
+            )
+            ent_codes.append(codes)
+        quantise_entity_weight(2)
         quantise_entity_weight(3, parts=2)
-        rel_codes.append(placed([P, CHUNK], U32, "rel_codes3", LAST_CAST_AT))
+        rel_codes.append(placed([P, CHUNK], U32, "rel_codes3", LAST_CAST_AT - 1.5))
         gather_relation(3)
 
+        ent_planes.append(move_planes("later_planes", LATER_PLANES_AT, slice(SOON // 4, J // 4)))
         n_raw = []
         for w, src in enumerate((nr, ni)):
-            raw = placed([P, PACK, N], F32, "n_raw%d" % w, WEIGHT_ROWS_AT[2 + w])
+            raw = placed([P, PACK, N], F32, "n_raw%d" % w, WEIGHT_ROWS_AT[1 + w])
             rows = src.rearrange("(b t m) n -> t b m n", t=PACK, m=RUN)
             for t in range(PACK):
                 nc.sync.dma_start(out=raw[:, t, :], in_=rows[t])
             n_raw.append(raw)
 
-        planes.append(placed([P, 3, (J - SOON) // 4], I32, "later_planes", LATER_PLANES_AT))
-        move_first_planes(planes[1], slice(SOON // 4, J // 4))
-        move_last_plane(planes[1], slice(SOON // 4, J // 4))
-
         n_grouped = []
         n_codes = []
 
-        def cast_candidates(w, half):
-            cols = slice(half * N // 2, (half + 1) * N // 2)
-            nc.scalar.copy(
-                out=n_grouped[w][:].rearrange("p (n t) -> p n t", t=PACK)[:, cols, :],
-                in_=n_raw[w][:].rearrange("p t n -> p n t")[:, cols, :],
-            )
+        def cast_candidates(w):
+            grouped = placed([P, N * PACK], BF16, "n_grouped%d" % w, N_GROUPED_AT[w])
+            for half in range(2):
+                cols = slice(half * N // 2, (half + 1) * N // 2)
+                nc.scalar.copy(
+                    out=grouped[:].rearrange("p (n t) -> p n t", t=PACK)[:, cols, :],
+                    in_=n_raw[w][:].rearrange("p t n -> p n t")[:, cols, :],
+                )
+            n_grouped.append(grouped)
 
         def quantise_candidates(w):
-            codes = keep.tile([P, N], U32, name="n_codes", tag="cand%d" % w, align_bytes=64)
+            codes = placed([P, N], U32, "n_codes%d" % w, rel_at(FIRST_CANDIDATE_ROUND + w + 1) + 1)
             nc.vector.quantize_mx(out=codes[:].bitcast(FP8X4), scales=n_scales[:, w, :], in_=n_grouped[w][:])
             n_codes.append(codes)
 
-        def plane_of(step, which):
-            part = int(step * STEP >= SOON)
-            at = step * STEP - part * SOON
-            return planes[part][:].bitcast(U8)[:, which, at:at + STEP]
+        def part_of(parts, first, step):
+            part = int(step * STEP >= first)
+            at = step * STEP - part * first
+            return parts[part][:].bitcast(U8), slice(at, at + STEP)
 
         wr_planes = wr_scales[:].bitcast(U8)
+
+        def flat(bank):
+            return bank[:].rearrange("p t n -> p (t n)")
 
         def project_relation(step):
             chunk, at = divmod(step * STEP, CHUNK)
             codes = rel_codes[chunk][:, at:at + STEP].bitcast(FP8X4)
-            candidate = step - FIRST_CANDIDATE_STEP
-            if candidate in (0, 1):
-                both = keep.tile([P, 2, STEP, PACK], F32, name="rel", tag="cand%d" % candidate, align_bytes=64)
-            elif step in (0, 1):
-                both = keep.tile([P, 2, STEP, PACK], F32, name="rel", tag="n_grouped%d" % step, align_bytes=64)
-            else:
-                both = ring.tile([P, 2, STEP, PACK], F32, name="rel", bufs=4)
-            for w in (step % 2, 1 - step % 2):
-                bank = psum1.tile([P, PACK, STEP], F32, name="rel_bank", tag="rel%d" % w)
-                if step == TURNED:
+            planes, cols = part_of(rel_planes, CHUNK, step)
+            plane = planes[:, cols]
+            both = placed([P, 2, STEP, PACK], F32, "rel%d" % step, rel_at(step))
+            for w in range(2):
+                if step >= HELD_STEP:
+                    bank = psum1.tile([P, PACK, STEP], F32, name="rel_bank", tag="rel%d" % w)
+                elif w == 0:
+                    bank = psum3.tile([P, PACK, STEP], F32, name="rel_bank", tag="ent")
+                else:
+                    bank = psum2.tile([P, PACK, STEP], F32, name="rel_bank", tag="score")
+                if step in (SPREAD, LAST):
                     nc.tensor.matmul_mx(
-                        out=bank[:].rearrange("p t n -> p (t n)"),
+                        out=flat(bank),
                         lhsT=codes,
-                        lhsT_scale=plane_of(step, 0),
+                        lhsT_scale=plane,
                         rhs=wr_codes[:, w, :].bitcast(FP8X4),
                         rhs_scale=wr_planes[:, w, :],
                         start=True,
                         stop=True,
                     )
-                    nc.scalar.copy(out=both[:, w].rearrange("p n t -> p (n t)"), in_=bank[:].rearrange("p t n -> p (t n)"))
+                    nc.scalar.copy(out=both[:, w].rearrange("p n t -> p (n t)"), in_=flat(bank))
                     continue
                 for t in range(PACK):
                     nc.tensor.matmul_mx(
@@ -243,51 +286,57 @@ def tile_list_ckg_sig_kernel(
                         lhsT=wr_codes[:, w, t * P:(t + 1) * P].bitcast(FP8X4),
                         lhsT_scale=wr_planes[:, w, t * P:(t + 1) * P],
                         rhs=codes,
-                        rhs_scale=plane_of(step, 0),
+                        rhs_scale=plane,
                         start=True,
                         stop=True,
                     )
                 nc.scalar.copy(out=both[:, w], in_=bank[:].rearrange("p t n -> p n t"))
             return both
 
-        def project_entity(step):
-            codes = [ent_codes[:, a, 2 * step * STEP:2 * (step + 1) * STEP].bitcast(FP4X4) for a in range(2)]
-            ent = {}
-            for w in (0, 1) if step == 0 else (1, 0):
-                bank = psum2.tile([P, PACK, STEP], F32, name="ent_bank", tag="ent%d" % w)
-                if step == TURNED:
-                    for a in range(2):
-                        nc.tensor.matmul_mx(
-                            out=bank[:].rearrange("p t n -> p (t n)"),
-                            lhsT=codes[a],
-                            lhsT_scale=plane_of(step, 1 + a),
-                            rhs=we_codes[:, 2 * w + a, :].bitcast(FP8X4),
-                            rhs_scale=we_scales[:, 2 * w + a, :],
-                            start=(a == 0),
-                            stop=(a == 1),
-                        )
-                    ent[w] = bank[:].rearrange("p t n -> p (t n)").rearrange("p (n t) -> p n t", t=PACK)
-                    continue
-                for t in range(PACK):
-                    for a in range(2):
-                        nc.tensor.matmul_mx(
-                            out=bank[:, t, :],
-                            lhsT=we_codes[:, 2 * w + a, t * P:(t + 1) * P].bitcast(FP8X4),
-                            lhsT_scale=we_scales[:, 2 * w + a, t * P:(t + 1) * P],
-                            rhs=codes[a],
-                            rhs_scale=plane_of(step, 1 + a),
-                            start=(a == 0),
-                            stop=(a == 1),
-                        )
-                ent[w] = bank[:].rearrange("p t n -> p n t")
-            return ent
+        def project_entity(step, w):
+            planes, cols = part_of(ent_planes, SOON, step)
+            words = ent_codes[int(step * STEP >= SOON)]
+            codes = [words[:, a, 2 * cols.start:2 * cols.stop].bitcast(FP4X4) for a in range(2)]
+            if step == SPREAD or (step, w) == (LAST, 1):
+                bank = psum1.tile([P, PACK, STEP], F32, name="spread_bank", tag="spread")
+            else:
+                bank = psum3.tile([P, PACK, STEP], F32, name="ent_bank", tag="ent")
+            if step in (SPREAD, LAST):
+                for a in range(2):
+                    nc.tensor.matmul_mx(
+                        out=flat(bank),
+                        lhsT=codes[a],
+                        lhsT_scale=planes[:, a, cols],
+                        rhs=we_codes[:, 2 * w + a, :].bitcast(FP8X4),
+                        rhs_scale=we_scales[:, 2 * w + a, :],
+                        start=(a == 0),
+                        stop=(a == 1),
+                    )
+                return flat(bank).rearrange("p (n t) -> p n t", t=PACK)
+            for t in range(PACK):
+                for a in range(2):
+                    nc.tensor.matmul_mx(
+                        out=bank[:, t, :],
+                        lhsT=we_codes[:, 2 * w + a, t * P:(t + 1) * P].bitcast(FP8X4),
+                        lhsT_scale=we_scales[:, 2 * w + a, t * P:(t + 1) * P],
+                        rhs=codes[a],
+                        rhs_scale=planes[:, a, cols],
+                        start=(a == 0),
+                        stop=(a == 1),
+                    )
+            return bank[:].rearrange("p t n -> p n t")
 
-        def multiply(ent, rel, order):
-            first = ring.tile([P, 2, STEP, PACK], F32, name="first")
-            second = ring.tile([P, 2, STEP, PACK], F32, name="second")
+        def multiply(turn, ent, rel, order):
+            if turn == 1:
+                first = placed([P, 2, STEP, PACK], F32, "held_first", rel_at(1) - 1)
+            else:
+                first = placed([P, 2, STEP, PACK], F32, "first%d" % (turn % 3), FIRST_AT + 4 * (turn % 3))
+            second = placed([P, 2, STEP, PACK], F32, "second%d" % (turn % 3), SECOND_AT + 4 * (turn % 3))
             for product in order:
                 if product == "aer both":
                     nc.vector.tensor_tensor(first[:], ent[0].unsqueeze(1).to_broadcast([P, 2, STEP, PACK]), rel[:], MULT)
+                elif product == "pieces":
+                    multiply_pieces(turn)
                 elif product == "aer arr":
                     nc.vector.tensor_tensor(first[:, 0], ent[0], rel[:, 0], MULT)
                 elif product == "aer ari":
@@ -303,6 +352,36 @@ def tile_list_ckg_sig_kernel(
                         )
             return first, second
 
+        def multiply_piece(index, ent, rel, kib):
+            product, t = divmod(index, PACK)
+            cols = slice(t * P, (t + 1) * P)
+            piece = placed([P, P], F32, "piece%d" % index, kib)
+            left = ent[product // 2].rearrange("p n t -> p (n t)")[:, cols]
+            right = rel[:, int(product in (0, 3))].rearrange("p n t -> p (n t)")[:, cols]
+            if product == 3:
+                nc.vector.scalar_tensor_tensor(piece[:], left, -1.0, right, MULT, MULT)
+            else:
+                nc.vector.tensor_tensor(piece[:], left, right, MULT)
+            return piece[:]
+
+        def multiply_pieces(turn):
+            if turn == 0:
+                due = range(EARLY_PIECES)
+                kib = LAST_CAST_AT + 0.5
+            else:
+                due = [
+                    i for i in range(EARLY_PIECES, PIECES)
+                    if FIRST_PIECE_ROUND + (i - EARLY_PIECES) * PIECE_ROUNDS // (PIECES - EARLY_PIECES) == turn
+                ]
+                kib = rel_at(turn) + int(turn > AHEAD)
+            for at, index in enumerate(due):
+                pieces.append(multiply_piece(index, ents[SPREAD], rels[SPREAD], kib + at / 2))
+                if index == PIECES // 2 - 1:
+                    ents[SPREAD][1] = project_entity(SPREAD, 1)
+
+        def quarters(product):
+            return [product.rearrange("p n t -> p (n t)")[:, t * P:(t + 1) * P] for t in range(PACK)]
+
         def new_sums():
             return ring.tile([P, 2 * STEP * PACK], BF16, name="h", align_bytes=64, bufs=QUANTISE_LAG + 2)
 
@@ -313,24 +392,17 @@ def tile_list_ckg_sig_kernel(
             )
             return h
 
-        def add_by_turning(first, second):
-            h = new_sums()
-            for w in (1, 0):
-                bank = psum1.tile([P, PACK, STEP], F32, name="rel_bank", tag="rel%d" % w)
-                for term, product in enumerate((first, second)):
-                    for t in range(PACK):
-                        nc.tensor.matmul(
-                            bank[:, t, :],
-                            product[:, w].rearrange("p n t -> p (n t)")[:, t * P:(t + 1) * P],
-                            identity[:],
-                            start=(term == 0 and t == 0),
-                            stop=(term == 1 and t == PACK - 1),
-                            is_transpose=True,
-                        )
-                (nc.scalar.copy if w == 1 else nc.vector.tensor_copy)(
-                    out=h[:].rearrange("p (w n t) -> p w n t", w=2, t=PACK)[:, w], in_=bank[:].rearrange("p t n -> p n t")
+        def add_by_turning(h, w, terms, bank, copy):
+            for index, term in enumerate(terms):
+                nc.tensor.matmul(
+                    bank[:, index % PACK, :],
+                    term,
+                    identity[:],
+                    start=(index == 0),
+                    stop=(index == len(terms) - 1),
+                    is_transpose=True,
                 )
-            return h
+            copy(out=h[:].rearrange("p (w n t) -> p w n t", w=2, t=PACK)[:, w], in_=bank[:].rearrange("p t n -> p n t"))
 
         out_view = out.rearrange("(a p) j -> p a j", p=P)
 
@@ -360,7 +432,7 @@ def tile_list_ckg_sig_kernel(
             scales = ring.tile([P, 2, 2 * STEP], U8, name="pair_scales", align_bytes=64)
             return codes, scales
 
-        def score_pair(index, pair, blocks):
+        def score_pair(step, pair, blocks):
             bank = psum2.tile([P, len(blocks), 2 * STEP], F32, name="score_bank", tag="score")
             for at, a in enumerate(blocks):
                 for w in range(2):
@@ -375,15 +447,14 @@ def tile_list_ckg_sig_kernel(
                     )
             result = ring.tile([P, len(blocks), 2 * STEP], F32, name="result", bufs=6)
             nc.scalar.activation(result[:], bank[:], SIGMOID)
-            cols = slice(2 * index * STEP, 2 * (index + 1) * STEP)
-            nc.sync.dma_start(out=out_view[:, blocks[0]:blocks[-1] + 1, cols], in_=result[:])
+            nc.sync.dma_start(out=out_view[:, blocks[0]:blocks[-1] + 1, step * STEP:(step + 2) * STEP], in_=result[:])
 
-        def score(step, h_codes, h_scales, blocks=range(N // P), queue=nc.sync):
-            bank = psum2.tile([P, len(blocks), STEP], F32, name="score_bank", tag="score")
-            for at, a in enumerate(blocks):
+        def score(step, h_codes, h_scales):
+            bank = psum2.tile([P, N // P, STEP], F32, name="score_bank", tag="score")
+            for a in range(N // P):
                 for w in range(2):
                     nc.tensor.matmul_mx(
-                        out=bank[:, at, :],
+                        out=bank[:, a, :],
                         lhsT=n_codes[w][:, a * P:(a + 1) * P].bitcast(FP8X4),
                         lhsT_scale=n_scales[:, w, a * P:(a + 1) * P],
                         rhs=h_codes[:, w * STEP:(w + 1) * STEP].bitcast(FP8X4),
@@ -391,9 +462,9 @@ def tile_list_ckg_sig_kernel(
                         start=(w == 0),
                         stop=(w == 1),
                     )
-            result = ring.tile([P, len(blocks), STEP], F32, name="result", bufs=6)
+            result = ring.tile([P, N // P, STEP], F32, name="result", bufs=6)
             nc.scalar.activation(result[:], bank[:], SIGMOID)
-            queue.dma_start(out=out_view[:, blocks[0]:blocks[-1] + 1, step * STEP:(step + 1) * STEP], in_=result[:])
+            nc.sync.dma_start(out=out_view[:, :, step * STEP:(step + 1) * STEP], in_=result[:])
 
         def score_last(h):
             h_codes = ring.tile([P, 2 * STEP], U32, name="h_codes", align_bytes=64, bufs=4)
@@ -401,7 +472,7 @@ def tile_list_ckg_sig_kernel(
             shares = (range(0, 2), range(2, 3), range(3, 4))
             banks = [
                 pool.tile([P, len(blocks), STEP], F32, name="last_bank", tag=tag)
-                for blocks, pool, tag in zip(shares, (psum2, psum2, psum1), ("ent0", "ent1", "rel1"))
+                for blocks, pool, tag in zip(shares, (psum3, psum3, psum1), ("ent", "ent", "rel1"))
             ]
             for w in (1, 0):
                 cols = slice(w * STEP, (w + 1) * STEP)
@@ -422,49 +493,61 @@ def tile_list_ckg_sig_kernel(
                             stop=(w == 0 and at == len(blocks) - 1),
                         )
             for blocks, bank, queue in zip(shares, banks, (nc.sync, nc.sync, nc.scalar)):
-                result = keep.tile([P, len(blocks), STEP], F32, name="last_result%d" % blocks[0])
+                result = placed([P, len(blocks), STEP], F32, "last_result%d" % blocks[0], LAST_RESULTS_AT + blocks[0] / 2)
                 nc.scalar.activation(result[:], bank[:], SIGMOID)
                 queue.dma_start(out=out_view[:, blocks[0]:blocks[-1] + 1, J - STEP:J], in_=result[:])
 
-        rels = [project_relation(0)]
-        ents = [project_entity(0)]
-        rels.append(project_relation(1))
+        rels = {step: project_relation(step) for step in range(HELD_STEP)}
+        ents = {1: {w: project_entity(1, w) for w in range(2)}, SPREAD: {0: project_entity(SPREAD, 0)}}
+        pieces = []
+        spread_sums = keep.tile([P, 2 * STEP * PACK], BF16, name="spread_sums", align_bytes=64)
         sums = []
+        added = 0
         pairs = []
         quantised = {}
-        for step in range(STEPS):
-            if step + 2 < STEPS:
-                rels.append(project_relation(step + 2))
-            if step + 1 < STEPS:
-                ents.append(project_entity(step + 1))
-            if step >= SCORE_LAG:
-                index, half = divmod(step - SCORE_LAG, 2)
-                score_pair(index, pairs[index], range(2 * half, 2 * half + 2))
-            if step == TURNED:
-                score(PAIRED, *quantised[PAIRED])
-            if step in (1, 2):
-                n_grouped.append(keep.tile([P, N * PACK], BF16, name="n_grouped%d" % (step - 1), align_bytes=64))
-                cast_candidates(step - 1, 0)
-                cast_candidates(step - 1, 1)
-            if step == 0:
-                order = ("aer arr", "aer ari", "aei arr", "aei ari")
-            elif step == TURNED:
+        for turn in range(ROUNDS):
+            step = turn + 1
+            if step < LAST:
+                ents[step + 1] = {w: project_entity(step + 1, w) for w in range(2)}
+            if turn + AHEAD < STEPS:
+                rels[turn + AHEAD] = project_relation(turn + AHEAD)
+            if turn in (0, 1):
+                cast_candidates(turn)
+            if turn >= SCORE_LAG:
+                index, half = divmod(turn - SCORE_LAG, 2)
+                if 2 * index < PAIRED:
+                    score_pair(2 * index + 1, pairs[index], range(2 * half, 2 * half + 2))
+            if len(pieces) >= PACK * (added + 3):
+                bank = psum2.tile([P, PACK, STEP], F32, name="sum_bank", tag="score")
+                add_by_turning(spread_sums, 1 - added, pieces[4 * added:4 * added + 4] + pieces[4 * added + 8:4 * added + 12], bank, nc.scalar.copy)
+                added = added + 1
+            if turn == ROUNDS - 2:
+                score(SPREAD, *spread_codes)
+                score(PAIRED + 1, *quantised[PAIRED])
+            if turn == ROUNDS - 1:
+                score(PAIRED + 2, *quantised[PAIRED + 1])
+            if step == LAST:
                 order = ("aer ari", "aei arr", "aer arr", "aei ari in halves")
             else:
-                order = ("aer both", "aei arr", "aei ari")
-            first, second = multiply(ents[step], rels[step], order)
-            if step != TURNED:
+                order = ("aer both", "pieces", "aei arr", "aei ari")
+            first, second = multiply(turn, ents[step], rels[step], order)
+            if step != LAST:
                 sums.append(add_products(first, second))
-            due = step - QUANTISE_LAG
+            due = turn - QUANTISE_LAG
             if due >= PAIRED:
                 quantised[due] = quantise_sum(sums[due])
             elif due >= 0:
                 if due % 2 == 0:
                     pairs.append(new_pair())
                 quantise_into_pair(sums[due], pairs[-1], due % 2)
-            if step - FIRST_CANDIDATE_STEP in (0, 1):
-                quantise_candidates(step - FIRST_CANDIDATE_STEP)
-        last_sums = add_by_turning(first, second)
-        score(STEPS - 3, *quantised[STEPS - 3])
-        score(STEPS - 2, *quantise_sum(sums[STEPS - 2]))
+            if turn - FIRST_CANDIDATE_ROUND in (0, 1):
+                quantise_candidates(turn - FIRST_CANDIDATE_ROUND)
+            if turn == ROUNDS - 3:
+                spread_codes = quantise_sum(spread_sums)
+        last_sums = new_sums()
+        for w, copy in ((1, nc.scalar.copy), (0, nc.vector.tensor_copy)):
+            bank = psum1.tile([P, PACK, STEP], F32, name="sum_bank", tag="rel%d" % w)
+            add_by_turning(last_sums, w, quarters(first[:, w]) + quarters(second[:, w]), bank, copy)
+        score(LAST - 2, *quantised[ROUNDS - 3])
+        score(LAST - 1, *quantise_sum(sums[ROUNDS - 2]))
         score_last(last_sums)

@@ -36,7 +36,7 @@ PAIRED = 10
 PIECES = 16
 FIRST_PIECE_ROUND = 2
 PIECE_ROUNDS = 9
-EARLY_PIECES = 3
+EARLY_PIECES = 6
 QUANTISE_LAG = 2
 SCORE_LAG = 4
 FIRST_CANDIDATE_ROUND = 2
@@ -51,18 +51,18 @@ WR_RAW_WORDS_AT = 46.5
 SOON_PLANES_AT = 48
 LATER_PLANES_AT = 4
 N_GROUPED_AT = (53, 0)
-HELD_STEP = 7
-LAST_CAST_AT = 138
-AHEAD = 7
+HELD_STEP = 6
+LAST_CAST_AT = 145
+AHEAD = 6
 REL_WORD_WIN_AT = 57
 LAST_RESULTS_AT = 61
 SECOND_CAST_AT = 73
 ENT_CODES_AT = 73
 ENT_SCALE_WIN_AT = 81
 REL_SCALE_WIN_AT = 85
-SPREAD_REL_AT = 89
-REL_AT = 94
-REL_CODES_AT = (85, 87)
+SPREAD_REL_AT = 90
+REL_AT = 95
+REL_CODES_AT = (83.5, 85.5, 87.5)
 
 
 def tile_list_ckg_sig_kernel(
@@ -86,12 +86,10 @@ def tile_list_ckg_sig_kernel(
             if step == SPREAD:
                 return SPREAD_REL_AT
             if step == HELD_STEP:
-                return LAST_CAST_AT + 2
-            if step == LAST:
-                return REL_AT
+                return LAST_CAST_AT + 3
             if step > AHEAD:
                 return rel_at(step - AHEAD) + 3
-            return REL_AT + 7 * (step - 1)
+            return REL_AT + 10 * (step - 1)
 
         ent_list = lists.tile([P, J // LANES], U16, name="ent_list")
         rel_list = lists.tile([P, J // LANES], U16, name="rel_list")
@@ -190,16 +188,19 @@ def tile_list_ckg_sig_kernel(
             for part in range(parts):
                 blocks = slice(part * SCALE_ROWS // parts, (part + 1) * SCALE_ROWS // parts)
                 for t in range(PACK):
-                    if piece < 2:
+                    if piece == 0 or (piece == 1 and t < PACK // 2):
                         nc.gpsimd.tensor_scalar(dst[:, t, blocks], src[:, t, blocks], 1.0, 0.0, MULT, ADD)
                     else:
-                        nc.scalar.copy(out=dst[:, t, blocks], in_=src[:, t, blocks])
+                        nc.scalar.copy(
+                            out=dst[:, t, blocks].rearrange("p b (h i) j -> p b h j i", i=4),
+                            in_=src[:, t, blocks].rearrange("p b (h i) j -> p b h j i", i=4),
+                        )
             nc.vector.quantize_mx(out=we_codes[:, piece, :].bitcast(FP8X4), scales=we_scales[:, piece, :], in_=grouped[:])
 
         nc.vector.tensor_copy(rel_planes[0][:], rel_scale_win[:].bitcast(U8).indirect(rel_list[:, 0:CHUNK // LANES]))
         gather_relation(0)
         nc.vector.tensor_copy(rel_planes[1][:], rel_scale_win[:].bitcast(U8).indirect(rel_list[:, CHUNK // LANES:J // LANES]))
-        for chunk in (1, 2):
+        for chunk in (1, 2, 3):
             rel_codes.append(placed([P, CHUNK], U32, "rel_codes%d" % chunk, REL_CODES_AT[chunk - 1]))
             gather_relation(chunk)
         quantise_entity_weight(0)
@@ -215,8 +216,6 @@ def tile_list_ckg_sig_kernel(
             ent_codes.append(codes)
         quantise_entity_weight(2)
         quantise_entity_weight(3, parts=2)
-        rel_codes.append(placed([P, CHUNK], U32, "rel_codes3", LAST_CAST_AT - 1.5))
-        gather_relation(3)
 
         ent_planes.append(move_planes("later_planes", LATER_PLANES_AT, slice(SOON // 4, J // 4)))
         n_raw = []
@@ -367,7 +366,7 @@ def tile_list_ckg_sig_kernel(
         def multiply_pieces(turn):
             if turn == 0:
                 due = range(EARLY_PIECES)
-                kib = LAST_CAST_AT + 0.5
+                kib = LAST_CAST_AT
             else:
                 due = [
                     i for i in range(EARLY_PIECES, PIECES)

@@ -29,17 +29,13 @@ CHUNK = 512
 STEP = 128
 STEPS = J // STEP
 SOON = 4 * STEP
-SPREAD = 0
+SHARED = (0, 1)
+EARLY_TURNED = (2, 3)
 LAST = STEPS - 1
+TURNED = EARLY_TURNED + (LAST,)
 ROUNDS = STEPS - 1
-PAIRED = 10
-PIECES = 16
-FIRST_PIECE_ROUND = 2
-PIECE_ROUNDS = 9
-EARLY_PIECES = 6
-QUANTISE_LAG = 2
-SCORE_LAG = 4
-FIRST_CANDIDATE_ROUND = 2
+PAIRED = 12
+HELD_STEP = 6
 
 WEIGHT_ROWS_AT = (0, 32, 40, 49)
 ENT_PAIRS_AT = 8
@@ -51,18 +47,18 @@ WR_RAW_WORDS_AT = 46.5
 SOON_PLANES_AT = 48
 LATER_PLANES_AT = 4
 N_GROUPED_AT = (53, 0)
-HELD_STEP = 6
-LAST_CAST_AT = 145
-AHEAD = 6
+SHARED_AER_AT = (49, 51)
 REL_WORD_WIN_AT = 57
-LAST_RESULTS_AT = 61
+TURNED_SECOND_AT = (57, 61)
+SHARED_FIRST_AT = 65
+LAST_RESULTS_AT = 69
 SECOND_CAST_AT = 73
 ENT_CODES_AT = 73
 ENT_SCALE_WIN_AT = 81
 REL_SCALE_WIN_AT = 85
-SPREAD_REL_AT = 90
-REL_AT = 95
-REL_CODES_AT = (83.5, 85.5, 87.5)
+REL_CODES_AT = (85, 87)
+REL_AT = 89
+LAST_CAST_AT = 125
 
 
 def tile_list_ckg_sig_kernel(
@@ -76,20 +72,20 @@ def tile_list_ckg_sig_kernel(
         ring = ctx.enter_context(tc.tile_pool(name="ring", bufs=3))
         arena = ctx.enter_context(tc.tile_pool(name="arena", bufs=1))
         psum2 = ctx.enter_context(tc.psum_pool(name="psum2", bufs=2))
-        psum3 = ctx.enter_context(tc.psum_pool(name="psum3", bufs=3))
+        psum4 = ctx.enter_context(tc.psum_pool(name="psum4", bufs=4))
         psum1 = ctx.enter_context(tc.psum_pool(name="psum1", bufs=1))
 
         def placed(shape, dtype, name, kib):
             return arena.tile(shape, dtype, name=name, tag=name, offset=int(kib * 1024), align_bytes=64)
 
         def rel_at(step):
-            if step == SPREAD:
-                return SPREAD_REL_AT
             if step == HELD_STEP:
-                return LAST_CAST_AT + 3
-            if step > AHEAD:
-                return rel_at(step - AHEAD) + 3
-            return REL_AT + 10 * (step - 1)
+                return LAST_CAST_AT + 12
+            if step < HELD_STEP:
+                return REL_AT + 6 * step
+            if step < HELD_STEP + 3:
+                return rel_at(step - HELD_STEP - 1) + 2
+            return rel_at(step - 5)
 
         ent_list = lists.tile([P, J // LANES], U16, name="ent_list")
         rel_list = lists.tile([P, J // LANES], U16, name="rel_list")
@@ -101,7 +97,7 @@ def tile_list_ckg_sig_kernel(
             keep.tile([P, CHUNK], U8, name="rel_plane0", align_bytes=64),
             keep.tile([P, J - CHUNK], U8, name="rel_plane1", align_bytes=64),
         ]
-        rel_codes = [keep.tile([P, CHUNK], U32, name="rel_codes0", align_bytes=64)]
+        rel_codes = [keep.tile([P, CHUNK], U32, name="rel_codes%d" % c, align_bytes=64) for c in range(2)]
         wr_raw_words = placed([P, 2, R], I32, "wr_raw_words", WR_RAW_WORDS_AT)
         wr_raw_scales = placed([SCALE_ROWS, 2, R // 4], I32, "wr_raw_scales", WR_RAW_SCALES_AT)
         wr_scale_rows = keep.tile([SCALE_ROWS, 2, R // 4], I32, name="wr_scale_rows", align_bytes=64)
@@ -178,13 +174,13 @@ def tile_list_ckg_sig_kernel(
 
         def quantise_entity_weight(piece, parts=1):
             if piece == 1:
-                grouped = placed([P, PACK * R], BF16, "second_cast", SECOND_CAST_AT)
+                grouped = placed([P, PACK * R], BF16, "second_cast", SECOND_CAST_AT)[:]
             elif piece == 3:
-                grouped = placed([P, PACK * R], BF16, "last_cast", LAST_CAST_AT)
+                grouped = placed([P, 4 * PACK * R], BF16, "last_cast", LAST_CAST_AT)[:, 0:PACK * R]
             else:
-                grouped = keep.tile([P, PACK * R], BF16, name="cast%d" % piece, align_bytes=64)
+                grouped = keep.tile([P, PACK * R], BF16, name="cast%d" % piece, align_bytes=64)[:]
             src = we_raw[piece][:].rearrange("p j (b t m) -> p t b m j", t=PACK, m=RUN)
-            dst = grouped[:].rearrange("p (t b m j) -> p t b m j", t=PACK, m=RUN, j=PACK)
+            dst = grouped.rearrange("p (t b m j) -> p t b m j", t=PACK, m=RUN, j=PACK)
             for part in range(parts):
                 blocks = slice(part * SCALE_ROWS // parts, (part + 1) * SCALE_ROWS // parts)
                 for t in range(PACK):
@@ -195,13 +191,14 @@ def tile_list_ckg_sig_kernel(
                             out=dst[:, t, blocks].rearrange("p b (h i) j -> p b h j i", i=4),
                             in_=src[:, t, blocks].rearrange("p b (h i) j -> p b h j i", i=4),
                         )
-            nc.vector.quantize_mx(out=we_codes[:, piece, :].bitcast(FP8X4), scales=we_scales[:, piece, :], in_=grouped[:])
+            nc.vector.quantize_mx(out=we_codes[:, piece, :].bitcast(FP8X4), scales=we_scales[:, piece, :], in_=grouped)
 
-        nc.vector.tensor_copy(rel_planes[0][:], rel_scale_win[:].bitcast(U8).indirect(rel_list[:, 0:CHUNK // LANES]))
         gather_relation(0)
+        gather_relation(1)
+        nc.vector.tensor_copy(rel_planes[0][:], rel_scale_win[:].bitcast(U8).indirect(rel_list[:, 0:CHUNK // LANES]))
         nc.vector.tensor_copy(rel_planes[1][:], rel_scale_win[:].bitcast(U8).indirect(rel_list[:, CHUNK // LANES:J // LANES]))
-        for chunk in (1, 2, 3):
-            rel_codes.append(placed([P, CHUNK], U32, "rel_codes%d" % chunk, REL_CODES_AT[chunk - 1]))
+        for chunk in (2, 3):
+            rel_codes.append(placed([P, CHUNK], U32, "rel_codes%d" % chunk, REL_CODES_AT[chunk - 2]))
             gather_relation(chunk)
         quantise_entity_weight(0)
         ent_pairs = placed([P, J], U32, "ent_pairs", ENT_PAIRS_AT)
@@ -240,7 +237,7 @@ def tile_list_ckg_sig_kernel(
             n_grouped.append(grouped)
 
         def quantise_candidates(w):
-            codes = placed([P, N], U32, "n_codes%d" % w, rel_at(FIRST_CANDIDATE_ROUND + w + 1) + 1)
+            codes = placed([P, N], U32, "n_codes%d" % w, rel_at(SHARED[w]))
             nc.vector.quantize_mx(out=codes[:].bitcast(FP8X4), scales=n_scales[:, w, :], in_=n_grouped[w][:])
             n_codes.append(codes)
 
@@ -264,10 +261,10 @@ def tile_list_ckg_sig_kernel(
                 if step >= HELD_STEP:
                     bank = psum1.tile([P, PACK, STEP], F32, name="rel_bank", tag="rel%d" % w)
                 elif w == 0:
-                    bank = psum3.tile([P, PACK, STEP], F32, name="rel_bank", tag="ent")
+                    bank = psum4.tile([P, PACK, STEP], F32, name="rel_bank", tag="ent")
                 else:
                     bank = psum2.tile([P, PACK, STEP], F32, name="rel_bank", tag="score")
-                if step in (SPREAD, LAST):
+                if step in TURNED:
                     nc.tensor.matmul_mx(
                         out=flat(bank),
                         lhsT=codes,
@@ -292,15 +289,12 @@ def tile_list_ckg_sig_kernel(
                 nc.scalar.copy(out=both[:, w], in_=bank[:].rearrange("p t n -> p n t"))
             return both
 
-        def project_entity(step, w):
+        def project_entity(step, w, tag="ent"):
             planes, cols = part_of(ent_planes, SOON, step)
             words = ent_codes[int(step * STEP >= SOON)]
             codes = [words[:, a, 2 * cols.start:2 * cols.stop].bitcast(FP4X4) for a in range(2)]
-            if step == SPREAD or (step, w) == (LAST, 1):
-                bank = psum1.tile([P, PACK, STEP], F32, name="spread_bank", tag="spread")
-            else:
-                bank = psum3.tile([P, PACK, STEP], F32, name="ent_bank", tag="ent")
-            if step in (SPREAD, LAST):
+            bank = (psum4 if tag == "ent" else psum2).tile([P, PACK, STEP], F32, name="ent_bank", tag=tag)
+            if step in TURNED:
                 for a in range(2):
                     nc.tensor.matmul_mx(
                         out=flat(bank),
@@ -325,64 +319,22 @@ def tile_list_ckg_sig_kernel(
                     )
             return bank[:].rearrange("p t n -> p n t")
 
-        def multiply(turn, ent, rel, order):
-            if turn == 1:
-                first = placed([P, 2, STEP, PACK], F32, "held_first", rel_at(1) - 1)
-            else:
-                first = placed([P, 2, STEP, PACK], F32, "first%d" % (turn % 3), FIRST_AT + 4 * (turn % 3))
-            second = placed([P, 2, STEP, PACK], F32, "second%d" % (turn % 3), SECOND_AT + 4 * (turn % 3))
-            for product in order:
-                if product == "aer both":
-                    nc.vector.tensor_tensor(first[:], ent[0].unsqueeze(1).to_broadcast([P, 2, STEP, PACK]), rel[:], MULT)
-                elif product == "pieces":
-                    multiply_pieces(turn)
-                elif product == "aer arr":
-                    nc.vector.tensor_tensor(first[:, 0], ent[0], rel[:, 0], MULT)
-                elif product == "aer ari":
-                    nc.vector.tensor_tensor(first[:, 1], ent[0], rel[:, 1], MULT)
-                elif product == "aei arr":
-                    nc.vector.tensor_tensor(second[:, 1], ent[1], rel[:, 0], MULT)
-                elif product == "aei ari":
-                    nc.vector.scalar_tensor_tensor(second[:, 0], ent[1], -1.0, rel[:, 1], MULT, MULT)
-                else:
-                    for part in (slice(0, 3 * STEP // 4), slice(3 * STEP // 4, STEP)):
-                        nc.vector.scalar_tensor_tensor(
-                            second[:, 0, part], ent[1][:, part], -1.0, rel[:, 1, part], MULT, MULT
-                        )
-            return first, second
+        def product_tile(name, base, step):
+            slot = (step + int(step > SHARED[-1])) % 3
+            return placed([P, 2, STEP, PACK], F32, "%s%d" % (name, slot), base + 4 * slot)
 
-        def multiply_piece(index, ent, rel, kib):
-            product, t = divmod(index, PACK)
-            cols = slice(t * P, (t + 1) * P)
-            piece = placed([P, P], F32, "piece%d" % index, kib)
-            left = ent[product // 2].rearrange("p n t -> p (n t)")[:, cols]
-            right = rel[:, int(product in (0, 3))].rearrange("p n t -> p (n t)")[:, cols]
-            if product == 3:
-                nc.vector.scalar_tensor_tensor(piece[:], left, -1.0, right, MULT, MULT)
-            else:
-                nc.vector.tensor_tensor(piece[:], left, right, MULT)
-            return piece[:]
+        def times_aer(engine, first, aer, rel):
+            engine.tensor_tensor(first[:], aer.unsqueeze(1).to_broadcast([P, 2, STEP, PACK]), rel[:], MULT)
 
-        def multiply_pieces(turn):
-            if turn == 0:
-                due = range(EARLY_PIECES)
-                kib = LAST_CAST_AT
-            else:
-                due = [
-                    i for i in range(EARLY_PIECES, PIECES)
-                    if FIRST_PIECE_ROUND + (i - EARLY_PIECES) * PIECE_ROUNDS // (PIECES - EARLY_PIECES) == turn
-                ]
-                kib = rel_at(turn) + int(turn > AHEAD)
-            for at, index in enumerate(due):
-                pieces.append(multiply_piece(index, ents[SPREAD], rels[SPREAD], kib + at / 2))
-                if index == PIECES // 2 - 1:
-                    ents[SPREAD][1] = project_entity(SPREAD, 1)
+        def times_aei(second, aei, rel):
+            nc.vector.tensor_tensor(second[:, 1], aei, rel[:, 0], MULT)
+            nc.vector.scalar_tensor_tensor(second[:, 0], aei, -1.0, rel[:, 1], MULT, MULT)
 
         def quarters(product):
             return [product.rearrange("p n t -> p (n t)")[:, t * P:(t + 1) * P] for t in range(PACK)]
 
         def new_sums():
-            return ring.tile([P, 2 * STEP * PACK], BF16, name="h", align_bytes=64, bufs=QUANTISE_LAG + 2)
+            return ring.tile([P, 2 * STEP * PACK], BF16, name="h", align_bytes=64, bufs=6)
 
         def add_products(first, second):
             h = new_sums()
@@ -427,8 +379,8 @@ def tile_list_ckg_sig_kernel(
                 )
 
         def new_pair():
-            codes = ring.tile([P, 2, 2 * STEP], U32, name="pair_codes", align_bytes=64)
-            scales = ring.tile([P, 2, 2 * STEP], U8, name="pair_scales", align_bytes=64)
+            codes = ring.tile([P, 2, 2 * STEP], U32, name="pair_codes", align_bytes=64, bufs=4)
+            scales = ring.tile([P, 2, 2 * STEP], U8, name="pair_scales", align_bytes=64, bufs=4)
             return codes, scales
 
         def score_pair(step, pair, blocks):
@@ -471,7 +423,7 @@ def tile_list_ckg_sig_kernel(
             shares = (range(0, 2), range(2, 3), range(3, 4))
             banks = [
                 pool.tile([P, len(blocks), STEP], F32, name="last_bank", tag=tag)
-                for blocks, pool, tag in zip(shares, (psum3, psum3, psum1), ("ent", "ent", "rel1"))
+                for blocks, pool, tag in zip(shares, (psum4, psum4, psum1), ("ent", "ent", "rel1"))
             ]
             for w in (1, 0):
                 cols = slice(w * STEP, (w + 1) * STEP)
@@ -496,57 +448,100 @@ def tile_list_ckg_sig_kernel(
                 nc.scalar.activation(result[:], bank[:], SIGMOID)
                 queue.dma_start(out=out_view[:, blocks[0]:blocks[-1] + 1, J - STEP:J], in_=result[:])
 
-        rels = {step: project_relation(step) for step in range(HELD_STEP)}
-        ents = {1: {w: project_entity(1, w) for w in range(2)}, SPREAD: {0: project_entity(SPREAD, 0)}}
-        pieces = []
-        spread_sums = keep.tile([P, 2 * STEP * PACK], BF16, name="spread_sums", align_bytes=64)
-        sums = []
-        added = 0
-        pairs = []
+        rels = {step: project_relation(step) for step in EARLY_TURNED + SHARED + (4, 5)}
+        aer = {step: project_entity(step, 0) for step in EARLY_TURNED}
+        for step in SHARED:
+            bank = project_entity(step, 0, "score")
+            copied = placed([P, STEP, PACK], F32, "shared_aer%d" % step, SHARED_AER_AT[step])
+            nc.scalar.copy(out=copied[:], in_=bank)
+            aer[step] = copied[:]
+        aei = {}
+        for turned, shared, tag in zip(EARLY_TURNED, SHARED, ("ent", "score")):
+            aei[turned] = project_entity(turned, 1, tag)
+            aei[shared] = project_entity(shared, 1, tag)
+        first = {}
+        second = {}
+        sums = {}
+        pairs = {}
         quantised = {}
+        halves = []
+
+        def quantise_step(step):
+            if step >= PAIRED:
+                quantised[step] = quantise_sum(sums[step])
+                return
+            if step % 2 == 0:
+                pairs[step // 2] = new_pair()
+            quantise_into_pair(sums[step], pairs[step // 2], step % 2)
+            if step % 2 == 1:
+                halves.extend((step // 2, half) for half in range(2))
+
+        later = HELD_STEP
         for turn in range(ROUNDS):
             step = turn + 1
-            if step < LAST:
-                ents[step + 1] = {w: project_entity(step + 1, w) for w in range(2)}
-            if turn + AHEAD < STEPS:
-                rels[turn + AHEAD] = project_relation(turn + AHEAD)
+            if 2 <= turn < ROUNDS - 1:
+                aer[step + 1] = project_entity(step + 1, 0)
+                aei[step + 1] = project_entity(step + 1, 1)
+            relation_due = turn != 1 and later < STEPS
+            if relation_due:
+                rels[later] = project_relation(later)
+                later = later + 1
             if turn in (0, 1):
                 cast_candidates(turn)
-            if turn >= SCORE_LAG:
-                index, half = divmod(turn - SCORE_LAG, 2)
-                if 2 * index < PAIRED:
-                    score_pair(2 * index + 1, pairs[index], range(2 * half, 2 * half + 2))
-            if len(pieces) >= PACK * (added + 3):
-                bank = psum2.tile([P, PACK, STEP], F32, name="sum_bank", tag="score")
-                add_by_turning(spread_sums, 1 - added, pieces[4 * added:4 * added + 4] + pieces[4 * added + 8:4 * added + 12], bank, nc.scalar.copy)
-                added = added + 1
-            if turn == ROUNDS - 2:
-                score(SPREAD, *spread_codes)
-                score(PAIRED + 1, *quantised[PAIRED])
+            if turn - 2 in (0, 1):
+                turned = EARLY_TURNED[turn - 2]
+                sums[turned] = new_sums()
+                pool, tag = ((psum4, "ent"), (psum2, "score"))[turn - 2]
+                for w in (1, 0):
+                    bank = pool.tile([P, PACK, STEP], F32, name="sum_bank", tag=tag)
+                    add_by_turning(sums[turned], w, quarters(first[turned][:, w]) + quarters(second[turned][:, w]), bank, nc.scalar.copy)
+            for index, half in sorted(halves)[:1 if relation_due else 2]:
+                halves.remove((index, half))
+                score_pair(2 * index, pairs[index], range(2 * half, 2 * half + 2))
             if turn == ROUNDS - 1:
-                score(PAIRED + 2, *quantised[PAIRED + 1])
-            if step == LAST:
-                order = ("aer ari", "aei arr", "aer arr", "aei ari in halves")
+                score(PAIRED, *quantised[PAIRED])
+            if turn == 0:
+                first[0] = placed([P, 2, STEP, PACK], F32, "shared_first0", LAST_CAST_AT)
+                first[1] = placed([P, 2, STEP, PACK], F32, "shared_first1", SHARED_FIRST_AT)
+                for shared in SHARED:
+                    times_aer(nc.gpsimd, first[shared], aer[shared], rels[shared])
+                for at, turned in enumerate(EARLY_TURNED):
+                    first[turned] = placed([P, 2, STEP, PACK], F32, "turned_first%d" % at, LAST_CAST_AT + 4 + 4 * at)
+                    times_aer(nc.vector, first[turned], aer[turned], rels[turned])
+            elif turn in (1, 2):
+                turned, shared = EARLY_TURNED[turn - 1], SHARED[turn - 1]
+                second[turned] = placed([P, 2, STEP, PACK], F32, "turned_second%d" % turn, TURNED_SECOND_AT[turn - 1])
+                times_aei(second[turned], aei[turned], rels[turned])
+                second[shared] = product_tile("second", SECOND_AT, shared)
+                times_aei(second[shared], aei[shared], rels[shared])
+                sums[shared] = add_products(first[shared], second[shared])
+                quantise_candidates(turn - 1)
+            elif step < LAST:
+                first[step] = product_tile("first", FIRST_AT, step)
+                second[step] = product_tile("second", SECOND_AT, step)
+                times_aer(nc.vector, first[step], aer[step], rels[step])
+                times_aei(second[step], aei[step], rels[step])
+                sums[step] = add_products(first[step], second[step])
             else:
-                order = ("aer both", "pieces", "aei arr", "aei ari")
-            first, second = multiply(turn, ents[step], rels[step], order)
-            if step != LAST:
-                sums.append(add_products(first, second))
-            due = turn - QUANTISE_LAG
-            if due >= PAIRED:
-                quantised[due] = quantise_sum(sums[due])
-            elif due >= 0:
-                if due % 2 == 0:
-                    pairs.append(new_pair())
-                quantise_into_pair(sums[due], pairs[-1], due % 2)
-            if turn - FIRST_CANDIDATE_ROUND in (0, 1):
-                quantise_candidates(turn - FIRST_CANDIDATE_ROUND)
-            if turn == ROUNDS - 3:
-                spread_codes = quantise_sum(spread_sums)
+                first[step] = product_tile("first", FIRST_AT, step)
+                second[step] = product_tile("second", SECOND_AT, step)
+                nc.vector.tensor_tensor(first[step][:, 1], aer[step], rels[step][:, 1], MULT)
+                nc.vector.tensor_tensor(second[step][:, 1], aei[step], rels[step][:, 0], MULT)
+                nc.vector.tensor_tensor(first[step][:, 0], aer[step], rels[step][:, 0], MULT)
+                for part in (slice(0, 3 * STEP // 4), slice(3 * STEP // 4, STEP)):
+                    nc.vector.scalar_tensor_tensor(
+                        second[step][:, 0, part], aei[step][:, part], -1.0, rels[step][:, 1, part], MULT, MULT
+                    )
+            if turn in (3, 4):
+                quantise_step(SHARED[turn - 3])
+            if turn >= 5:
+                quantise_step(turn - 1)
+            if turn in (4, 5):
+                quantise_step(EARLY_TURNED[turn - 4])
         last_sums = new_sums()
         for w, copy in ((1, nc.scalar.copy), (0, nc.vector.tensor_copy)):
             bank = psum1.tile([P, PACK, STEP], F32, name="sum_bank", tag="rel%d" % w)
-            add_by_turning(last_sums, w, quarters(first[:, w]) + quarters(second[:, w]), bank, copy)
-        score(LAST - 2, *quantised[ROUNDS - 3])
-        score(LAST - 1, *quantise_sum(sums[ROUNDS - 2]))
+            add_by_turning(last_sums, w, quarters(first[LAST][:, w]) + quarters(second[LAST][:, w]), bank, copy)
+        score(LAST - 2, *quantised[LAST - 2])
+        score(LAST - 1, *quantise_sum(sums[LAST - 1]))
         score_last(last_sums)

@@ -34,6 +34,10 @@ EARLY_TURNED = (2, 3)
 LAST = STEPS - 1
 TURNED = EARLY_TURNED + (LAST,)
 ROUNDS = STEPS - 1
+SHARE = (128, 64)
+REL_BANKS = (4, 5)
+SCORE_BANKS = (7, 6)
+EARLY_REL_BANKS = (0, 1, 2, 3, 6, 7)
 PAIRED = 12
 HELD_STEP = 6
 
@@ -50,7 +54,6 @@ N_GROUPED_AT = (53, 0)
 SHARED_AER_AT = (49, 51)
 REL_WORD_WIN_AT = 57
 TURNED_SECOND_AT = (57, 61)
-SHARED_FIRST_AT = 65
 LAST_RESULTS_AT = 69
 SECOND_CAST_AT = 73
 ENT_CODES_AT = 73
@@ -71,9 +74,16 @@ def tile_list_ckg_sig_kernel(
         keep = ctx.enter_context(tc.tile_pool(name="keep", bufs=1))
         ring = ctx.enter_context(tc.tile_pool(name="ring", bufs=3))
         arena = ctx.enter_context(tc.tile_pool(name="arena", bufs=1))
-        psum2 = ctx.enter_context(tc.psum_pool(name="psum2", bufs=2))
-        psum4 = ctx.enter_context(tc.psum_pool(name="psum4", bufs=4))
-        psum1 = ctx.enter_context(tc.psum_pool(name="psum1", bufs=1))
+        psum = ctx.enter_context(tc.psum_pool(name="psum", bufs=1))
+
+        def new_bank(index, groups=PACK, width=STEP):
+            return psum.tile([P, groups, width], F32, name="bank", tag="bank%d" % index)
+
+        scored = []
+
+        def score_bank(groups, width):
+            scored.append(len(scored))
+            return new_bank(SCORE_BANKS[scored[-1] % 2], groups, width)
 
         def placed(shape, dtype, name, kib):
             return arena.tile(shape, dtype, name=name, tag=name, offset=int(kib * 1024), align_bytes=64)
@@ -176,7 +186,7 @@ def tile_list_ckg_sig_kernel(
             if piece == 1:
                 grouped = placed([P, PACK * R], BF16, "second_cast", SECOND_CAST_AT)[:]
             elif piece == 3:
-                grouped = placed([P, 4 * PACK * R], BF16, "last_cast", LAST_CAST_AT)[:, 0:PACK * R]
+                grouped = placed([P, 5 * PACK * R], BF16, "last_cast", LAST_CAST_AT)[:, 0:PACK * R]
             else:
                 grouped = keep.tile([P, PACK * R], BF16, name="cast%d" % piece, align_bytes=64)[:]
             src = we_raw[piece][:].rearrange("p j (b t m) -> p t b m j", t=PACK, m=RUN)
@@ -237,7 +247,7 @@ def tile_list_ckg_sig_kernel(
             n_grouped.append(grouped)
 
         def quantise_candidates(w):
-            codes = placed([P, N], U32, "n_codes%d" % w, rel_at(SHARED[w]))
+            codes = placed([P, N], U32, "n_codes%d" % w, rel_at((3, 1)[w]))
             nc.vector.quantize_mx(out=codes[:].bitcast(FP8X4), scales=n_scales[:, w, :], in_=n_grouped[w][:])
             n_codes.append(codes)
 
@@ -259,11 +269,9 @@ def tile_list_ckg_sig_kernel(
             both = placed([P, 2, STEP, PACK], F32, "rel%d" % step, rel_at(step))
             for w in range(2):
                 if step >= HELD_STEP:
-                    bank = psum1.tile([P, PACK, STEP], F32, name="rel_bank", tag="rel%d" % w)
-                elif w == 0:
-                    bank = psum4.tile([P, PACK, STEP], F32, name="rel_bank", tag="ent")
+                    bank = new_bank(REL_BANKS[w])
                 else:
-                    bank = psum2.tile([P, PACK, STEP], F32, name="rel_bank", tag="score")
+                    bank = new_bank(EARLY_REL_BANKS[(2 * len(rels) + w) % len(EARLY_REL_BANKS)])
                 if step in TURNED:
                     nc.tensor.matmul_mx(
                         out=flat(bank),
@@ -289,11 +297,11 @@ def tile_list_ckg_sig_kernel(
                 nc.scalar.copy(out=both[:, w], in_=bank[:].rearrange("p t n -> p n t"))
             return both
 
-        def project_entity(step, w, tag="ent"):
+        def project_entity(step, w, index):
             planes, cols = part_of(ent_planes, SOON, step)
             words = ent_codes[int(step * STEP >= SOON)]
             codes = [words[:, a, 2 * cols.start:2 * cols.stop].bitcast(FP4X4) for a in range(2)]
-            bank = (psum4 if tag == "ent" else psum2).tile([P, PACK, STEP], F32, name="ent_bank", tag=tag)
+            bank = new_bank(index)
             if step in TURNED:
                 for a in range(2):
                     nc.tensor.matmul_mx(
@@ -323,8 +331,9 @@ def tile_list_ckg_sig_kernel(
             slot = (step + int(step > SHARED[-1])) % 3
             return placed([P, 2, STEP, PACK], F32, "%s%d" % (name, slot), base + 4 * slot)
 
-        def times_aer(engine, first, aer, rel):
-            engine.tensor_tensor(first[:], aer.unsqueeze(1).to_broadcast([P, 2, STEP, PACK]), rel[:], MULT)
+        def times_aer(engine, first, aer, rel, cols=slice(0, STEP)):
+            both = aer.unsqueeze(1).to_broadcast([P, 2, cols.stop - cols.start, PACK])
+            engine.tensor_tensor(first[:, :, cols], both, rel[:, :, cols], MULT)
 
         def times_aei(second, aei, rel):
             nc.vector.tensor_tensor(second[:, 1], aei, rel[:, 0], MULT)
@@ -336,8 +345,8 @@ def tile_list_ckg_sig_kernel(
         def new_sums():
             return ring.tile([P, 2 * STEP * PACK], BF16, name="h", align_bytes=64, bufs=6)
 
-        def add_products(first, second):
-            h = new_sums()
+        def add_products(first, second, kib=None):
+            h = new_sums() if kib is None else placed([P, 2 * STEP * PACK], BF16, "held_sums", kib)
             nc.gpsimd.tensor_tensor(
                 h[:], first[:].rearrange("p w n t -> p (w n t)"), second[:].rearrange("p w n t -> p (w n t)"), ADD
             )
@@ -384,7 +393,7 @@ def tile_list_ckg_sig_kernel(
             return codes, scales
 
         def score_pair(step, pair, blocks):
-            bank = psum2.tile([P, len(blocks), 2 * STEP], F32, name="score_bank", tag="score")
+            bank = score_bank(len(blocks), 2 * STEP)
             for at, a in enumerate(blocks):
                 for w in range(2):
                     nc.tensor.matmul_mx(
@@ -401,7 +410,7 @@ def tile_list_ckg_sig_kernel(
             nc.sync.dma_start(out=out_view[:, blocks[0]:blocks[-1] + 1, step * STEP:(step + 2) * STEP], in_=result[:])
 
         def score(step, h_codes, h_scales):
-            bank = psum2.tile([P, N // P, STEP], F32, name="score_bank", tag="score")
+            bank = score_bank(N // P, STEP)
             for a in range(N // P):
                 for w in range(2):
                     nc.tensor.matmul_mx(
@@ -421,10 +430,7 @@ def tile_list_ckg_sig_kernel(
             h_codes = ring.tile([P, 2 * STEP], U32, name="h_codes", align_bytes=64, bufs=4)
             h_scales = ring.tile([P, 2 * STEP], U8, name="h_scales", align_bytes=64, bufs=4)
             shares = (range(0, 2), range(2, 3), range(3, 4))
-            banks = [
-                pool.tile([P, len(blocks), STEP], F32, name="last_bank", tag=tag)
-                for blocks, pool, tag in zip(shares, (psum4, psum4, psum1), ("ent", "ent", "rel1"))
-            ]
+            banks = [new_bank(index, len(blocks)) for blocks, index in zip(shares, (2, 3, REL_BANKS[1]))]
             for w in (1, 0):
                 cols = slice(w * STEP, (w + 1) * STEP)
                 nc.vector.quantize_mx(
@@ -448,17 +454,21 @@ def tile_list_ckg_sig_kernel(
                 nc.scalar.activation(result[:], bank[:], SIGMOID)
                 queue.dma_start(out=out_view[:, blocks[0]:blocks[-1] + 1, J - STEP:J], in_=result[:])
 
-        rels = {step: project_relation(step) for step in EARLY_TURNED + SHARED + (4, 5)}
-        aer = {step: project_entity(step, 0) for step in EARLY_TURNED}
-        for step in SHARED:
-            bank = project_entity(step, 0, "score")
-            copied = placed([P, STEP, PACK], F32, "shared_aer%d" % step, SHARED_AER_AT[step])
-            nc.scalar.copy(out=copied[:], in_=bank)
-            aer[step] = copied[:]
-        aei = {}
-        for turned, shared, tag in zip(EARLY_TURNED, SHARED, ("ent", "score")):
-            aei[turned] = project_entity(turned, 1, tag)
-            aei[shared] = project_entity(shared, 1, tag)
+        rels = {}
+        for step in EARLY_TURNED + SHARED + (4, 5):
+            rels[step] = project_relation(step)
+        aer = {}
+        copied = {}
+
+        def project_shared(step, index):
+            aer[step] = project_entity(step, 0, index)
+            copied[step] = placed([P, SHARE[step], PACK], F32, "shared_aer%d" % step, SHARED_AER_AT[step])
+            nc.scalar.copy(out=copied[step][:], in_=aer[step][:, 0:SHARE[step]])
+
+        project_shared(0, 6)
+        aer[2] = project_entity(2, 0, 0)
+        aer[3] = project_entity(3, 0, 6)
+        aei = {step: project_entity(step, 1, index) for step, index in ((2, 2), (0, 3), (3, 7))}
         first = {}
         second = {}
         sums = {}
@@ -479,21 +489,28 @@ def tile_list_ckg_sig_kernel(
         later = HELD_STEP
         for turn in range(ROUNDS):
             step = turn + 1
+            if turn == 1:
+                aei[1] = project_entity(1, 1, 6)
+            if turn == 2:
+                turned = EARLY_TURNED[0]
+                sums[turned] = new_sums()
+                for w in (1, 0):
+                    bank = new_bank(1 - w)
+                    add_by_turning(sums[turned], w, quarters(first[turned][:, w]) + quarters(second[turned][:, w]), bank, nc.scalar.copy)
             if 2 <= turn < ROUNDS - 1:
-                aer[step + 1] = project_entity(step + 1, 0)
-                aei[step + 1] = project_entity(step + 1, 1)
+                aer[step + 1] = project_entity(step + 1, 0, 2 * (step % 2))
+                aei[step + 1] = project_entity(step + 1, 1, 2 * (step % 2) + 1)
             relation_due = turn != 1 and later < STEPS
             if relation_due:
                 rels[later] = project_relation(later)
                 later = later + 1
             if turn in (0, 1):
                 cast_candidates(turn)
-            if turn - 2 in (0, 1):
-                turned = EARLY_TURNED[turn - 2]
+            if turn == 3:
+                turned = EARLY_TURNED[1]
                 sums[turned] = new_sums()
-                pool, tag = ((psum4, "ent"), (psum2, "score"))[turn - 2]
                 for w in (1, 0):
-                    bank = pool.tile([P, PACK, STEP], F32, name="sum_bank", tag=tag)
+                    bank = score_bank(PACK, STEP)
                     add_by_turning(sums[turned], w, quarters(first[turned][:, w]) + quarters(second[turned][:, w]), bank, nc.scalar.copy)
             for index, half in sorted(halves)[:1 if relation_due else 2]:
                 halves.remove((index, half))
@@ -502,20 +519,25 @@ def tile_list_ckg_sig_kernel(
                 score(PAIRED, *quantised[PAIRED])
             if turn == 0:
                 first[0] = placed([P, 2, STEP, PACK], F32, "shared_first0", LAST_CAST_AT)
-                first[1] = placed([P, 2, STEP, PACK], F32, "shared_first1", SHARED_FIRST_AT)
-                for shared in SHARED:
-                    times_aer(nc.gpsimd, first[shared], aer[shared], rels[shared])
+                first[1] = placed([P, 2, STEP, PACK], F32, "shared_first1", LAST_CAST_AT + 16)
+                times_aer(nc.gpsimd, first[0], copied[0][:], rels[0])
                 for at, turned in enumerate(EARLY_TURNED):
                     first[turned] = placed([P, 2, STEP, PACK], F32, "turned_first%d" % at, LAST_CAST_AT + 4 + 4 * at)
                     times_aer(nc.vector, first[turned], aer[turned], rels[turned])
+                    if at == 0:
+                        project_shared(1, 0)
+                times_aer(nc.vector, first[1], aer[1][:, SHARE[1]:STEP], rels[1], slice(SHARE[1], STEP))
+                times_aer(nc.gpsimd, first[1], copied[1][:], rels[1], slice(0, SHARE[1]))
             elif turn in (1, 2):
                 turned, shared = EARLY_TURNED[turn - 1], SHARED[turn - 1]
                 second[turned] = placed([P, 2, STEP, PACK], F32, "turned_second%d" % turn, TURNED_SECOND_AT[turn - 1])
                 times_aei(second[turned], aei[turned], rels[turned])
                 second[shared] = product_tile("second", SECOND_AT, shared)
                 times_aei(second[shared], aei[shared], rels[shared])
-                sums[shared] = add_products(first[shared], second[shared])
-                quantise_candidates(turn - 1)
+                if turn == 2:
+                    quantise_candidates(0)
+                    quantise_step(SHARED[0])
+                sums[shared] = add_products(first[shared], second[shared], N_GROUPED_AT[0] if turn == 2 else None)
             elif step < LAST:
                 first[step] = product_tile("first", FIRST_AT, step)
                 second[step] = product_tile("second", SECOND_AT, step)
@@ -532,15 +554,17 @@ def tile_list_ckg_sig_kernel(
                     nc.vector.scalar_tensor_tensor(
                         second[step][:, 0, part], aei[step][:, part], -1.0, rels[step][:, 1, part], MULT, MULT
                     )
-            if turn in (3, 4):
-                quantise_step(SHARED[turn - 3])
+            if turn == 3:
+                quantise_candidates(1)
+            if turn == 4:
+                quantise_step(SHARED[1])
             if turn >= 5:
                 quantise_step(turn - 1)
             if turn in (4, 5):
                 quantise_step(EARLY_TURNED[turn - 4])
         last_sums = new_sums()
         for w, copy in ((1, nc.scalar.copy), (0, nc.vector.tensor_copy)):
-            bank = psum1.tile([P, PACK, STEP], F32, name="sum_bank", tag="rel%d" % w)
+            bank = new_bank(REL_BANKS[w])
             add_by_turning(last_sums, w, quarters(first[LAST][:, w]) + quarters(second[LAST][:, w]), bank, copy)
         score(LAST - 2, *quantised[LAST - 2])
         score(LAST - 1, *quantise_sum(sums[LAST - 1]))

from contextlib import ExitStack

import concourse.mybir as mybir
from concourse.masks import make_identity

K, L, R, N, T, J = 1024, 512, 512, 512, 4096, 2048
FLOPS = 2 * J * (2 * K * R + 2 * L * R + 2 * R * N)

F32 = mybir.dt.float32
BF16 = mybir.dt.bfloat16
I32 = mybir.dt.int32
U32 = mybir.dt.uint32
U16 = mybir.dt.uint16
U8 = mybir.dt.uint8
FP8X4 = mybir.dt.float8_e4m3fn_x4
FP4X4 = mybir.dt.float4_e2m1fn_x4
MULT = mybir.AluOpType.mult
ADD = mybir.AluOpType.add
SIGMOID = mybir.ActivationFunctionType.Sigmoid

P = 128
PACK = 4
K_PASS = P * PACK
RUN = 8
SCALE_ROWS = K_PASS // 32
QUADRANT = 32
LANES = 16
CHUNK = 512
STEP = 128
STEPS = J // STEP
SOON = 4 * STEP
SHARED = (0, 1)
EARLY_TURNED = (2, 3)
LAST = STEPS - 1
TURNED = EARLY_TURNED + (LAST,)
ROUNDS = STEPS - 1
SHARE = (128, 64)
REL_BANKS = (4, 5)
SCORE_BANKS = (7, 6)
EARLY_REL_BANKS = (0, 1, 2, 3, 6, 7)
PAIRED = 12
HELD_STEP = 6

WEIGHT_ROWS_AT = (0, 32, 40, 49)
ENT_PAIRS_AT = 8
ENT_WORD_WIN_AT = 16
FIRST_AT = 8
SECOND_AT = 20
WR_RAW_SCALES_AT = 31.5
WR_RAW_WORDS_AT = 46.5
SOON_PLANES_AT = 48
LATER_PLANES_AT = 4
N_GROUPED_AT = (53, 0)
SHARED_AER_AT = (49, 51)
REL_WORD_WIN_AT = 57
TURNED_SECOND_AT = (57, 61)
LAST_RESULTS_AT = 69
SECOND_CAST_AT = 73
ENT_CODES_AT = 73
ENT_SCALE_WIN_AT = 81
REL_SCALE_WIN_AT = 85
REL_CODES_AT = (85, 87)
REL_AT = 89
LAST_CAST_AT = 125


def tile_list_ckg_sig_kernel(
    tc, tab_words, tab_scales, tab2_words, tab2_scales, wer, wei, wrr_words, wrr_scales,
    wri_words, wri_scales, nr, ni, offs, offs2, out
):
    nc = tc.nc
    with ExitStack() as ctx:
        lists = ctx.enter_context(tc.tile_pool(name="lists", bufs=1))
        keep = ctx.enter_context(tc.tile_pool(name="keep", bufs=1))
        ring = ctx.enter_context(tc.tile_pool(name="ring", bufs=3))
        arena = ctx.enter_context(tc.tile_pool(name="arena", bufs=1))
        psum = ctx.enter_context(tc.psum_pool(name="psum", bufs=1))

        def new_bank(index, groups=PACK, width=STEP):
            return psum.tile([P, groups, width], F32, name="bank", tag="bank%d" % index)

        scored = []

        def score_bank(groups, width):
            scored.append(len(scored))
            return new_bank(SCORE_BANKS[scored[-1] % 2], groups, width)

        def placed(shape, dtype, name, kib):
            return arena.tile(shape, dtype, name=name, tag=name, offset=int(kib * 1024), align_bytes=64)

        def rel_at(step):
            if step == HELD_STEP:
                return LAST_CAST_AT + 12
            if step < HELD_STEP:
                return REL_AT + 6 * step
            if step < HELD_STEP + 3:
                return rel_at(step - HELD_STEP - 1) + 2
            return rel_at(step - 5)

        ent_list = lists.tile([P, J // LANES], U16, name="ent_list")
        rel_list = lists.tile([P, J // LANES], U16, name="rel_list")
        ent_scale_win = placed([P, T // 4], I32, "ent_scale_win", ENT_SCALE_WIN_AT)
        rel_scale_win = placed([P, T // 4], I32, "rel_scale_win", REL_SCALE_WIN_AT)
        rel_word_win = placed([P, T], I32, "rel_word_win", REL_WORD_WIN_AT)
        ent_rows = keep.tile([P, J], U8, name="ent_rows", align_bytes=64)
        rel_planes = [
            keep.tile([P, CHUNK], U8, name="rel_plane0", align_bytes=64),
            keep.tile([P, J - CHUNK], U8, name="rel_plane1", align_bytes=64),
        ]
        rel_codes = [keep.tile([P, CHUNK], U32, name="rel_codes%d" % c, align_bytes=64) for c in range(2)]
        wr_raw_words = placed([P, 2, R], I32, "wr_raw_words", WR_RAW_WORDS_AT)
        wr_raw_scales = placed([SCALE_ROWS, 2, R // 4], I32, "wr_raw_scales", WR_RAW_SCALES_AT)
        wr_scale_rows = keep.tile([SCALE_ROWS, 2, R // 4], I32, name="wr_scale_rows", align_bytes=64)
        wr_codes = keep.tile([P, 2, R], I32, name="wr_codes", align_bytes=64)
        wr_scales = keep.tile([P, 2, R // 4], I32, name="wr_scales", align_bytes=64)
        we_codes = keep.tile([P, 4, R], U32, name="we_codes", align_bytes=64)
        we_scales = keep.tile([P, 4, R], U8, name="we_scales", align_bytes=64)
        n_scales = keep.tile([P, 2, N], U8, name="n_scales", align_bytes=64)

        nc.gpsimd.memset(rel_scale_win[:], 0)
        nc.vector.memset(ent_scale_win[32:64, :], 0)
        nc.vector.memset(ent_scale_win[64:P, :], 0)
        nc.gpsimd.memset(wr_scales[:], 0)

        identity = keep.tile([P, P], F32, name="identity")
        make_identity(nc, identity[:])

        def words_view(words):
            return words[0].rearrange("p n i -> p (n i)").bitcast(I32)

        def load_rows(src, piece, parts=1):
            raw = placed([P, PACK, R], F32, "raw%d" % piece, WEIGHT_ROWS_AT[piece])
            for part in range(parts):
                cols = slice(part * R // parts, (part + 1) * R // parts)
                nc.sync.dma_start(out=raw[:, :, cols], in_=src.rearrange("(p j) c -> p j c", j=PACK)[:, :, cols])
            return raw

        nc.sync.dma_start(ent_list[:], offs)
        nc.sync.dma_start(out=ent_scale_win[0:2 * SCALE_ROWS, :], in_=tab_scales.bitcast(I32).rearrange("a q t -> q a t"))
        nc.sync.dma_start(rel_list[:], offs2)
        for w, scales in enumerate((wrr_scales, wri_scales)):
            nc.sync.dma_start(out=wr_raw_scales[:, w, :], in_=scales[0].bitcast(I32))
        nc.sync.dma_start(out=rel_word_win[:], in_=words_view(tab2_words))
        for quad in range(4):
            nc.sync.dma_start(
                out=rel_scale_win[QUADRANT * quad:QUADRANT * quad + 4, :], in_=tab2_scales[0].bitcast(I32)[4 * quad:4 * quad + 4]
            )
        for w, words in enumerate((wrr_words, wri_words)):
            nc.sync.dma_start(out=wr_raw_words[:, w, :], in_=words_view(words))
        we_raw = [load_rows(wer[0:K_PASS, :], 0)]
        for w in range(2):
            nc.scalar.copy(
                out=wr_scale_rows[:].bitcast(U32)[:, w, :].rearrange("p (t b m) -> p t b m", t=PACK, m=RUN // 4),
                in_=wr_raw_scales[:].bitcast(U32)[:, w, :].rearrange("p (b t m) -> p t b m", t=PACK, m=RUN // 4),
            )
        for row in range(4):
            nc.scalar.dma_start(out=wr_scales[row:P:QUADRANT], in_=wr_scale_rows[row:SCALE_ROWS:4])
        ent_word_win = placed([P, T], I32, "ent_word_win", ENT_WORD_WIN_AT)
        nc.sync.dma_start(out=ent_word_win[:], in_=words_view(tab_words))
        we_raw.append(load_rows(wer[K_PASS:K, :], 1))
        for w in range(2):
            nc.scalar.copy(
                out=wr_codes[:].bitcast(U32)[:, w, :].rearrange("p (t b m) -> p t b m", t=PACK, m=RUN),
                in_=wr_raw_words[:].bitcast(U32)[:, w, :].rearrange("p (b t m) -> p t b m", t=PACK, m=RUN),
            )

        nc.vector.tensor_copy(ent_rows[:], ent_scale_win[:].bitcast(U8).indirect(ent_list[:]))

        def move_planes(name, kib, words):
            plane = placed([P, 2, words.stop - words.start], I32, name, kib)
            for quad in range(4):
                nc.sync.dma_start(
                    out=plane[QUADRANT * quad:QUADRANT * quad + 4], in_=ent_rows[:].bitcast(I32)[8 * quad:8 * quad + 8, words]
                )
            return plane

        we_raw.append(load_rows(wei[0:K_PASS, :], 2))
        ent_planes = [move_planes("soon_planes", SOON_PLANES_AT, slice(0, SOON // 4))]
        we_raw.append(load_rows(wei[K_PASS:K, :], 3, parts=2))

        def gather_relation(chunk):
            entries = slice(chunk * CHUNK // LANES, (chunk + 1) * CHUNK // LANES)
            nc.vector.tensor_copy(rel_codes[chunk][:], rel_word_win[:].bitcast(U32).indirect(rel_list[:, entries]))

        def quantise_entity_weight(piece, parts=1):
            if piece == 1:
                grouped = placed([P, PACK * R], BF16, "second_cast", SECOND_CAST_AT)[:]
            elif piece == 3:
                grouped = placed([P, 5 * PACK * R], BF16, "last_cast", LAST_CAST_AT)[:, 0:PACK * R]
            else:
                grouped = keep.tile([P, PACK * R], BF16, name="cast%d" % piece, align_bytes=64)[:]
            src = we_raw[piece][:].rearrange("p j (b t m) -> p t b m j", t=PACK, m=RUN)
            dst = grouped.rearrange("p (t b m j) -> p t b m j", t=PACK, m=RUN, j=PACK)
            for part in range(parts):
                blocks = slice(part * SCALE_ROWS // parts, (part + 1) * SCALE_ROWS // parts)
                for t in range(PACK):
                    if piece == 0 or (piece == 1 and t < PACK // 2):
                        nc.gpsimd.tensor_scalar(dst[:, t, blocks], src[:, t, blocks], 1.0, 0.0, MULT, ADD)
                    else:
                        nc.scalar.copy(
                            out=dst[:, t, blocks].rearrange("p b (h i) j -> p b h j i", i=4),
                            in_=src[:, t, blocks].rearrange("p b (h i) j -> p b h j i", i=4),
                        )
            nc.vector.quantize_mx(out=we_codes[:, piece, :].bitcast(FP8X4), scales=we_scales[:, piece, :], in_=grouped)

        gather_relation(0)
        gather_relation(1)
        nc.vector.tensor_copy(rel_planes[0][:], rel_scale_win[:].bitcast(U8).indirect(rel_list[:, 0:CHUNK // LANES]))
        nc.vector.tensor_copy(rel_planes[1][:], rel_scale_win[:].bitcast(U8).indirect(rel_list[:, CHUNK // LANES:J // LANES]))
        for chunk in (2, 3):
            rel_codes.append(placed([P, CHUNK], U32, "rel_codes%d" % chunk, REL_CODES_AT[chunk - 2]))
            gather_relation(chunk)
        quantise_entity_weight(0)
        ent_pairs = placed([P, J], U32, "ent_pairs", ENT_PAIRS_AT)
        nc.vector.tensor_copy(ent_pairs[:], ent_word_win[:].bitcast(U32).indirect(ent_list[:]))
        quantise_entity_weight(1)
        ent_codes = []
        for name, lo, hi in (("soon_codes", 0, SOON), ("later_codes", SOON, J)):
            codes = placed([P, 2, 2 * (hi - lo)], U8, name, ENT_CODES_AT + lo / 256)
            nc.vector.tensor_copy(
                out=codes[:].bitcast(U16), in_=ent_pairs[:, lo:hi].bitcast(U16).rearrange("p (n d) -> p d n", d=2)
            )
            ent_codes.append(codes)
        quantise_entity_weight(2)
        quantise_entity_weight(3, parts=2)

        ent_planes.append(move_planes("later_planes", LATER_PLANES_AT, slice(SOON // 4, J // 4)))
        n_raw = []
        for w, src in enumerate((nr, ni)):
            raw = placed([P, PACK, N], F32, "n_raw%d" % w, WEIGHT_ROWS_AT[1 + w])
            rows = src.rearrange("(b t m) n -> t b m n", t=PACK, m=RUN)
            for t in range(PACK):
                nc.sync.dma_start(out=raw[:, t, :], in_=rows[t])
            n_raw.append(raw)

        n_grouped = []
        n_codes = []

        def cast_candidates(w):
            grouped = placed([P, N * PACK], BF16, "n_grouped%d" % w, N_GROUPED_AT[w])
            for half in range(2):
                cols = slice(half * N // 2, (half + 1) * N // 2)
                nc.scalar.copy(
                    out=grouped[:].rearrange("p (n t) -> p n t", t=PACK)[:, cols, :],
                    in_=n_raw[w][:].rearrange("p t n -> p n t")[:, cols, :],
                )
            n_grouped.append(grouped)

        def quantise_candidates(w):
            codes = placed([P, N], U32, "n_codes%d" % w, rel_at((3, 1)[w]))
            nc.vector.quantize_mx(out=codes[:].bitcast(FP8X4), scales=n_scales[:, w, :], in_=n_grouped[w][:])
            n_codes.append(codes)

        def part_of(parts, first, step):
            part = int(step * STEP >= first)
            at = step * STEP - part * first
            return parts[part][:].bitcast(U8), slice(at, at + STEP)

        wr_planes = wr_scales[:].bitcast(U8)

        def flat(bank):
            return bank[:].rearrange("p t n -> p (t n)")

        def project_relation(step):
            chunk, at = divmod(step * STEP, CHUNK)
            codes = rel_codes[chunk][:, at:at + STEP].bitcast(FP8X4)
            planes, cols = part_of(rel_planes, CHUNK, step)
            plane = planes[:, cols]
            both = placed([P, 2, STEP, PACK], F32, "rel%d" % step, rel_at(step))
            for w in range(2):
                if step >= HELD_STEP:
                    bank = new_bank(REL_BANKS[w])
                else:
                    bank = new_bank(EARLY_REL_BANKS[(2 * len(rels) + w) % len(EARLY_REL_BANKS)])
                if step in TURNED:
                    nc.tensor.matmul_mx(
                        out=flat(bank),
                        lhsT=codes,
                        lhsT_scale=plane,
                        rhs=wr_codes[:, w, :].bitcast(FP8X4),
                        rhs_scale=wr_planes[:, w, :],
                        start=True,
                        stop=True,
                    )
                    nc.scalar.copy(out=both[:, w].rearrange("p n t -> p (n t)"), in_=flat(bank))
                    continue
                for t in range(PACK):
                    nc.tensor.matmul_mx(
                        out=bank[:, t, :],
                        lhsT=wr_codes[:, w, t * P:(t + 1) * P].bitcast(FP8X4),
                        lhsT_scale=wr_planes[:, w, t * P:(t + 1) * P],
                        rhs=codes,
                        rhs_scale=plane,
                        start=True,
                        stop=True,
                    )
                nc.scalar.copy(out=both[:, w], in_=bank[:].rearrange("p t n -> p n t"))
            return both

        def project_entity(step, w, index):
            planes, cols = part_of(ent_planes, SOON, step)
            words = ent_codes[int(step * STEP >= SOON)]
            codes = [words[:, a, 2 * cols.start:2 * cols.stop].bitcast(FP4X4) for a in range(2)]
            bank = new_bank(index)
            if step in TURNED:
                for a in range(2):
                    nc.tensor.matmul_mx(
                        out=flat(bank),
                        lhsT=codes[a],
                        lhsT_scale=planes[:, a, cols],
                        rhs=we_codes[:, 2 * w + a, :].bitcast(FP8X4),
                        rhs_scale=we_scales[:, 2 * w + a, :],
                        start=(a == 0),
                        stop=(a == 1),
                    )
                return flat(bank).rearrange("p (n t) -> p n t", t=PACK)
            for t in range(PACK):
                for a in range(2):
                    nc.tensor.matmul_mx(
                        out=bank[:, t, :],
                        lhsT=we_codes[:, 2 * w + a, t * P:(t + 1) * P].bitcast(FP8X4),
                        lhsT_scale=we_scales[:, 2 * w + a, t * P:(t + 1) * P],
                        rhs=codes[a],
                        rhs_scale=planes[:, a, cols],
                        start=(a == 0),
                        stop=(a == 1),
                    )
            return bank[:].rearrange("p t n -> p n t")

        def product_tile(name, base, step):
            slot = (step + int(step > SHARED[-1])) % 3
            return placed([P, 2, STEP, PACK], F32, "%s%d" % (name, slot), base + 4 * slot)

        def times_aer(engine, first, aer, rel, cols=slice(0, STEP)):
            both = aer.unsqueeze(1).to_broadcast([P, 2, cols.stop - cols.start, PACK])
            engine.tensor_tensor(first[:, :, cols], both, rel[:, :, cols], MULT)

        def times_aei(second, aei, rel):
            nc.vector.tensor_tensor(second[:, 1], aei, rel[:, 0], MULT)
            nc.vector.scalar_tensor_tensor(second[:, 0], aei, -1.0, rel[:, 1], MULT, MULT)

        def quarters(product):
            return [product.rearrange("p n t -> p (n t)")[:, t * P:(t + 1) * P] for t in range(PACK)]

        def new_sums():
            return ring.tile([P, 2 * STEP * PACK], BF16, name="h", align_bytes=64, bufs=6)

        def add_products(first, second, kib=None):
            h = new_sums() if kib is None else placed([P, 2 * STEP * PACK], BF16, "held_sums", kib)
            nc.gpsimd.tensor_tensor(
                h[:], first[:].rearrange("p w n t -> p (w n t)"), second[:].rearrange("p w n t -> p (w n t)"), ADD
            )
            return h

        def add_by_turning(h, w, terms, bank, copy):
            for index, term in enumerate(terms):
                nc.tensor.matmul(
                    bank[:, index % PACK, :],
                    term,
                    identity[:],
                    start=(index == 0),
                    stop=(index == len(terms) - 1),
                    is_transpose=True,
                )
            copy(out=h[:].rearrange("p (w n t) -> p w n t", w=2, t=PACK)[:, w], in_=bank[:].rearrange("p t n -> p n t"))

        out_view = out.rearrange("(a p) j -> p a j", p=P)

        def quantise_sum(h):
            h_codes = ring.tile([P, 2 * STEP], U32, name="h_codes", align_bytes=64, bufs=4)
            h_scales = ring.tile([P, 2 * STEP], U8, name="h_scales", align_bytes=64, bufs=4)
            for w in range(2):
                cols = slice(w * STEP, (w + 1) * STEP)
                nc.vector.quantize_mx(
                    out=h_codes[:, cols].bitcast(FP8X4),
                    scales=h_scales[:, cols],
                    in_=h[:, w * STEP * PACK:(w + 1) * STEP * PACK],
                )
            return h_codes, h_scales

        def quantise_into_pair(h, pair, half):
            cols = slice(half * STEP, (half + 1) * STEP)
            for w in range(2):
                nc.vector.quantize_mx(
                    out=pair[0][:, w, cols].bitcast(FP8X4),
                    scales=pair[1][:, w, cols],
                    in_=h[:, w * STEP * PACK:(w + 1) * STEP * PACK],
                )

        def new_pair():
            codes = ring.tile([P, 2, 2 * STEP], U32, name="pair_codes", align_bytes=64, bufs=4)
            scales = ring.tile([P, 2, 2 * STEP], U8, name="pair_scales", align_bytes=64, bufs=4)
            return codes, scales

        def score_pair(step, pair, blocks):
            bank = score_bank(len(blocks), 2 * STEP)
            for at, a in enumerate(blocks):
                for w in range(2):
                    nc.tensor.matmul_mx(
                        out=bank[:, at, :],
                        lhsT=n_codes[w][:, a * P:(a + 1) * P].bitcast(FP8X4),
                        lhsT_scale=n_scales[:, w, a * P:(a + 1) * P],
                        rhs=pair[0][:, w, :].bitcast(FP8X4),
                        rhs_scale=pair[1][:, w, :],
                        start=(w == 0),
                        stop=(w == 1),
                    )
            result = ring.tile([P, len(blocks), 2 * STEP], F32, name="result", bufs=6)
            nc.scalar.activation(result[:], bank[:], SIGMOID)
            nc.sync.dma_start(out=out_view[:, blocks[0]:blocks[-1] + 1, step * STEP:(step + 2) * STEP], in_=result[:])

        def score(step, h_codes, h_scales):
            bank = score_bank(N // P, STEP)
            for a in range(N // P):
                for w in range(2):
                    nc.tensor.matmul_mx(
                        out=bank[:, a, :],
                        lhsT=n_codes[w][:, a * P:(a + 1) * P].bitcast(FP8X4),
                        lhsT_scale=n_scales[:, w, a * P:(a + 1) * P],
                        rhs=h_codes[:, w * STEP:(w + 1) * STEP].bitcast(FP8X4),
                        rhs_scale=h_scales[:, w * STEP:(w + 1) * STEP],
                        start=(w == 0),
                        stop=(w == 1),
                    )
            result = ring.tile([P, N // P, STEP], F32, name="result", bufs=6)
            nc.scalar.activation(result[:], bank[:], SIGMOID)
            nc.sync.dma_start(out=out_view[:, :, step * STEP:(step + 1) * STEP], in_=result[:])

        def score_last(h):
            h_codes = ring.tile([P, 2 * STEP], U32, name="h_codes", align_bytes=64, bufs=4)
            h_scales = ring.tile([P, 2 * STEP], U8, name="h_scales", align_bytes=64, bufs=4)
            shares = (range(0, 2), range(2, 3), range(3, 4))
            banks = [new_bank(index, len(blocks)) for blocks, index in zip(shares, (2, 3, REL_BANKS[1]))]
            for w in (1, 0):
                cols = slice(w * STEP, (w + 1) * STEP)
                nc.vector.quantize_mx(
                    out=h_codes[:, cols].bitcast(FP8X4),
                    scales=h_scales[:, cols],
                    in_=h[:, w * STEP * PACK:(w + 1) * STEP * PACK],
                )
                for blocks, bank in zip(shares, banks):
                    for at, a in enumerate(blocks):
                        nc.tensor.matmul_mx(
                            out=bank[:, at, :],
                            lhsT=n_codes[w][:, a * P:(a + 1) * P].bitcast(FP8X4),
                            lhsT_scale=n_scales[:, w, a * P:(a + 1) * P],
                            rhs=h_codes[:, cols].bitcast(FP8X4),
                            rhs_scale=h_scales[:, cols],
                            start=(w == 1 and at == 0),
                            stop=(w == 0 and at == len(blocks) - 1),
                        )
            for blocks, bank, queue in zip(shares, banks, (nc.sync, nc.sync, nc.scalar)):
                result = placed([P, len(blocks), STEP], F32, "last_result%d" % blocks[0], LAST_RESULTS_AT + blocks[0] / 2)
                nc.scalar.activation(result[:], bank[:], SIGMOID)
                queue.dma_start(out=out_view[:, blocks[0]:blocks[-1] + 1, J - STEP:J], in_=result[:])

        rels = {}
        for step in EARLY_TURNED + SHARED + (4, 5):
            rels[step] = project_relation(step)
        aer = {}
        copied = {}

        def project_shared(step, index):
            aer[step] = project_entity(step, 0, index)
            copied[step] = placed([P, SHARE[step], PACK], F32, "shared_aer%d" % step, SHARED_AER_AT[step])
            nc.scalar.copy(out=copied[step][:], in_=aer[step][:, 0:SHARE[step]])

        project_shared(0, 6)
        aer[2] = project_entity(2, 0, 0)
        aer[3] = project_entity(3, 0, 6)
        aei = {step: project_entity(step, 1, index) for step, index in ((2, 2), (0, 3), (3, 7))}
        first = {}
        second = {}
        sums = {}
        pairs = {}
        quantised = {}
        halves = []

        def quantise_step(step):
            if step >= PAIRED:
                quantised[step] = quantise_sum(sums[step])
                return
            if step % 2 == 0:
                pairs[step // 2] = new_pair()
            quantise_into_pair(sums[step], pairs[step // 2], step % 2)
            if step % 2 == 1:
                halves.extend((step // 2, half) for half in range(2))

        later = HELD_STEP
        for turn in range(ROUNDS):
            step = turn + 1
            if turn == 1:
                aei[1] = project_entity(1, 1, 6)
            if turn == 2:
                turned = EARLY_TURNED[0]
                sums[turned] = new_sums()
                for w in (1, 0):
                    bank = new_bank(1 - w)
                    add_by_turning(sums[turned], w, quarters(first[turned][:, w]) + quarters(second[turned][:, w]), bank, nc.scalar.copy)
            if 2 <= turn < ROUNDS - 1:
                aer[step + 1] = project_entity(step + 1, 0, 2 * (step % 2))
                aei[step + 1] = project_entity(step + 1, 1, 2 * (step % 2) + 1)
            relation_due = turn != 1 and later < STEPS
            if relation_due:
                rels[later] = project_relation(later)
                later = later + 1
            if turn in (0, 1):
                cast_candidates(turn)
            if turn == 3:
                turned = EARLY_TURNED[1]
                sums[turned] = new_sums()
                for w in (1, 0):
                    bank = score_bank(PACK, STEP)
                    add_by_turning(sums[turned], w, quarters(first[turned][:, w]) + quarters(second[turned][:, w]), bank, nc.scalar.copy)
            for index, half in sorted(halves)[:1 if relation_due else 2]:
                halves.remove((index, half))
                score_pair(2 * index, pairs[index], range(2 * half, 2 * half + 2))
            if turn == ROUNDS - 1:
                score(PAIRED, *quantised[PAIRED])
            if turn == 0:
                first[0] = placed([P, 2, STEP, PACK], F32, "shared_first0", LAST_CAST_AT)
                first[1] = placed([P, 2, STEP, PACK], F32, "shared_first1", LAST_CAST_AT + 16)
                times_aer(nc.gpsimd, first[0], copied[0][:], rels[0])
                for at, turned in enumerate(EARLY_TURNED):
                    first[turned] = placed([P, 2, STEP, PACK], F32, "turned_first%d" % at, LAST_CAST_AT + 4 + 4 * at)
                    times_aer(nc.vector, first[turned], aer[turned], rels[turned])
                    if at == 0:
                        project_shared(1, 0)
                times_aer(nc.vector, first[1], aer[1][:, SHARE[1]:STEP], rels[1], slice(SHARE[1], STEP))
                times_aer(nc.gpsimd, first[1], copied[1][:], rels[1], slice(0, SHARE[1]))
            elif turn in (1, 2):
                turned, shared = EARLY_TURNED[turn - 1], SHARED[turn - 1]
                second[turned] = placed([P, 2, STEP, PACK], F32, "turned_second%d" % turn, TURNED_SECOND_AT[turn - 1])
                times_aei(second[turned], aei[turned], rels[turned])
                second[shared] = product_tile("second", SECOND_AT, shared)
                times_aei(second[shared], aei[shared], rels[shared])
                if turn == 2:
                    quantise_candidates(0)
                    quantise_step(SHARED[0])
                sums[shared] = add_products(first[shared], second[shared], N_GROUPED_AT[0] if turn == 2 else None)
            elif step < LAST:
                first[step] = product_tile("first", FIRST_AT, step)
                second[step] = product_tile("second", SECOND_AT, step)
                times_aer(nc.vector, first[step], aer[step], rels[step])
                times_aei(second[step], aei[step], rels[step])
                sums[step] = add_products(first[step], second[step])
            else:
                first[step] = product_tile("first", FIRST_AT, step)
                second[step] = product_tile("second", SECOND_AT, step)
                nc.vector.tensor_tensor(first[step][:, 1], aer[step], rels[step][:, 1], MULT)
                nc.vector.tensor_tensor(second[step][:, 1], aei[step], rels[step][:, 0], MULT)
                nc.vector.tensor_tensor(first[step][:, 0], aer[step], rels[step][:, 0], MULT)
                for part in (slice(0, 3 * STEP // 4), slice(3 * STEP // 4, STEP)):
                    nc.vector.scalar_tensor_tensor(
                        second[step][:, 0, part], aei[step][:, part], -1.0, rels[step][:, 1, part], MULT, MULT
                    )
            if turn == 3:
                quantise_candidates(1)
            if turn == 4:
                quantise_step(SHARED[1])
            if turn >= 5:
                quantise_step(turn - 1)
            if turn in (4, 5):
                quantise_step(EARLY_TURNED[turn - 4])
        last_sums = new_sums()
        for w, copy in ((1, nc.scalar.copy), (0, nc.vector.tensor_copy)):
            bank = new_bank(REL_BANKS[w])
            add_by_turning(last_sums, w, quarters(first[LAST][:, w]) + quarters(second[LAST][:, w]), bank, copy)
        score(LAST - 2, *quantised[LAST - 2])
        score(LAST - 1, *quantise_sum(sums[LAST - 1]))
        score_last(last_sums)
